import numpy as np
import ml_dtypes


def mxq(x, axis, fmt="e4m3"):
    dtype, down = {"e4m3": (ml_dtypes.float8_e4m3fn, 7), "e5m2": (ml_dtypes.float8_e5m2, 14)}[fmt]
    v = np.moveaxis(np.asarray(x, np.float32).astype(ml_dtypes.bfloat16).astype(np.float64), axis, -1)
    blocks = v.reshape(v.shape[:-1] + (-1, 32))
    amax = np.abs(blocks).max(-1, keepdims=True)
    byte = np.maximum(np.where(amax > 0, np.frexp(amax)[1] - 1 + 127, 0) - down, 1)
    scale = np.exp2(byte - 127.0)
    codes = (blocks / scale).astype(np.float32).astype(dtype).astype(np.float64)
    return np.moveaxis((codes * scale).reshape(v.shape), -1, axis)


WIDE = False


def mx_kscale(k):
    if not WIDE:
        return np.ones(k)
    levels = np.array([24, -24, 12, -12, 0])
    if k % 512:
        return np.exp2(np.random.permutation(np.resize(levels, k // 32))).repeat(32)
    a = np.empty((k // 512, 16))
    for p in range(k // 512):
        a[p, :8] = np.random.permutation(np.resize(levels, 8))
        for g in range(8):
            far = levels[np.abs(levels - a[p, g]) >= 10]
            a[p, g + 8] = far[np.random.randint(len(far))]
    return np.exp2(a.ravel()).repeat(32)


def f64(x):
    return np.asarray(x).astype(np.float64)


def striped8(idx):
    return np.concatenate([v.reshape(-1, 16).T for v in idx]).astype(np.uint16)


def unstriped8(offs):
    return np.stack([offs[16 * g:16 * g + 16].T.reshape(-1) for g in range(8)]).astype(np.int64)


E2M1 = np.array([0.0, 0.5, 1.0, 1.5, 2.0, 3.0, 4.0, 6.0, -0.0, -0.5, -1.0, -1.5, -2.0, -3.0, -4.0, -6.0])


def pack_weight(w, fmt):
    k, n = w.shape
    w = f64(np.asarray(w, np.float32).astype(ml_dtypes.bfloat16)).reshape(k // 32, 32, n)
    amax = np.abs(w).max(1)
    if fmt == "e4m3":
        byte = np.frexp(amax)[1] - 1 + 127 - 7
    else:
        mant, ex = np.frexp(amax / 6.0)
        byte = np.where(mant > 0.5, ex, ex - 1) + 127
    byte = np.clip(np.where(amax > 0, byte, 1), 1, 254)
    scaled = (w * np.exp2(127.0 - byte)[:, None, :]).reshape(k, n).astype(np.float32)
    by_word = np.ascontiguousarray(scaled.reshape(k // 512, 128, 4, n).transpose(0, 1, 3, 2))
    if fmt == "e4m3":
        words = by_word.astype(ml_dtypes.float8_e4m3fn).view(np.uint8)
    else:
        c = by_word.astype(ml_dtypes.float4_e2m1fn).view(np.uint8) & 0xF
        words = (c[..., 0::2] | (c[..., 1::2] << 4)).reshape(k // 512, 128, 2 * n)
    return np.ascontiguousarray(words), np.ascontiguousarray(byte.astype(np.uint8).reshape(k // 512, 16, n))


def unpack_weight(words, scales, fmt):
    g, _, n = scales.shape
    words = np.ascontiguousarray(words).reshape(g, 128, n, -1)
    if fmt == "e4m3":
        vals = words.view(ml_dtypes.float8_e4m3fn).astype(np.float64)
    else:
        nib = np.empty((g, 128, n, 4), np.uint8)
        nib[..., 0::2] = words & 0xF
        nib[..., 1::2] = words >> 4
        vals = E2M1[nib]
    vals = vals * np.repeat(np.exp2(scales.astype(np.float64) - 127.0), 8, axis=1)[..., None]
    return vals.transpose(0, 1, 3, 2).reshape(g * 512, n)


def silu(f):
    return f / (1.0 + np.exp(-np.maximum(f, -700.0)))


K, R, N, T, J = 512, 1024, 512, 2048, 1024


def setup_inputs():
    n = np.random.standard_normal
    s = mx_kscale(K)[:, None]
    u = mx_kscale(R)[:, None]
    wd = n((R, N)) / np.sqrt(R) / u
    p_wu = pack_weight(n((K, R)) / np.sqrt(K) / s * u.T, "e2m1")
    p_wd8 = pack_weight(wd[:512], "e4m3")
    p_wd4 = pack_weight(wd[512:], "e2m1")
    return {
        "xT": (n((K, T)) * s).astype(np.float32),
        "wgt": np.repeat(np.random.uniform(0.5, 2.0, (8, J)), 16, axis=0).astype(np.float32),
        "wg": (n((K, R)) / np.sqrt(K) / s).astype(np.float32),
        "wu_words": p_wu[0],
        "wu_scales": p_wu[1],
        "wd8_words": p_wd8[0],
        "wd8_scales": p_wd8[1],
        "wd4_words": p_wd4[0],
        "wd4_scales": p_wd4[1],
        "res": (n((N, J))).astype(np.float32),
        "offs": striped8(np.stack([np.random.permutation(T)[:J] for _ in range(8)])),
    }


def reference(xT, wgt, wg, wu_words, wu_scales, wd8_words, wd8_scales, wd4_words, wd4_scales, res, offs):
    idx = unstriped8(offs)
    rows = np.arange(K)
    xg = f64(wgt)[rows // 4 % 128] * f64(xT)[rows[:, None], idx[rows % 512 // 64]]
    xT_ = mxq(xg, 0, "e4m3")
    wg_ = mxq(f64(wg), 0, "e4m3")
    wu_ = unpack_weight(wu_words, wu_scales, "e2m1")
    ga = wg_.T @ xT_
    ub = wu_.T @ xT_
    h = silu(ga) * ub
    h_ = mxq(h, 0, "e4m3")
    wd8_ = unpack_weight(wd8_words, wd8_scales, "e4m3")
    wd4_ = unpack_weight(wd4_words, wd4_scales, "e2m1")
    y = wd8_.T @ h_[:512] + wd4_.T @ h_[512:]
    return f64(res) + y

@@ -1,0 +1,285 @@
+from contextlib import ExitStack
+
+import concourse.mybir as mybir
+
+K, R, N, T, J = 512, 1024, 512, 2048, 1024
+FLOPS = 2 * K * R * J * 2 + 2 * R * N * J
+
+F32 = mybir.dt.float32
+BF16 = mybir.dt.bfloat16
+I32 = mybir.dt.int32
+U32 = mybir.dt.uint32
+U16 = mybir.dt.uint16
+U8 = mybir.dt.uint8
+FP8X4 = mybir.dt.float8_e4m3fn_x4
+FP4X4 = mybir.dt.float4_e2m1fn_x4
+MULT = mybir.AluOpType.mult
+ADD = mybir.AluOpType.add
+ACT = mybir.ActivationFunctionType
+
+P = 128
+PACK = 4
+HALF = 512
+TOK = 128
+QUANT = [0, 0, 0, 4, 0, 2, 0, 2, 0, 0, 0, 4, 0, 2, 1, 1]
+VIA_GPSIMD = ()
+GSTEP = 2
+WG0V = True
+WG1V = False
+
+
+def tile_list_silu_mix_res_kernel(
+    tc, xT, wgt, wg, wu_words, wu_scales, wd8_words, wd8_scales, wd4_words, wd4_scales, res, offs, out
+):
+    nc = tc.nc
+    with ExitStack() as ctx:
+        keep = ctx.enter_context(tc.tile_pool(name="keep", bufs=1))
+        ring = ctx.enter_context(tc.tile_pool(name="ring", bufs=4))
+        ps_ga = ctx.enter_context(tc.psum_pool(name="ps_ga", bufs=3))
+        ps_ub = ctx.enter_context(tc.psum_pool(name="ps_ub", bufs=3))
+        ps_y = ctx.enter_context(tc.psum_pool(name="ps_y", bufs=2))
+
+        offsets = keep.tile([P, J // 16], U16, name="offsets")
+        nc.sync.dma_start(offsets[:], offs)
+
+        wu_sc_in = keep.tile([P, R], U8, name="wu_sc_in", align_bytes=64)
+        wd_sc = keep.tile([P, 2 * N], U8, name="wd_sc", align_bytes=64)
+        nc.gpsimd.memset(wu_sc_in[:].bitcast(I32), 0)
+        for q in range(4):
+            nc.gpsimd.dma_start(
+                wu_sc_in[32 * q : 32 * q + 4, :].bitcast(I32), wu_scales[0, 4 * q : 4 * q + 4, :].bitcast(I32)
+            )
+        zero_in = keep.tile([P, 1], F32, name="zero_in")
+        nc.vector.memset(zero_in[:], 0.0)
+        nc.vector.memset(wd_sc[:].bitcast(I32), 0)
+        zero = keep.tile([P, 1], F32, name="zero")
+        nc.scalar.activation(zero[:], zero_in[:], ACT.Silu)
+        for src, c0 in ((wd8_scales, 0), (wd4_scales, N)):
+            for q in range(4):
+                nc.gpsimd.dma_start(
+                    wd_sc[32 * q : 32 * q + 4, c0 : c0 + N].bitcast(I32),
+                    src[0, 4 * q : 4 * q + 4, :].bitcast(I32),
+                )
+
+        wu_in = keep.tile([P, 2 * R], U8, name="wu_in", align_bytes=64)
+        nc.sync.dma_start(wu_in[:].bitcast(I32), wu_words[0].bitcast(I32))
+        x_rows = xT.rearrange("(p i) t -> i p t", i=PACK)
+        wgt_sb = [keep.tile([P, HALF], F32, name=f"wgt{a}") for a in range(2)]
+        planes = [keep.tile([P, T], F32, name=f"plane{i}") for i in range(PACK)]
+        nc.sync.dma_start(wgt_sb[0][:], wgt[:, 0:HALF])
+        nc.sync.dma_start(planes[0][:], x_rows[0])
+        nc.sync.dma_start(wgt_sb[1][:], wgt[:, HALF:J])
+        for i in range(1, PACK):
+            nc.sync.dma_start(planes[i][:], x_rows[i])
+        wg_rows = wg.rearrange("(p i) r -> p i r", i=PACK)
+        wg_in = [keep.tile([P, PACK, 256], F32, name=f"wg_in{c}") for c in range(4)]
+        for c in range(4):
+            nc.sync.dma_start(wg_in[c][:], wg_rows[:, :, 256 * c : 256 * (c + 1)])
+        wd8_sb = keep.tile([P, N], U32, name="wd8_sb", align_bytes=64)
+        nc.sync.dma_start(wd8_sb[:].bitcast(I32), wd8_words[0].rearrange("p n t -> p (n t)").bitcast(I32))
+        wd4_sb = keep.tile([P, 2 * N], U8, name="wd4_sb", align_bytes=64)
+        nc.sync.dma_start(wd4_sb[:].bitcast(I32), wd4_words[0].bitcast(I32))
+        res_rows = res.rearrange("(a p) j -> p a j", p=P)
+        out_rows = out.rearrange("(a p) j -> p a j", p=P)
+        res_sb = [keep.tile([P, 4, HALF], F32, name=f"res{a}") for a in range(2)]
+        for a in range(2):
+            nc.sync.dma_start(res_sb[a][:], res_rows[:, :, HALF * a : HALF * (a + 1)])
+
+        wu_codes = keep.tile([P, 2 * R], U8, name="wu_codes", align_bytes=64)
+        wu_sc = keep.tile([P, R], U8, name="wu_sc", align_bytes=64)
+        nc.vector.tensor_copy(
+            wu_codes[:].bitcast(U16).rearrange("p (b t m) -> p b t m", b=2, t=PACK),
+            wu_in[:].bitcast(U16).rearrange("p (b m t) -> p b t m", b=2, t=PACK),
+        )
+
+        picked = [keep.tile([P, PACK, HALF], F32, name=f"picked{a}") for a in range(2)]
+        xg_bf = keep.tile([P, J, PACK], BF16, name="xg_bf", align_bytes=64)
+        xg_codes = keep.tile([P, J], U32, name="xg_codes", align_bytes=64)
+        xg_sc = keep.tile([P, J], U8, name="xg_sc", align_bytes=64)
+        wg_bf = [keep.tile([P, PACK, P, PACK], BF16, name=f"wg_bf{b}", align_bytes=64) for b in range(2)]
+        wg_codes = [keep.tile([P, HALF], U32, name=f"wg_codes{b}", align_bytes=64) for b in range(2)]
+        wg_sc = [keep.tile([P, HALF], U8, name=f"wg_sc{b}", align_bytes=64) for b in range(2)]
+        h_codes = [keep.tile([P, J], U32, name=f"h_codes{b}", align_bytes=64) for b in range(2)]
+        h_sc = [keep.tile([P, J], U8, name=f"h_sc{b}", align_bytes=64) for b in range(2)]
+
+        def gather(i, j0, n):
+            a, c = divmod(j0, HALF)
+            nc.vector.tensor_tensor(
+                picked[a][:, i, c : c + n],
+                planes[i][:].indirect(offsets[:, j0 // 16 : (j0 + n) // 16]),
+                wgt_sb[a][:, c : c + n],
+                MULT,
+            )
+
+        def round_x(j0, n, i0):
+            a, c = divmod(j0, HALF)
+            nc.scalar.copy(
+                xg_bf[:, j0 : j0 + n, i0 : i0 + 2],
+                picked[a][:, i0 : i0 + 2, c : c + n].rearrange("p i j -> p j i"),
+            )
+
+        def quant_x(j0, n):
+            nc.vector.quantize_mx(
+                out=xg_codes[:, j0 : j0 + n].bitcast(FP8X4),
+                scales=xg_sc[:, j0 : j0 + n],
+                in_=xg_bf[:, j0 : j0 + n, :].rearrange("p j i -> p (j i)"),
+            )
+
+        def round_wg(b, m0, n, on_vector):
+            c, mm = divmod(b * P + m0, 64)
+            dst = wg_bf[b][:, :, m0 : m0 + n, :].rearrange("p t m i -> p m i t")
+            src = wg_in[c][:, :, 4 * mm : 4 * (mm + n)].rearrange("p i (m t) -> p m i t", t=PACK)
+            if on_vector:
+                nc.vector.tensor_copy(dst, src)
+            else:
+                nc.scalar.copy(dst, src)
+
+        def quant_wg(b):
+            nc.vector.quantize_mx(
+                out=wg_codes[b][:].bitcast(FP8X4),
+                scales=wg_sc[b][:],
+                in_=wg_bf[b][:].rearrange("p t m i -> p (t m i)"),
+            )
+
+        ga_of, ub_of, gate_of, h_of, y_of = {}, {}, {}, {}, {}
+
+        def up(b, c):
+            cols = slice(TOK * c, TOK * (c + 1))
+            ga = ps_ga.tile([P, PACK, TOK], F32, name="ga")
+            ub = ps_ub.tile([P, PACK, TOK], F32, name="ub")
+            for t in range(PACK):
+                nc.tensor.matmul_mx(
+                    out=ga[:, t, :],
+                    lhsT=wg_codes[b][:, P * t : P * (t + 1)].bitcast(FP8X4),
+                    lhsT_scale=wg_sc[b][:, P * t : P * (t + 1)],
+                    rhs=xg_codes[:, cols].bitcast(FP8X4),
+                    rhs_scale=xg_sc[:, cols],
+                    start=True,
+                    stop=True,
+                )
+            for t in range(PACK):
+                s = PACK * b + t
+                nc.tensor.matmul_mx(
+                    out=ub[:, t, :],
+                    lhsT=wu_codes[:, 2 * P * s : 2 * P * (s + 1)].bitcast(FP4X4),
+                    lhsT_scale=wu_sc[:, P * s : P * (s + 1)],
+                    rhs=xg_codes[:, cols].bitcast(FP8X4),
+                    rhs_scale=xg_sc[:, cols],
+                    start=True,
+                    stop=True,
+                )
+            ga_of[b, c], ub_of[b, c] = ga, ub
+
+        def silu(b, c):
+            gate = ring.tile([P, TOK, PACK], F32, name="gate")
+            nc.scalar.activation(gate[:], ga_of[b, c][:].rearrange("p t j -> p j t"), ACT.Silu, bias=zero[:])
+            gate_of[b, c] = gate
+
+        h_bf = [keep.tile([P, J, PACK], BF16, name=f"h_bf{b}", align_bytes=64) for b in range(2)]
+
+        def product(b, c):
+            nc.vector.tensor_tensor(
+                h_bf[b][:, TOK * c : TOK * (c + 1), :], ub_of[b, c][:].rearrange("p t j -> p j t"), gate_of[b, c][:], MULT
+            )
+
+        def quant_h(b, c, n):
+            cols = slice(TOK * c, TOK * (c + n))
+            nc.vector.quantize_mx(
+                out=h_codes[b][:, cols].bitcast(FP8X4),
+                scales=h_sc[b][:, cols],
+                in_=h_bf[b][:, cols, :].rearrange("p j t -> p (j t)"),
+            )
+
+        def down(c):
+            cols = slice(TOK * c, TOK * (c + 1))
+            y = ps_y.tile([P, 4, TOK], F32, name="y")
+            for a in range(4):
+                nc.tensor.matmul_mx(
+                    out=y[:, a, :],
+                    lhsT=wd8_sb[:, P * a : P * (a + 1)].bitcast(FP8X4),
+                    lhsT_scale=wd_sc[:, P * a : P * (a + 1)],
+                    rhs=h_codes[0][:, cols].bitcast(FP8X4),
+                    rhs_scale=h_sc[0][:, cols],
+                    start=True,
+                    stop=False,
+                )
+                nc.tensor.matmul_mx(
+                    out=y[:, a, :],
+                    lhsT=wd4_sb[:, 2 * P * a : 2 * P * (a + 1)].bitcast(FP4X4),
+                    lhsT_scale=wd_sc[:, N + P * a : N + P * (a + 1)],
+                    rhs=h_codes[1][:, cols].bitcast(FP8X4),
+                    rhs_scale=h_sc[1][:, cols],
+                    start=False,
+                    stop=True,
+                )
+            y_of[c] = y
+
+        def finish(c):
+            a, c0 = divmod(TOK * c, HALF)
+            result = ring.tile([P, 4, TOK], F32, name="result")
+            if c in VIA_GPSIMD:
+                y_sb = ring.tile([P, 4, TOK], F32, name="y_sb")
+                nc.scalar.copy(y_sb[:], y_of[c][:])
+                for e in range(0, 4, GSTEP):
+                    nc.gpsimd.tensor_tensor(result[:, e : e + GSTEP, :], y_sb[:, e : e + GSTEP, :], res_sb[a][:, e : e + GSTEP, c0 : c0 + TOK], ADD)
+            else:
+                nc.vector.tensor_tensor(result[:], y_of[c][:], res_sb[a][:, :, c0 : c0 + TOK], ADD)
+            nc.sync.dma_start(out_rows[:, :, TOK * c : TOK * (c + 1)], result[:])
+
+        for i in range(PACK - 1):
+            gather(i, 0, HALF)
+            gather(i, HALF, HALF)
+            if i == 0:
+                nc.vector.tensor_copy(
+                    wu_sc[:].rearrange("p (b t m) -> p b t m", b=2, t=PACK),
+                    wu_sc_in[:].rearrange("p (b m t) -> p b t m", b=2, t=PACK),
+                )
+            if i == 1:
+                round_x(0, HALF, 0)
+                round_x(HALF, HALF, 0)
+        gather(3, 0, 128)
+        round_x(0, 128, 2)
+        gather(3, 128, 128)
+        round_wg(0, 0, 64, False)
+        round_wg(0, 64, 64, WG0V)
+        quant_wg(0)
+        quant_x(0, 128)
+        round_x(128, 128, 2)
+        gather(3, 256, 256)
+        quant_x(128, 128)
+        round_x(256, 256, 2)
+        gather(3, 512, 256)
+        gather(3, 768, 256)
+
+        units = [(b, c) for g in range(2) for b in range(2) for c in range(4 * g, 4 * g + 4)]
+        extra = {
+            0: [lambda: quant_x(256, 256), lambda: round_wg(1, 0, 32, False)],
+            1: [lambda: round_wg(1, 32, 32, False), lambda: round_wg(1, 64, 32, False)],
+            2: [lambda: round_wg(1, 96, 32, WG1V)],
+            3: [lambda: quant_wg(1)],
+            4: [lambda: round_x(512, 256, 2)],
+            5: [lambda: round_x(768, 256, 2)],
+            6: [lambda: quant_x(512, 512)],
+        }
+        todo = []
+        for k in range(len(units) + 6):
+            if k < len(units):
+                up(*units[k])
+                silu(*units[k])
+            if 0 <= k - 1 < len(units):
+                product(*units[k - 1])
+            ready = []
+            if 0 <= k - 2 < len(units):
+                b, c = units[k - 2]
+                n = QUANT[k - 2]
+                if n:
+                    quant_h(b, c + 1 - n, n)
+                    if b == 1:
+                        ready = list(range(c + 1 - n, c + 1))
+            if todo:
+                finish(todo.pop(0))
+            for c in ready:
+                down(c)
+            todo += ready
+            for step in extra.get(k, []):
+                step()

@@ -21,11 +21,11 @@ P = 128
 PACK = 4
 HALF = 512
 TOK = 128
-QUANT = [0, 0, 0, 4, 0, 2, 0, 2, 0, 0, 0, 4, 0, 2, 1, 1]
-VIA_GPSIMD = ()
-GSTEP = 2
-WG0V = True
-WG1V = False
+TAGS = ("ga","ub","y")
+BUFS = (2,3,3)
+WSPLIT = 256
+LOADS = "wu wa wus x0 wb x1 x2 x3 g0 g1 g2 g3 wd wds r0 r1"
+ORDER = "pw ps g:0:0:256 g:0:256:256 g:0:512:512 g:1:0:512 rx:0:512:0 g:1:512:512 rx:512:512:0 g:2:0:512 g:3:0:128 rx:0:128:2 qx:0:128 rw:0:0:64:1 rw:0:64:64:1 qw:0 g:3:128:128 rx:128:128:2 qx:128:128 g:3:256:256 rx:256:256:2 qx:256:256 g:2:512:384 g:2:896:128 u:0:0 b:0:0 rw:1:0:32:0 rw:1:32:32:0 u:0:1 b:0:1 p:0:0 rw:1:64:32:0 rw:1:96:32:0 g:3:512:256 u:0:2 b:0:2 p:0:1 qw:1 g:3:768:256 u:0:3 b:0:3 p:0:2 u:1:0 b:1:0 p:0:3 rx:512:256:2 u:1:1 b:1:1 p:1:0 qh:0:0:4 qx:512:256 rx:768:256:2 u:1:2 b:1:2 p:1:1 qx:768:256 u:1:3 b:1:3 p:1:2 qh:1:0:2 d:0 d:1 u:0:4 b:0:4 p:1:3 f:0:0:0 u:0:5 b:0:5 p:0:4 qh:1:2:2 f:1:0:0 d:2 d:3 u:0:6 b:0:6 p:0:5 f:2:0:0 u:0:7 b:0:7 p:0:6 f:3:0:0 u:1:4 b:1:4 p:0:7 u:1:5 b:1:5 p:1:4 qh:0:4:4 u:1:6 b:1:6 p:1:5 u:1:7 b:1:7 p:1:6 qh:1:4:2 d:4 d:5 p:1:7 qh:1:6:1 f:4:0:0 d:6 qh:1:7:1 f:5:0:0 d:7 f:6:0:0 f:7:0:0"
 
 
 def tile_list_silu_mix_res_kernel(
@@ -35,62 +35,73 @@ def tile_list_silu_mix_res_kernel(
     with ExitStack() as ctx:
         keep = ctx.enter_context(tc.tile_pool(name="keep", bufs=1))
         ring = ctx.enter_context(tc.tile_pool(name="ring", bufs=4))
-        ps_ga = ctx.enter_context(tc.psum_pool(name="ps_ga", bufs=3))
-        ps_ub = ctx.enter_context(tc.psum_pool(name="ps_ub", bufs=3))
-        ps_y = ctx.enter_context(tc.psum_pool(name="ps_y", bufs=2))
+        psum = ctx.enter_context(tc.psum_pool(name="psum", bufs=1))
 
         offsets = keep.tile([P, J // 16], U16, name="offsets")
         nc.sync.dma_start(offsets[:], offs)
 
         wu_sc_in = keep.tile([P, R], U8, name="wu_sc_in", align_bytes=64)
         wd_sc = keep.tile([P, 2 * N], U8, name="wd_sc", align_bytes=64)
-        nc.gpsimd.memset(wu_sc_in[:].bitcast(I32), 0)
-        for q in range(4):
-            nc.gpsimd.dma_start(
-                wu_sc_in[32 * q : 32 * q + 4, :].bitcast(I32), wu_scales[0, 4 * q : 4 * q + 4, :].bitcast(I32)
-            )
+        nc.vector.memset(wu_sc_in[:].bitcast(I32), 0)
         zero_in = keep.tile([P, 1], F32, name="zero_in")
         nc.vector.memset(zero_in[:], 0.0)
         nc.vector.memset(wd_sc[:].bitcast(I32), 0)
         zero = keep.tile([P, 1], F32, name="zero")
         nc.scalar.activation(zero[:], zero_in[:], ACT.Silu)
-        for src, c0 in ((wd8_scales, 0), (wd4_scales, N)):
+
+        def load_scales(dst, src):
             for q in range(4):
-                nc.gpsimd.dma_start(
-                    wd_sc[32 * q : 32 * q + 4, c0 : c0 + N].bitcast(I32),
-                    src[0, 4 * q : 4 * q + 4, :].bitcast(I32),
-                )
+                nc.sync.dma_start(dst[32 * q : 32 * q + 4, :].bitcast(I32), src[0, 4 * q : 4 * q + 4, :].bitcast(I32))
 
         wu_in = keep.tile([P, 2 * R], U8, name="wu_in", align_bytes=64)
-        nc.sync.dma_start(wu_in[:].bitcast(I32), wu_words[0].bitcast(I32))
         x_rows = xT.rearrange("(p i) t -> i p t", i=PACK)
-        wgt_sb = [keep.tile([P, HALF], F32, name=f"wgt{a}") for a in range(2)]
+        wgt_sb = keep.tile([P, J], F32, name="wgt_sb")
         planes = [keep.tile([P, T], F32, name=f"plane{i}") for i in range(PACK)]
-        nc.sync.dma_start(wgt_sb[0][:], wgt[:, 0:HALF])
-        nc.sync.dma_start(planes[0][:], x_rows[0])
-        nc.sync.dma_start(wgt_sb[1][:], wgt[:, HALF:J])
-        for i in range(1, PACK):
-            nc.sync.dma_start(planes[i][:], x_rows[i])
         wg_rows = wg.rearrange("(p i) r -> p i r", i=PACK)
         wg_in = [keep.tile([P, PACK, 256], F32, name=f"wg_in{c}") for c in range(4)]
-        for c in range(4):
-            nc.sync.dma_start(wg_in[c][:], wg_rows[:, :, 256 * c : 256 * (c + 1)])
         wd8_sb = keep.tile([P, N], U32, name="wd8_sb", align_bytes=64)
-        nc.sync.dma_start(wd8_sb[:].bitcast(I32), wd8_words[0].rearrange("p n t -> p (n t)").bitcast(I32))
         wd4_sb = keep.tile([P, 2 * N], U8, name="wd4_sb", align_bytes=64)
-        nc.sync.dma_start(wd4_sb[:].bitcast(I32), wd4_words[0].bitcast(I32))
         res_rows = res.rearrange("(a p) j -> p a j", p=P)
         out_rows = out.rearrange("(a p) j -> p a j", p=P)
         res_sb = [keep.tile([P, 4, HALF], F32, name=f"res{a}") for a in range(2)]
-        for a in range(2):
-            nc.sync.dma_start(res_sb[a][:], res_rows[:, :, HALF * a : HALF * (a + 1)])
+        for what in LOADS.split():
+            if what == "wu":
+                nc.sync.dma_start(wu_in[:].bitcast(I32), wu_words[0].bitcast(I32))
+            elif what == "wus":
+                load_scales(wu_sc_in[:], wu_scales)
+            elif what == "wa":
+                nc.sync.dma_start(wgt_sb[:, 0:WSPLIT], wgt[:, 0:WSPLIT])
+            elif what == "wb":
+                nc.sync.dma_start(wgt_sb[:, WSPLIT:J], wgt[:, WSPLIT:J])
+            elif what[0] == "x":
+                nc.sync.dma_start(planes[int(what[1])][:], x_rows[int(what[1])])
+            elif what[0] == "g":
+                c = int(what[1])
+                nc.sync.dma_start(wg_in[c][:], wg_rows[:, :, 256 * c : 256 * (c + 1)])
+            elif what == "wd":
+                nc.sync.dma_start(wd8_sb[:].bitcast(I32), wd8_words[0].rearrange("p n t -> p (n t)").bitcast(I32))
+                nc.sync.dma_start(wd4_sb[:].bitcast(I32), wd4_words[0].bitcast(I32))
+            elif what == "wds":
+                load_scales(wd_sc[:, 0:N], wd8_scales)
+                load_scales(wd_sc[:, N : 2 * N], wd4_scales)
+            elif what[0] == "r":
+                a = int(what[1])
+                nc.sync.dma_start(res_sb[a][:], res_rows[:, :, HALF * a : HALF * (a + 1)])
 
         wu_codes = keep.tile([P, 2 * R], U8, name="wu_codes", align_bytes=64)
         wu_sc = keep.tile([P, R], U8, name="wu_sc", align_bytes=64)
-        nc.vector.tensor_copy(
-            wu_codes[:].bitcast(U16).rearrange("p (b t m) -> p b t m", b=2, t=PACK),
-            wu_in[:].bitcast(U16).rearrange("p (b m t) -> p b t m", b=2, t=PACK),
-        )
+
+        def permute_words():
+            nc.vector.tensor_copy(
+                wu_codes[:].bitcast(U16).rearrange("p (b t m) -> p b t m", b=2, t=PACK),
+                wu_in[:].bitcast(U16).rearrange("p (b m t) -> p b t m", b=2, t=PACK),
+            )
+
+        def permute_scales():
+            nc.vector.tensor_copy(
+                wu_sc[:].rearrange("p (b t m) -> p b t m", b=2, t=PACK),
+                wu_sc_in[:].rearrange("p (b m t) -> p b t m", b=2, t=PACK),
+            )
 
         picked = [keep.tile([P, PACK, HALF], F32, name=f"picked{a}") for a in range(2)]
         xg_bf = keep.tile([P, J, PACK], BF16, name="xg_bf", align_bytes=64)
@@ -107,16 +118,22 @@ def tile_list_silu_mix_res_kernel(
             nc.vector.tensor_tensor(
                 picked[a][:, i, c : c + n],
                 planes[i][:].indirect(offsets[:, j0 // 16 : (j0 + n) // 16]),
-                wgt_sb[a][:, c : c + n],
+                wgt_sb[:, j0 : j0 + n],
                 MULT,
             )
 
         def round_x(j0, n, i0):
             a, c = divmod(j0, HALF)
-            nc.scalar.copy(
-                xg_bf[:, j0 : j0 + n, i0 : i0 + 2],
-                picked[a][:, i0 : i0 + 2, c : c + n].rearrange("p i j -> p j i"),
-            )
+            if i0 == 4:
+                nc.scalar.copy(
+                    xg_bf[:, j0 : j0 + n, :].rearrange("p (c e) i -> p c i e", e=4),
+                    picked[a][:, :, c : c + n].rearrange("p i (c e) -> p c i e", e=4),
+                )
+            else:
+                nc.scalar.copy(
+                    xg_bf[:, j0 : j0 + n, i0 : i0 + 2],
+                    picked[a][:, i0 : i0 + 2, c : c + n].rearrange("p i j -> p j i"),
+                )
 
         def quant_x(j0, n):
             nc.vector.quantize_mx(
@@ -145,8 +162,7 @@ def tile_list_silu_mix_res_kernel(
 
         def up(b, c):
             cols = slice(TOK * c, TOK * (c + 1))
-            ga = ps_ga.tile([P, PACK, TOK], F32, name="ga")
-            ub = ps_ub.tile([P, PACK, TOK], F32, name="ub")
+            ga = psum.tile([P, PACK, TOK], F32, name="ga", tag=TAGS[0], bufs=BUFS[0])
             for t in range(PACK):
                 nc.tensor.matmul_mx(
                     out=ga[:, t, :],
@@ -157,6 +173,11 @@ def tile_list_silu_mix_res_kernel(
                     start=True,
                     stop=True,
                 )
+            ga_of[b, c] = ga
+
+        def up_b(b, c):
+            cols = slice(TOK * c, TOK * (c + 1))
+            ub = psum.tile([P, PACK, TOK], F32, name="ub", tag=TAGS[1], bufs=BUFS[1])
             for t in range(PACK):
                 s = PACK * b + t
                 nc.tensor.matmul_mx(
@@ -168,7 +189,7 @@ def tile_list_silu_mix_res_kernel(
                     start=True,
                     stop=True,
                 )
-            ga_of[b, c], ub_of[b, c] = ga, ub
+            ub_of[b, c] = ub
 
         def silu(b, c):
             gate = ring.tile([P, TOK, PACK], F32, name="gate")
@@ -190,96 +211,59 @@ def tile_list_silu_mix_res_kernel(
                 in_=h_bf[b][:, cols, :].rearrange("p j t -> p (j t)"),
             )
 
-        def down(c):
-            cols = slice(TOK * c, TOK * (c + 1))
-            y = ps_y.tile([P, 4, TOK], F32, name="y")
-            for a in range(4):
-                nc.tensor.matmul_mx(
-                    out=y[:, a, :],
-                    lhsT=wd8_sb[:, P * a : P * (a + 1)].bitcast(FP8X4),
-                    lhsT_scale=wd_sc[:, P * a : P * (a + 1)],
-                    rhs=h_codes[0][:, cols].bitcast(FP8X4),
-                    rhs_scale=h_sc[0][:, cols],
-                    start=True,
-                    stop=False,
-                )
-                nc.tensor.matmul_mx(
-                    out=y[:, a, :],
-                    lhsT=wd4_sb[:, 2 * P * a : 2 * P * (a + 1)].bitcast(FP4X4),
-                    lhsT_scale=wd_sc[:, N + P * a : N + P * (a + 1)],
-                    rhs=h_codes[1][:, cols].bitcast(FP8X4),
-                    rhs_scale=h_sc[1][:, cols],
-                    start=False,
-                    stop=True,
-                )
-            y_of[c] = y
-
-        def finish(c):
-            a, c0 = divmod(TOK * c, HALF)
-            result = ring.tile([P, 4, TOK], F32, name="result")
-            if c in VIA_GPSIMD:
-                y_sb = ring.tile([P, 4, TOK], F32, name="y_sb")
-                nc.scalar.copy(y_sb[:], y_of[c][:])
-                for e in range(0, 4, GSTEP):
-                    nc.gpsimd.tensor_tensor(result[:, e : e + GSTEP, :], y_sb[:, e : e + GSTEP, :], res_sb[a][:, e : e + GSTEP, c0 : c0 + TOK], ADD)
+        def down_pass(y, a, b, cols):
+            if b == 0:
+                lhsT = wd8_sb[:, P * a : P * (a + 1)].bitcast(FP8X4)
             else:
-                nc.vector.tensor_tensor(result[:], y_of[c][:], res_sb[a][:, :, c0 : c0 + TOK], ADD)
-            nc.sync.dma_start(out_rows[:, :, TOK * c : TOK * (c + 1)], result[:])
+                lhsT = wd4_sb[:, 2 * P * a : 2 * P * (a + 1)].bitcast(FP4X4)
+            nc.tensor.matmul_mx(
+                out=y,
+                lhsT=lhsT,
+                lhsT_scale=wd_sc[:, N * b + P * a : N * b + P * (a + 1)],
+                rhs=h_codes[b][:, cols].bitcast(FP8X4),
+                rhs_scale=h_sc[b][:, cols],
+                start=(b == 0),
+                stop=(b == 1),
+            )
 
-        for i in range(PACK - 1):
-            gather(i, 0, HALF)
-            gather(i, HALF, HALF)
-            if i == 0:
-                nc.vector.tensor_copy(
-                    wu_sc[:].rearrange("p (b t m) -> p b t m", b=2, t=PACK),
-                    wu_sc_in[:].rearrange("p (b m t) -> p b t m", b=2, t=PACK),
-                )
-            if i == 1:
-                round_x(0, HALF, 0)
-                round_x(HALF, HALF, 0)
-        gather(3, 0, 128)
-        round_x(0, 128, 2)
-        gather(3, 128, 128)
-        round_wg(0, 0, 64, False)
-        round_wg(0, 64, 64, WG0V)
-        quant_wg(0)
-        quant_x(0, 128)
-        round_x(128, 128, 2)
-        gather(3, 256, 256)
-        quant_x(128, 128)
-        round_x(256, 256, 2)
-        gather(3, 512, 256)
-        gather(3, 768, 256)
+        def down(c):
+            y = psum.tile([P, 4, TOK], F32, name="y", tag=TAGS[2], bufs=BUFS[2])
+            for a in range(4):
+                for b in range(2):
+                    down_pass(y[:, a, :], a, b, slice(TOK * c, TOK * (c + 1)))
+            y_of[c] = y[:]
 
-        units = [(b, c) for g in range(2) for b in range(2) for c in range(4 * g, 4 * g + 4)]
-        extra = {
-            0: [lambda: quant_x(256, 256), lambda: round_wg(1, 0, 32, False)],
-            1: [lambda: round_wg(1, 32, 32, False), lambda: round_wg(1, 64, 32, False)],
-            2: [lambda: round_wg(1, 96, 32, WG1V)],
-            3: [lambda: quant_wg(1)],
-            4: [lambda: round_x(512, 256, 2)],
-            5: [lambda: round_x(768, 256, 2)],
-            6: [lambda: quant_x(512, 512)],
-        }
-        todo = []
-        for k in range(len(units) + 6):
-            if k < len(units):
-                up(*units[k])
-                silu(*units[k])
-            if 0 <= k - 1 < len(units):
-                product(*units[k - 1])
-            ready = []
-            if 0 <= k - 2 < len(units):
-                b, c = units[k - 2]
-                n = QUANT[k - 2]
-                if n:
-                    quant_h(b, c + 1 - n, n)
-                    if b == 1:
-                        ready = list(range(c + 1 - n, c + 1))
-            if todo:
-                finish(todo.pop(0))
-            for c in ready:
-                down(c)
-            todo += ready
-            for step in extra.get(k, []):
-                step()
+        def wide(g, a, b):
+            if b == 0:
+                y = psum.tile([P, HALF], F32, name="y", tag=TAGS[2], bufs=BUFS[2])
+                y_of[4 * g + a] = y[:]
+            down_pass(y_of[4 * g + a], a, b, slice(HALF * g, HALF * (g + 1)))
+
+        def finish(c, is_wide, via_gpsimd):
+            a, c0 = divmod(TOK * c, HALF)
+            if is_wide:
+                result = ring.tile([P, HALF], F32, name="result")
+                src = res_sb[a][:, c % 4, :]
+                dst = out_rows[:, c % 4, HALF * a : HALF * (a + 1)]
+            else:
+                result = ring.tile([P, 4, TOK], F32, name="result")
+                src = res_sb[a][:, :, c0 : c0 + TOK]
+                dst = out_rows[:, :, TOK * c : TOK * (c + 1)]
+            if via_gpsimd:
+                y_sb = ring.tile(list(result.shape), F32, name="y_sb")
+                nc.scalar.copy(y_sb[:], y_of[c])
+                nc.gpsimd.tensor_tensor(result[:], y_sb[:], src, ADD)
+            else:
+                nc.vector.tensor_tensor(result[:], y_of[c], src, ADD)
+            nc.sync.dma_start(dst, result[:])
+
+        for step in ORDER.split():
+            name, args = step.split(":")[0], [int(v) for v in step.split(":")[1:]]
+            if name == "u":
+                up(*args)
+                silu(*args)
+            elif name == "f":
+                finish(args[0], args[1], args[2])
+            else:
+                {"g": gather, "rx": round_x, "qx": quant_x, "rw": round_wg, "qw": quant_wg, "p": product, "qh": quant_h,
+                 "d": down, "b": up_b, "w": wide, "pw": permute_words, "ps": permute_scales}[name](*args)

@@ -22,10 +22,10 @@ PACK = 4
 HALF = 512
 TOK = 128
 TAGS = ("ga","ub","y")
-BUFS = (2,3,3)
+BUFS = (3,3,2)
 WSPLIT = 256
-LOADS = "wu wa wus x0 wb x1 x2 x3 g0 g1 g2 g3 wd wds r0 r1"
-ORDER = "pw ps g:0:0:256 g:0:256:256 g:0:512:512 g:1:0:512 rx:0:512:0 g:1:512:512 rx:512:512:0 g:2:0:512 g:3:0:128 rx:0:128:2 qx:0:128 rw:0:0:64:1 rw:0:64:64:1 qw:0 g:3:128:128 rx:128:128:2 qx:128:128 g:3:256:256 rx:256:256:2 qx:256:256 g:2:512:384 g:2:896:128 u:0:0 b:0:0 rw:1:0:32:0 rw:1:32:32:0 u:0:1 b:0:1 p:0:0 rw:1:64:32:0 rw:1:96:32:0 g:3:512:256 u:0:2 b:0:2 p:0:1 qw:1 g:3:768:256 u:0:3 b:0:3 p:0:2 u:1:0 b:1:0 p:0:3 rx:512:256:2 u:1:1 b:1:1 p:1:0 qh:0:0:4 qx:512:256 rx:768:256:2 u:1:2 b:1:2 p:1:1 qx:768:256 u:1:3 b:1:3 p:1:2 qh:1:0:2 d:0 d:1 u:0:4 b:0:4 p:1:3 f:0:0:0 u:0:5 b:0:5 p:0:4 qh:1:2:2 f:1:0:0 d:2 d:3 u:0:6 b:0:6 p:0:5 f:2:0:0 u:0:7 b:0:7 p:0:6 f:3:0:0 u:1:4 b:1:4 p:0:7 u:1:5 b:1:5 p:1:4 qh:0:4:4 u:1:6 b:1:6 p:1:5 u:1:7 b:1:7 p:1:6 qh:1:4:2 d:4 d:5 p:1:7 qh:1:6:1 f:4:0:0 d:6 qh:1:7:1 f:5:0:0 d:7 f:6:0:0 f:7:0:0"
+LOADS = "wu wt wus x0 x1 x2 g0 x3 g1 wd wds r0 r1"
+ORDER = "pw ps g:0:0:512 g:0:512:512 g:1:0:512 rx:0:512:0 g:1:512:512 rx:512:512:0 g:2:0:512 g:2:512:512 rw:0:0:32:0 rw:0:32:96:1 qw:0 g:3:0:128 rx:0:128:2 qx:0:128 g:3:128:128 rx:128:128:2 qx:128:128 g:3:256:256 rx:256:256:2 qx:256:256 u:0:0 b:0:0 rw:1:0:32:0 rw:1:32:96:1 u:0:1 b:0:1 p:0:0 g:3:512:256 qw:1 u:0:2 b:0:2 p:0:1 g:3:768:256 u:0:3 b:0:3 p:0:2 u:1:0 b:1:0 p:0:3 rx:512:256:2 u:1:1 b:1:1 p:1:0 qh:0:0:4 qx:512:256 rx:768:256:2 u:1:2 b:1:2 p:1:1 qx:768:256 u:1:3 b:1:3 p:1:2 u:0:4 b:0:4 p:1:3 u:0:5 b:0:5 p:0:4 qh:1:0:4 w:0:0:0 w:0:0:1 w:0:1:0 w:0:1:1 u:0:6 b:0:6 p:0:5 f:0:1:0 w:0:2:0 w:0:2:1 w:0:3:0 w:0:3:1 u:0:7 b:0:7 p:0:6 f:1:1:0 u:1:4 b:1:4 p:0:7 f:2:1:0 u:1:5 b:1:5 p:1:4 qh:0:4:4 f:3:1:0 u:1:6 b:1:6 p:1:5 qh:1:4:1 d:4 u:1:7 b:1:7 p:1:6 qh:1:5:1 f:4:0:0 d:5 p:1:7 qh:1:6:1 f:5:0:0 d:6 qh:1:7:1 f:6:0:0 d:7 f:7:0:0"
 
 
 def tile_list_silu_mix_res_kernel(
@@ -58,7 +58,7 @@ def tile_list_silu_mix_res_kernel(
         wgt_sb = keep.tile([P, J], F32, name="wgt_sb")
         planes = [keep.tile([P, T], F32, name=f"plane{i}") for i in range(PACK)]
         wg_rows = wg.rearrange("(p i) r -> p i r", i=PACK)
-        wg_in = [keep.tile([P, PACK, 256], F32, name=f"wg_in{c}") for c in range(4)]
+        wg_in = [keep.tile([P, PACK, HALF], F32, name=f"wg_in{c}") for c in range(2)]
         wd8_sb = keep.tile([P, N], U32, name="wd8_sb", align_bytes=64)
         wd4_sb = keep.tile([P, 2 * N], U8, name="wd4_sb", align_bytes=64)
         res_rows = res.rearrange("(a p) j -> p a j", p=P)
@@ -71,13 +71,15 @@ def tile_list_silu_mix_res_kernel(
                 load_scales(wu_sc_in[:], wu_scales)
             elif what == "wa":
                 nc.sync.dma_start(wgt_sb[:, 0:WSPLIT], wgt[:, 0:WSPLIT])
+            elif what == "wt":
+                nc.sync.dma_start(wgt_sb[:], wgt)
             elif what == "wb":
                 nc.sync.dma_start(wgt_sb[:, WSPLIT:J], wgt[:, WSPLIT:J])
             elif what[0] == "x":
                 nc.sync.dma_start(planes[int(what[1])][:], x_rows[int(what[1])])
             elif what[0] == "g":
                 c = int(what[1])
-                nc.sync.dma_start(wg_in[c][:], wg_rows[:, :, 256 * c : 256 * (c + 1)])
+                nc.sync.dma_start(wg_in[c][:], wg_rows[:, :, HALF * c : HALF * (c + 1)])
             elif what == "wd":
                 nc.sync.dma_start(wd8_sb[:].bitcast(I32), wd8_words[0].rearrange("p n t -> p (n t)").bitcast(I32))
                 nc.sync.dma_start(wd4_sb[:].bitcast(I32), wd4_words[0].bitcast(I32))
@@ -143,9 +145,8 @@ def tile_list_silu_mix_res_kernel(
             )
 
         def round_wg(b, m0, n, on_vector):
-            c, mm = divmod(b * P + m0, 64)
             dst = wg_bf[b][:, :, m0 : m0 + n, :].rearrange("p t m i -> p m i t")
-            src = wg_in[c][:, :, 4 * mm : 4 * (mm + n)].rearrange("p i (m t) -> p m i t", t=PACK)
+            src = wg_in[b][:, :, 4 * m0 : 4 * (m0 + n)].rearrange("p i (m t) -> p m i t", t=PACK)
             if on_vector:
                 nc.vector.tensor_copy(dst, src)
             else:

@@ -21,11 +21,11 @@ P = 128
 PACK = 4
 HALF = 512
 TOK = 128
-TAGS = ("ga","ub","y")
-BUFS = (3,3,2)
-WSPLIT = 256
-LOADS = "wu wt wus x0 x1 x2 g0 x3 g1 wd wds r0 r1"
-ORDER = "pw ps g:0:0:512 g:0:512:512 g:1:0:512 rx:0:512:0 g:1:512:512 rx:512:512:0 g:2:0:512 g:2:512:512 rw:0:0:32:0 rw:0:32:96:1 qw:0 g:3:0:128 rx:0:128:2 qx:0:128 g:3:128:128 rx:128:128:2 qx:128:128 g:3:256:256 rx:256:256:2 qx:256:256 u:0:0 b:0:0 rw:1:0:32:0 rw:1:32:96:1 u:0:1 b:0:1 p:0:0 g:3:512:256 qw:1 u:0:2 b:0:2 p:0:1 g:3:768:256 u:0:3 b:0:3 p:0:2 u:1:0 b:1:0 p:0:3 rx:512:256:2 u:1:1 b:1:1 p:1:0 qh:0:0:4 qx:512:256 rx:768:256:2 u:1:2 b:1:2 p:1:1 qx:768:256 u:1:3 b:1:3 p:1:2 u:0:4 b:0:4 p:1:3 u:0:5 b:0:5 p:0:4 qh:1:0:4 w:0:0:0 w:0:0:1 w:0:1:0 w:0:1:1 u:0:6 b:0:6 p:0:5 f:0:1:0 w:0:2:0 w:0:2:1 w:0:3:0 w:0:3:1 u:0:7 b:0:7 p:0:6 f:1:1:0 u:1:4 b:1:4 p:0:7 f:2:1:0 u:1:5 b:1:5 p:1:4 qh:0:4:4 f:3:1:0 u:1:6 b:1:6 p:1:5 qh:1:4:1 d:4 u:1:7 b:1:7 p:1:6 qh:1:5:1 f:4:0:0 d:5 p:1:7 qh:1:6:1 f:5:0:0 d:6 qh:1:7:1 f:6:0:0 d:7 f:7:0:0"
+TAGS = ("ga","ub","ga")
+BUFS = (5,3,5)
+WSPLIT = 512
+LOADS = "wu wa wus x0 wb x1 x2 x3 g0 g1 wd wds r0 r1"
+ORDER = "pw ps g:0:0:512 g:0:512:512 g:1:0:512 rx:0:512:0 g:1:512:512 rx:512:512:0 g:2:0:512 g:2:512:512 g:3:0:128 rx:0:128:2 qx:0:128 g:3:128:128 rx:128:128:2 qx:128:128 g:3:256:256 rx:256:256:2 rw:0:0:48:0 rw:0:48:80:1 qw:0 qx:256:256 u:0:0 b:0:0 rw:1:0:32:0 rw:1:32:96:1 u:0:1 b:0:1 p:0:0 g:3:512:256 qw:1 u:0:2 b:0:2 p:0:1 g:3:768:256 u:0:3 b:0:3 p:0:2 v:1:0 b:1:0 p:0:3 rx:512:256:2 b:1:1 p:1:0 qh:0:0:4 rx:768:256:2 v:1:2 b:1:2 p:1:1 qx:512:512 b:1:3 p:1:2 v:0:4 b:0:4 p:1:3 b:0:5 p:0:4 qh:1:0:4 w:0:0:0 w:0:0:1 w:0:1:0 w:0:1:1 v:0:6 b:0:6 p:0:5 f:0:1:0 w:0:2:0 w:0:2:1 w:0:3:0 w:0:3:1 b:0:7 p:0:6 f:1:1:0 v:1:4 b:1:4 p:0:7 f:2:1:0 b:1:5 v:1:6 b:1:6 b:1:7 p:1:4 qh:0:4:4 f:3:1:0 p:1:5 qh:1:4:1 d:4 p:1:6 qh:1:5:1 d:5 p:1:7 qh:1:6:1 qh:1:7:1 d:6 d:7 f:4:0:0 f:5:0:0 f:6:0:0 f:7:0:0"
 
 
 def tile_list_silu_mix_res_kernel(
@@ -176,6 +176,26 @@ def tile_list_silu_mix_res_kernel(
                 )
             ga_of[b, c] = ga
 
+        def up_pair(b, c):
+            cols = slice(TOK * c, TOK * (c + 2))
+            gate = ring.tile([P, 2, 2 * TOK, 2], F32, name="gate2", bufs=2)
+            for u in range(2):
+                ga = psum.tile([P, 2, 2 * TOK], F32, name="ga", tag=TAGS[0], bufs=BUFS[0])
+                for e in range(2):
+                    t = 2 * u + e
+                    nc.tensor.matmul_mx(
+                        out=ga[:, e, :],
+                        lhsT=wg_codes[b][:, P * t : P * (t + 1)].bitcast(FP8X4),
+                        lhsT_scale=wg_sc[b][:, P * t : P * (t + 1)],
+                        rhs=xg_codes[:, cols].bitcast(FP8X4),
+                        rhs_scale=xg_sc[:, cols],
+                        start=True,
+                        stop=True,
+                    )
+                nc.scalar.activation(gate[:, u, :, :], ga[:].rearrange("p e j -> p j e"), ACT.Silu, bias=zero[:])
+            for d in range(2):
+                gate_of[b, c + d] = gate[:, :, TOK * d : TOK * (d + 1), :].rearrange("p u j e -> p j u e")
+
         def up_b(b, c):
             cols = slice(TOK * c, TOK * (c + 1))
             ub = psum.tile([P, PACK, TOK], F32, name="ub", tag=TAGS[1], bufs=BUFS[1])
@@ -195,13 +215,16 @@ def tile_list_silu_mix_res_kernel(
         def silu(b, c):
             gate = ring.tile([P, TOK, PACK], F32, name="gate")
             nc.scalar.activation(gate[:], ga_of[b, c][:].rearrange("p t j -> p j t"), ACT.Silu, bias=zero[:])
-            gate_of[b, c] = gate
+            gate_of[b, c] = gate[:].rearrange("p j (u e) -> p j u e", u=2)
 
         h_bf = [keep.tile([P, J, PACK], BF16, name=f"h_bf{b}", align_bytes=64) for b in range(2)]
 
         def product(b, c):
             nc.vector.tensor_tensor(
-                h_bf[b][:, TOK * c : TOK * (c + 1), :], ub_of[b, c][:].rearrange("p t j -> p j t"), gate_of[b, c][:], MULT
+                h_bf[b][:, TOK * c : TOK * (c + 1), :].rearrange("p j (u e) -> p j u e", u=2),
+                ub_of[b, c][:].rearrange("p (u e) j -> p j u e", u=2),
+                gate_of[b, c],
+                MULT,
             )
 
         def quant_h(b, c, n):
@@ -267,4 +290,4 @@ def tile_list_silu_mix_res_kernel(
                 finish(args[0], args[1], args[2])
             else:
                 {"g": gather, "rx": round_x, "qx": quant_x, "rw": round_wg, "qw": quant_wg, "p": product, "qh": quant_h,
-                 "d": down, "b": up_b, "w": wide, "pw": permute_words, "ps": permute_scales}[name](*args)
+                 "d": down, "b": up_b, "v": up_pair, "w": wide, "pw": permute_words, "ps": permute_scales}[name](*args)

@@ -25,7 +25,8 @@ TAGS = ("ga","ub","ga")
 BUFS = (5,3,5)
 WSPLIT = 512
 LOADS = "wu wa wus x0 wb x1 x2 x3 g0 g1 wd wds r0 r1"
-ORDER = "pw ps g:0:0:512 g:0:512:512 g:1:0:512 rx:0:512:0 g:1:512:512 rx:512:512:0 g:2:0:512 g:2:512:512 g:3:0:128 rx:0:128:2 qx:0:128 g:3:128:128 rx:128:128:2 qx:128:128 g:3:256:256 rx:256:256:2 rw:0:0:48:0 rw:0:48:80:1 qw:0 qx:256:256 u:0:0 b:0:0 rw:1:0:32:0 rw:1:32:96:1 u:0:1 b:0:1 p:0:0 g:3:512:256 qw:1 u:0:2 b:0:2 p:0:1 g:3:768:256 u:0:3 b:0:3 p:0:2 v:1:0 b:1:0 p:0:3 rx:512:256:2 b:1:1 p:1:0 qh:0:0:4 rx:768:256:2 v:1:2 b:1:2 p:1:1 qx:512:512 b:1:3 p:1:2 v:0:4 b:0:4 p:1:3 b:0:5 p:0:4 qh:1:0:4 w:0:0:0 w:0:0:1 w:0:1:0 w:0:1:1 v:0:6 b:0:6 p:0:5 f:0:1:0 w:0:2:0 w:0:2:1 w:0:3:0 w:0:3:1 b:0:7 p:0:6 f:1:1:0 v:1:4 b:1:4 p:0:7 f:2:1:0 b:1:5 v:1:6 b:1:6 b:1:7 p:1:4 qh:0:4:4 f:3:1:0 p:1:5 qh:1:4:1 d:4 p:1:6 qh:1:5:1 d:5 p:1:7 qh:1:6:1 qh:1:7:1 d:6 d:7 f:4:0:0 f:5:0:0 f:6:0:0 f:7:0:0"
+ORDER = "pw ps g:0:0:512 g:0:512:512 g:1:0:512 rx:0:512:0 g:1:512:512 rx:512:512:0 g:2:0:512 g:2:512:512 g:3:0:128 rx:0:128:2 qx:0:128 g:3:128:128 rx:128:128:2 qx:128:128 g:3:256:256 rx:256:256:2 rw:0:0:48:0 rw:0:48:80:1 qw:0 qx:256:256 u:0:0 b:0:0 rw:1:0:32:0 rw:1:32:96:1 u:0:1 b:0:1 p:0:0 g:3:512:256 qw:1 u:0:2 b:0:2 p:0:1 g:3:768:256 u:0:3 b:0:3 p:0:2 v:1:0 b:1:0 p:0:3 rx:512:256:2 b:1:1 p:1:0 qh:0:0:4 rx:768:256:2 v:1:2 b:1:2 p:1:1 qx:512:512 b:1:3 p:1:2 v:0:4 b:0:4 p:1:3 b:0:5 p:0:4 qh:1:0:4 w:0:0:0 w:0:0:1 w:0:1:0 w:0:1:1 v:0:6 b:0:6 p:0:5 f:0:1:1 w:0:2:0 w:0:2:1 w:0:3:0 w:0:3:1 b:0:7 p:0:6 f:1:1:1 v:1:4 b:1:4 p:0:7 f:2:1:0 b:1:5 v:1:6 b:1:6 b:1:7 p:1:4 qh:0:4:4 f:3:1:0 p:1:5 qh:1:4:1 p:1:6 qh:1:5:1 e:4:0 e:4:1 p:1:7 qh:1:6:1 qh:1:7:1 e:6:0 e:6:1 F:4:0 F:4:1 F:6:0 F:6:1"
+GW = 256
 
 
 def tile_list_silu_mix_res_kernel(
@@ -257,6 +258,20 @@ def tile_list_silu_mix_res_kernel(
                     down_pass(y[:, a, :], a, b, slice(TOK * c, TOK * (c + 1)))
             y_of[c] = y[:]
 
+        def down2(c, u):
+            y = psum.tile([P, 2, 2 * TOK], F32, name="y", tag=TAGS[2], bufs=BUFS[2])
+            for d in range(2):
+                for e in range(2):
+                    for b in range(2):
+                        down_pass(y[:, e, TOK * d : TOK * (d + 1)], 2 * u + e, b, slice(TOK * (c + d), TOK * (c + d + 1)))
+            y_of[c + u] = y[:]
+
+        def finish2(c, u):
+            a, c0 = divmod(TOK * c, HALF)
+            result = ring.tile([P, 2, 2 * TOK], F32, name="result")
+            nc.vector.tensor_tensor(result[:], y_of[c + u], res_sb[a][:, 2 * u : 2 * u + 2, c0 : c0 + 2 * TOK], ADD)
+            nc.sync.dma_start(out_rows[:, 2 * u : 2 * u + 2, TOK * c : TOK * (c + 2)], result[:])
+
         def wide(g, a, b):
             if b == 0:
                 y = psum.tile([P, HALF], F32, name="y", tag=TAGS[2], bufs=BUFS[2])
@@ -276,7 +291,8 @@ def tile_list_silu_mix_res_kernel(
             if via_gpsimd:
                 y_sb = ring.tile(list(result.shape), F32, name="y_sb")
                 nc.scalar.copy(y_sb[:], y_of[c])
-                nc.gpsimd.tensor_tensor(result[:], y_sb[:], src, ADD)
+                for e in range(0, HALF, GW):
+                    nc.gpsimd.tensor_tensor(result[:, e : e + GW], y_sb[:, e : e + GW], src[:, e : e + GW], ADD)
             else:
                 nc.vector.tensor_tensor(result[:], y_of[c], src, ADD)
             nc.sync.dma_start(dst, result[:])
@@ -290,4 +306,4 @@ def tile_list_silu_mix_res_kernel(
                 finish(args[0], args[1], args[2])
             else:
                 {"g": gather, "rx": round_x, "qx": quant_x, "rw": round_wg, "qw": quant_wg, "p": product, "qh": quant_h,
-                 "d": down, "b": up_b, "v": up_pair, "w": wide, "pw": permute_words, "ps": permute_scales}[name](*args)
+                 "d": down, "b": up_b, "e": down2, "F": finish2, "v": up_pair, "w": wide, "pw": permute_words, "ps": permute_scales}[name](*args)

@@ -21,12 +21,35 @@ P = 128
 PACK = 4
 HALF = 512
 TOK = 128
-TAGS = ("ga","ub","ga")
-BUFS = (5,3,5)
-WSPLIT = 512
-LOADS = "wu wa wus x0 wb x1 x2 x3 g0 g1 wd wds r0 r1"
-ORDER = "pw ps g:0:0:512 g:0:512:512 g:1:0:512 rx:0:512:0 g:1:512:512 rx:512:512:0 g:2:0:512 g:2:512:512 g:3:0:128 rx:0:128:2 qx:0:128 g:3:128:128 rx:128:128:2 qx:128:128 g:3:256:256 rx:256:256:2 rw:0:0:48:0 rw:0:48:80:1 qw:0 qx:256:256 u:0:0 b:0:0 rw:1:0:32:0 rw:1:32:96:1 u:0:1 b:0:1 p:0:0 g:3:512:256 qw:1 u:0:2 b:0:2 p:0:1 g:3:768:256 u:0:3 b:0:3 p:0:2 v:1:0 b:1:0 p:0:3 rx:512:256:2 b:1:1 p:1:0 qh:0:0:4 rx:768:256:2 v:1:2 b:1:2 p:1:1 qx:512:512 b:1:3 p:1:2 v:0:4 b:0:4 p:1:3 b:0:5 p:0:4 qh:1:0:4 w:0:0:0 w:0:0:1 w:0:1:0 w:0:1:1 v:0:6 b:0:6 p:0:5 f:0:1:1 w:0:2:0 w:0:2:1 w:0:3:0 w:0:3:1 b:0:7 p:0:6 f:1:1:1 v:1:4 b:1:4 p:0:7 f:2:1:0 b:1:5 v:1:6 b:1:6 b:1:7 p:1:4 qh:0:4:4 f:3:1:0 p:1:5 qh:1:4:1 p:1:6 qh:1:5:1 e:4:0 e:4:1 p:1:7 qh:1:6:1 qh:1:7:1 e:6:0 e:6:1 F:4:0 F:4:1 F:6:0 F:6:1"
-GW = 256
+LOADS = "wu wus wa x0 wb x1 x2 x3 ga gb gc gd wd wds r0 r1"
+GSPLIT = 64
+RW0AT = 3
+QW0AT = 3
+EARLY = 1
+Q01 = 1
+GG = ((0, 1), (0, 1), (0,))
+QLAG = 1
+ALIAS = 1
+LAG = (1, 1, 0)
+DLAG = 1
+SPLIT = 1
+VLAG = 1
+VEARLY = 0
+GFULL = 1
+GW = 512
+RW0 = 64
+RW1 = 32
+LEAD = 4
+XCH = (128, 128, 256, 256, 256)
+NG = 4
+NUB = 3
+RW1AT = 0
+YPER = 1
+TAILG = 0
+SINGLE = 4
+NGATE = 8
+NGA = 3
+YLAG = 0
 
 
 def tile_list_silu_mix_res_kernel(
@@ -71,13 +94,19 @@ def tile_list_silu_mix_res_kernel(
             elif what == "wus":
                 load_scales(wu_sc_in[:], wu_scales)
             elif what == "wa":
-                nc.sync.dma_start(wgt_sb[:, 0:WSPLIT], wgt[:, 0:WSPLIT])
-            elif what == "wt":
-                nc.sync.dma_start(wgt_sb[:], wgt)
+                nc.sync.dma_start(wgt_sb[:, 0:HALF], wgt[:, 0:HALF])
             elif what == "wb":
-                nc.sync.dma_start(wgt_sb[:, WSPLIT:J], wgt[:, WSPLIT:J])
+                nc.sync.dma_start(wgt_sb[:, HALF:J], wgt[:, HALF:J])
             elif what[0] == "x":
                 nc.sync.dma_start(planes[int(what[1])][:], x_rows[int(what[1])])
+            elif what == "ga":
+                nc.sync.dma_start(wg_in[0][:, :, 0 : 4 * RW0], wg_rows[:, :, 0 : 4 * RW0])
+            elif what == "gb":
+                nc.sync.dma_start(wg_in[0][:, :, 4 * RW0 : HALF], wg_rows[:, :, 4 * RW0 : HALF])
+            elif what == "gc":
+                nc.sync.dma_start(wg_in[1][:, :, 0 : 4 * RW1], wg_rows[:, :, HALF : HALF + 4 * RW1])
+            elif what == "gd":
+                nc.sync.dma_start(wg_in[1][:, :, 4 * RW1 : HALF], wg_rows[:, :, HALF + 4 * RW1 : R])
             elif what[0] == "g":
                 c = int(what[1])
                 nc.sync.dma_start(wg_in[c][:], wg_rows[:, :, HALF * c : HALF * (c + 1)])
@@ -93,50 +122,58 @@ def tile_list_silu_mix_res_kernel(
 
         wu_codes = keep.tile([P, 2 * R], U8, name="wu_codes", align_bytes=64)
         wu_sc = keep.tile([P, R], U8, name="wu_sc", align_bytes=64)
+        nc.vector.tensor_copy(
+            wu_codes[:].bitcast(U16).rearrange("p (b t m) -> p b t m", b=2, t=PACK),
+            wu_in[:].bitcast(U16).rearrange("p (b m t) -> p b t m", b=2, t=PACK),
+        )
+        nc.vector.tensor_copy(
+            wu_sc[:].rearrange("p (b t m) -> p b t m", b=2, t=PACK),
+            wu_sc_in[:].rearrange("p (b m t) -> p b t m", b=2, t=PACK),
+        )
 
-        def permute_words():
-            nc.vector.tensor_copy(
-                wu_codes[:].bitcast(U16).rearrange("p (b t m) -> p b t m", b=2, t=PACK),
-                wu_in[:].bitcast(U16).rearrange("p (b m t) -> p b t m", b=2, t=PACK),
-            )
-
-        def permute_scales():
-            nc.vector.tensor_copy(
-                wu_sc[:].rearrange("p (b t m) -> p b t m", b=2, t=PACK),
-                wu_sc_in[:].rearrange("p (b m t) -> p b t m", b=2, t=PACK),
-            )
-
-        picked = [keep.tile([P, PACK, HALF], F32, name=f"picked{a}") for a in range(2)]
+        picked = keep.tile([P, PACK, J], F32, name="picked")
         xg_bf = keep.tile([P, J, PACK], BF16, name="xg_bf", align_bytes=64)
         xg_codes = keep.tile([P, J], U32, name="xg_codes", align_bytes=64)
         xg_sc = keep.tile([P, J], U8, name="xg_sc", align_bytes=64)
-        wg_bf = [keep.tile([P, PACK, P, PACK], BF16, name=f"wg_bf{b}", align_bytes=64) for b in range(2)]
+        wg_bf = [keep.tile([P, PACK, P, PACK], BF16, name=f"wg_bf{b}", tag=("wg_bf0", "stage0" if ALIAS else "wg_bf1")[b], align_bytes=64) for b in range(2)]
         wg_codes = [keep.tile([P, HALF], U32, name=f"wg_codes{b}", align_bytes=64) for b in range(2)]
         wg_sc = [keep.tile([P, HALF], U8, name=f"wg_sc{b}", align_bytes=64) for b in range(2)]
-        h_codes = [keep.tile([P, J], U32, name=f"h_codes{b}", align_bytes=64) for b in range(2)]
-        h_sc = [keep.tile([P, J], U8, name=f"h_sc{b}", align_bytes=64) for b in range(2)]
+        h_bf = [keep.tile([P, 2, 2 * TOK, PACK], BF16, name=f"h_bf{n}", tag=f"stage{n}", align_bytes=64) for n in range(4)]
+        h_codes = [keep.tile([P, 2, 2 * TOK], U32, name=f"h_codes{n}", align_bytes=64) for n in range(4)]
+        h_sc = [keep.tile([P, 2, 2 * TOK], U8, name=f"h_sc{n}", align_bytes=64) for n in range(4)]
+        banks = [psum.tile([P, HALF], F32, name=f"bank{k}") for k in range(8)]
+        gates = [keep.tile([P, 2 * HALF], F32, name=f"gate{k}") for k in range(NGATE)]
+        up_uses, other_uses, gate_uses, y_uses = [], [], [], []
+
+        def next_up_bank():
+            up_uses.append(0)
+            return banks[(len(up_uses) - 1) % NUB]
+
+        def next_bank():
+            other_uses.append(0)
+            return banks[NUB + (len(other_uses) - 1) % NGA]
+
+        def next_y_bank():
+            y_uses.append(0)
+            return banks[NUB + NGA + (len(y_uses) - 1) % (8 - NUB - NGA)]
+
+        def next_gate():
+            gate_uses.append(0)
+            return gates[(len(gate_uses) - 1) % NGATE]
 
         def gather(i, j0, n):
-            a, c = divmod(j0, HALF)
             nc.vector.tensor_tensor(
-                picked[a][:, i, c : c + n],
+                picked[:, i, j0 : j0 + n],
                 planes[i][:].indirect(offsets[:, j0 // 16 : (j0 + n) // 16]),
                 wgt_sb[:, j0 : j0 + n],
                 MULT,
             )
 
         def round_x(j0, n, i0):
-            a, c = divmod(j0, HALF)
-            if i0 == 4:
-                nc.scalar.copy(
-                    xg_bf[:, j0 : j0 + n, :].rearrange("p (c e) i -> p c i e", e=4),
-                    picked[a][:, :, c : c + n].rearrange("p i (c e) -> p c i e", e=4),
-                )
-            else:
-                nc.scalar.copy(
-                    xg_bf[:, j0 : j0 + n, i0 : i0 + 2],
-                    picked[a][:, i0 : i0 + 2, c : c + n].rearrange("p i j -> p j i"),
-                )
+            nc.scalar.copy(
+                xg_bf[:, j0 : j0 + n, i0 : i0 + 2],
+                picked[:, i0 : i0 + 2, j0 : j0 + n].rearrange("p i j -> p j i"),
+            )
 
         def quant_x(j0, n):
             nc.vector.quantize_mx(
@@ -160,46 +197,40 @@ def tile_list_silu_mix_res_kernel(
                 in_=wg_bf[b][:].rearrange("p t m i -> p (t m i)"),
             )
 
-        ga_of, ub_of, gate_of, h_of, y_of = {}, {}, {}, {}, {}
+        ub_of, gate_of, y_of = {}, {}, {}
 
-        def up(b, c):
-            cols = slice(TOK * c, TOK * (c + 1))
-            ga = psum.tile([P, PACK, TOK], F32, name="ga", tag=TAGS[0], bufs=BUFS[0])
+        def gate_pass(dst, b, t, cols):
+            nc.tensor.matmul_mx(
+                out=dst,
+                lhsT=wg_codes[b][:, P * t : P * (t + 1)].bitcast(FP8X4),
+                lhsT_scale=wg_sc[b][:, P * t : P * (t + 1)],
+                rhs=xg_codes[:, cols].bitcast(FP8X4),
+                rhs_scale=xg_sc[:, cols],
+                start=True,
+                stop=True,
+            )
+
+        def gate_single(b, c):
+            ga = next_bank()[:].rearrange("p (t j) -> p t j", t=PACK)
             for t in range(PACK):
-                nc.tensor.matmul_mx(
-                    out=ga[:, t, :],
-                    lhsT=wg_codes[b][:, P * t : P * (t + 1)].bitcast(FP8X4),
-                    lhsT_scale=wg_sc[b][:, P * t : P * (t + 1)],
-                    rhs=xg_codes[:, cols].bitcast(FP8X4),
-                    rhs_scale=xg_sc[:, cols],
-                    start=True,
-                    stop=True,
-                )
-            ga_of[b, c] = ga
+                gate_pass(ga[:, t, :], b, t, slice(TOK * c, TOK * (c + 1)))
+            gate = next_gate()[:, 0:HALF].rearrange("p (j t) -> p j t", t=PACK)
+            nc.scalar.activation(gate, ga.rearrange("p t j -> p j t"), ACT.Silu, bias=zero[:])
+            gate_of[b, c] = gate.rearrange("p j (u e) -> p j u e", u=2)
 
-        def up_pair(b, c):
-            cols = slice(TOK * c, TOK * (c + 2))
-            gate = ring.tile([P, 2, 2 * TOK, 2], F32, name="gate2", bufs=2)
+        def gate_pair(b, c):
+            gate = next_gate()[:].rearrange("p (u j e) -> p u j e", u=2, e=2)
             for u in range(2):
-                ga = psum.tile([P, 2, 2 * TOK], F32, name="ga", tag=TAGS[0], bufs=BUFS[0])
+                ga = next_bank()[:].rearrange("p (e j) -> p e j", e=2)
                 for e in range(2):
-                    t = 2 * u + e
-                    nc.tensor.matmul_mx(
-                        out=ga[:, e, :],
-                        lhsT=wg_codes[b][:, P * t : P * (t + 1)].bitcast(FP8X4),
-                        lhsT_scale=wg_sc[b][:, P * t : P * (t + 1)],
-                        rhs=xg_codes[:, cols].bitcast(FP8X4),
-                        rhs_scale=xg_sc[:, cols],
-                        start=True,
-                        stop=True,
-                    )
-                nc.scalar.activation(gate[:, u, :, :], ga[:].rearrange("p e j -> p j e"), ACT.Silu, bias=zero[:])
+                    gate_pass(ga[:, e, :], b, 2 * u + e, slice(TOK * c, TOK * (c + 2)))
+                nc.scalar.activation(gate[:, u, :, :], ga.rearrange("p e j -> p j e"), ACT.Silu, bias=zero[:])
             for d in range(2):
                 gate_of[b, c + d] = gate[:, :, TOK * d : TOK * (d + 1), :].rearrange("p u j e -> p j u e")
 
-        def up_b(b, c):
+        def up(b, c):
             cols = slice(TOK * c, TOK * (c + 1))
-            ub = psum.tile([P, PACK, TOK], F32, name="ub", tag=TAGS[1], bufs=BUFS[1])
+            ub = next_up_bank()[:].rearrange("p (t j) -> p t j", t=PACK)
             for t in range(PACK):
                 s = PACK * b + t
                 nc.tensor.matmul_mx(
@@ -213,30 +244,22 @@ def tile_list_silu_mix_res_kernel(
                 )
             ub_of[b, c] = ub
 
-        def silu(b, c):
-            gate = ring.tile([P, TOK, PACK], F32, name="gate")
-            nc.scalar.activation(gate[:], ga_of[b, c][:].rearrange("p t j -> p j t"), ACT.Silu, bias=zero[:])
-            gate_of[b, c] = gate[:].rearrange("p j (u e) -> p j u e", u=2)
-
-        h_bf = [keep.tile([P, J, PACK], BF16, name=f"h_bf{b}", align_bytes=64) for b in range(2)]
-
         def product(b, c):
             nc.vector.tensor_tensor(
-                h_bf[b][:, TOK * c : TOK * (c + 1), :].rearrange("p j (u e) -> p j u e", u=2),
-                ub_of[b, c][:].rearrange("p (u e) j -> p j u e", u=2),
+                h_bf[c // 2][:, b, TOK * (c % 2) : TOK * (c % 2 + 1), :].rearrange("p j (u e) -> p j u e", u=2),
+                ub_of[b, c].rearrange("p (u e) j -> p j u e", u=2),
                 gate_of[b, c],
                 MULT,
             )
 
-        def quant_h(b, c, n):
-            cols = slice(TOK * c, TOK * (c + n))
+        def quant_h(n, c0, w):
             nc.vector.quantize_mx(
-                out=h_codes[b][:, cols].bitcast(FP8X4),
-                scales=h_sc[b][:, cols],
-                in_=h_bf[b][:, cols, :].rearrange("p j t -> p (j t)"),
+                out=h_codes[n][:].rearrange("p b j -> p (b j)")[:, c0 : c0 + w].bitcast(FP8X4),
+                scales=h_sc[n][:].rearrange("p b j -> p (b j)")[:, c0 : c0 + w],
+                in_=h_bf[n][:].rearrange("p b j t -> p (b j t)")[:, PACK * c0 : PACK * (c0 + w)],
             )
 
-        def down_pass(y, a, b, cols):
+        def down_pass(y, a, b, n, c0, w, start, stop):
             if b == 0:
                 lhsT = wd8_sb[:, P * a : P * (a + 1)].bitcast(FP8X4)
             else:
@@ -245,65 +268,122 @@ def tile_list_silu_mix_res_kernel(
                 out=y,
                 lhsT=lhsT,
                 lhsT_scale=wd_sc[:, N * b + P * a : N * b + P * (a + 1)],
-                rhs=h_codes[b][:, cols].bitcast(FP8X4),
-                rhs_scale=h_sc[b][:, cols],
-                start=(b == 0),
-                stop=(b == 1),
+                rhs=h_codes[n][:, b, c0 : c0 + w].bitcast(FP8X4),
+                rhs_scale=h_sc[n][:, b, c0 : c0 + w],
+                start=start,
+                stop=stop,
             )
 
-        def down(c):
-            y = psum.tile([P, 4, TOK], F32, name="y", tag=TAGS[2], bufs=BUFS[2])
+        def down_pair(n, u):
+            y = next_y_bank()[:]
+            for e in range(2):
+                c0 = 2 * TOK * e
+                down_pass(y[:, c0 : c0 + 2 * TOK], 2 * u + e, 0, n, 0, 2 * TOK, True, False)
+                for d in range(2):
+                    down_pass(y[:, c0 + TOK * d : c0 + TOK * (d + 1)], 2 * u + e, 1, n, TOK * d, TOK, False, d == 1)
+            cols = slice(2 * TOK * n, 2 * TOK * (n + 1))
+            c0 = 2 * TOK * (n % 2)
+            y_of[n, u] = (y, res_sb[n // 2][:, 2 * u : 2 * u + 2, c0 : c0 + 2 * TOK], out_rows[:, 2 * u : 2 * u + 2, cols])
+
+        def open_narrow(d):
+            y = next_bank()[:]
             for a in range(4):
-                for b in range(2):
-                    down_pass(y[:, a, :], a, b, slice(TOK * c, TOK * (c + 1)))
-            y_of[c] = y[:]
+                down_pass(y[:, TOK * a : TOK * (a + 1)], a, 0, 3, TOK * d, TOK, a == 0, False)
+            c0 = TOK * (2 + d)
+            y_of[3, d] = (y, res_sb[1][:, :, c0 : c0 + TOK], out_rows[:, :, HALF + c0 : HALF + c0 + TOK])
 
-        def down2(c, u):
-            y = psum.tile([P, 2, 2 * TOK], F32, name="y", tag=TAGS[2], bufs=BUFS[2])
-            for d in range(2):
-                for e in range(2):
-                    for b in range(2):
-                        down_pass(y[:, e, TOK * d : TOK * (d + 1)], 2 * u + e, b, slice(TOK * (c + d), TOK * (c + d + 1)))
-            y_of[c + u] = y[:]
+        def close_narrow(d):
+            y = y_of[3, d][0]
+            for a in range(4):
+                down_pass(y[:, TOK * a : TOK * (a + 1)], a, 1, 3, TOK * d, TOK, False, a == 3)
 
-        def finish2(c, u):
-            a, c0 = divmod(TOK * c, HALF)
-            result = ring.tile([P, 2, 2 * TOK], F32, name="result")
-            nc.vector.tensor_tensor(result[:], y_of[c + u], res_sb[a][:, 2 * u : 2 * u + 2, c0 : c0 + 2 * TOK], ADD)
-            nc.sync.dma_start(out_rows[:, 2 * u : 2 * u + 2, TOK * c : TOK * (c + 2)], result[:])
+        def finish_vector(n, u, a0, a1):
+            y, src, dst = y_of[n, u]
+            result = ring.tile([P, a1 - a0, src.shape[2]], F32, name="result")
+            nc.vector.tensor_tensor(result[:], y.rearrange("p (a j) -> p a j", a=src.shape[1])[:, a0:a1], src[:, a0:a1], ADD)
+            nc.sync.dma_start(dst[:, a0:a1], result[:])
 
-        def wide(g, a, b):
-            if b == 0:
-                y = psum.tile([P, HALF], F32, name="y", tag=TAGS[2], bufs=BUFS[2])
-                y_of[4 * g + a] = y[:]
-            down_pass(y_of[4 * g + a], a, b, slice(HALF * g, HALF * (g + 1)))
+        def evacuate(n, u):
+            y, src, dst = y_of[n, u]
+            y_sb = ring.tile(list(src.shape), F32, name="y_sb")
+            nc.scalar.copy(y_sb[:], y.rearrange("p (a j) -> p a j", a=src.shape[1]))
+            y_of[n, u] = (y_sb, src, dst)
 
-        def finish(c, is_wide, via_gpsimd):
-            a, c0 = divmod(TOK * c, HALF)
-            if is_wide:
-                result = ring.tile([P, HALF], F32, name="result")
-                src = res_sb[a][:, c % 4, :]
-                dst = out_rows[:, c % 4, HALF * a : HALF * (a + 1)]
+        def finish_gpsimd(n, us):
+            result = keep.tile([P, 2, 2, 2 * TOK], F32, name=f"result{n}", tag=f"stage{n + 1}" if LAG[n] else f"res{n}", align_bytes=64)
+            for u in us:
+                y_sb, src, dst = y_of[n, u]
+                if GW == HALF:
+                    nc.gpsimd.tensor_tensor(result[:, u], y_sb[:], src, ADD)
+                else:
+                    for e in range(2):
+                        nc.gpsimd.tensor_tensor(result[:, u, e], y_sb[:, e], src[:, e], ADD)
+                nc.sync.dma_start(dst, result[:, u])
+
+        for i in range(3):
+            if GFULL and i != 1 and i != 0:
+                gather(i, 0, J)
             else:
-                result = ring.tile([P, 4, TOK], F32, name="result")
-                src = res_sb[a][:, :, c0 : c0 + TOK]
-                dst = out_rows[:, :, TOK * c : TOK * (c + 1)]
-            if via_gpsimd:
-                y_sb = ring.tile(list(result.shape), F32, name="y_sb")
-                nc.scalar.copy(y_sb[:], y_of[c])
-                for e in range(0, HALF, GW):
-                    nc.gpsimd.tensor_tensor(result[:, e : e + GW], y_sb[:, e : e + GW], src[:, e : e + GW], ADD)
-            else:
-                nc.vector.tensor_tensor(result[:], y_of[c], src, ADD)
-            nc.sync.dma_start(dst, result[:])
-
-        for step in ORDER.split():
-            name, args = step.split(":")[0], [int(v) for v in step.split(":")[1:]]
-            if name == "u":
-                up(*args)
-                silu(*args)
-            elif name == "f":
-                finish(args[0], args[1], args[2])
-            else:
-                {"g": gather, "rx": round_x, "qx": quant_x, "rw": round_wg, "qw": quant_wg, "p": product, "qh": quant_h,
-                 "d": down, "b": up_b, "e": down2, "F": finish2, "v": up_pair, "w": wide, "pw": permute_words, "ps": permute_scales}[name](*args)
+                for a in range(2):
+                    gather(i, HALF * a, HALF)
+                    if i == 1:
+                        round_x(HALF * a, HALF, 0)
+        j0 = 0
+        for k, n in enumerate(XCH):
+            if k == RW0AT:
+                round_wg(0, 0, RW0, False)
+            gather(3, j0, n)
+            round_x(j0, n, 2)
+            quant_x(j0, n)
+            j0 += n
+            if k == QW0AT:
+                round_wg(0, RW0, P - RW0, True)
+                quant_wg(0)
+        round_wg(1, 0, RW1, False)
+        round_wg(1, RW1, P - RW1, True)
+        quant_wg(1)
+        units = [(b, c + d) for c in range(0, 8, 2) for b in range(2) for d in range(2)]
+        for k in range(len(units) + 1):
+            n, step = divmod(k, 4)
+            if k < len(units):
+                b, c = units[k]
+                if k < SINGLE:
+                    gate_single(b, c)
+                elif c % 2 == 0:
+                    gate_pair(b, c)
+                up(b, c)
+            if k >= 1:
+                product(*units[k - 1])
+            if n >= 1 and step == QLAG and n < 4:
+                quant_h(n - 1, 0, HALF)
+                if n >= 2 and LAG[n - 2]:
+                    finish_gpsimd(n - 2, GG[n - 2])
+            for m in range(3):
+                for u in range(2):
+                    at = 4 * (m + 1) + QLAG + DLAG + u
+                    if k == at:
+                        down_pair(m, u)
+                        if u in GG[m]:
+                            evacuate(m, u)
+                            if not LAG[m] and u == GG[m][-1]:
+                                finish_gpsimd(m, GG[m])
+                    if k == min(at + VLAG, len(units)) and u not in GG[m] and (m < 2 or VEARLY):
+                        finish_vector(m, u, 0, 2)
+            if k == len(units) - 1:
+                quant_h(3, 0, 2 * TOK)
+                open_narrow(0)
+                open_narrow(1)
+        for d in range(2):
+            quant_h(3, (2 + d) * TOK, TOK)
+            close_narrow(d)
+        if LAG[2]:
+            finish_gpsimd(2, GG[2])
+        for u in range(2):
+            if u not in GG[2] and not VEARLY:
+                finish_vector(2, u, 0, 2)
+        finish_vector(3, 0, 0, 4)
+        if SPLIT:
+            finish_vector(3, 1, 0, 2)
+            finish_vector(3, 1, 2, 4)
+        else:
+            finish_vector(3, 1, 0, 4)

@@ -21,24 +21,29 @@ P = 128
 PACK = 4
 HALF = 512
 TOK = 128
-LOADS = "wu wus wa x0 wb x1 x2 x3 ga gb gc gd wd wds r0 r1"
+LOADS = "wu wa wus x0 wb x1 x2 x3 g0 g1 wd r0 r1"
 GSPLIT = 64
-RW0AT = 3
-QW0AT = 3
+RW0AT = 0
+QW0AT = 2
 EARLY = 1
 Q01 = 1
-GG = ((0, 1), (0, 1), (0,))
+GG = ((0,), (0,), ())
 QLAG = 1
 ALIAS = 1
-LAG = (1, 1, 0)
+HOLD = 0
+MERGE = 1
+Q6 = 1
+AHEAD = 0
+QD = 1
+LAG = (0, 0, 0)
 DLAG = 1
 SPLIT = 1
 VLAG = 1
-VEARLY = 0
+VEARLY = 1
 GFULL = 1
 GW = 512
-RW0 = 64
-RW1 = 32
+RW0 = 32
+RW1 = 80
 LEAD = 4
 XCH = (128, 128, 256, 256, 256)
 NG = 4
@@ -65,17 +70,15 @@ def tile_list_silu_mix_res_kernel(
         nc.sync.dma_start(offsets[:], offs)
 
         wu_sc_in = keep.tile([P, R], U8, name="wu_sc_in", align_bytes=64)
-        wd_sc = keep.tile([P, 2 * N], U8, name="wd_sc", align_bytes=64)
         nc.vector.memset(wu_sc_in[:].bitcast(I32), 0)
         zero_in = keep.tile([P, 1], F32, name="zero_in")
         nc.vector.memset(zero_in[:], 0.0)
-        nc.vector.memset(wd_sc[:].bitcast(I32), 0)
         zero = keep.tile([P, 1], F32, name="zero")
         nc.scalar.activation(zero[:], zero_in[:], ACT.Silu)
 
-        def load_scales(dst, src):
+        def load_scales(dst, src, queue):
             for q in range(4):
-                nc.sync.dma_start(dst[32 * q : 32 * q + 4, :].bitcast(I32), src[0, 4 * q : 4 * q + 4, :].bitcast(I32))
+                queue.dma_start(dst[32 * q : 32 * q + 4, :].bitcast(I32), src[0, 4 * q : 4 * q + 4, :].bitcast(I32))
 
         wu_in = keep.tile([P, 2 * R], U8, name="wu_in", align_bytes=64)
         x_rows = xT.rearrange("(p i) t -> i p t", i=PACK)
@@ -92,7 +95,7 @@ def tile_list_silu_mix_res_kernel(
             if what == "wu":
                 nc.sync.dma_start(wu_in[:].bitcast(I32), wu_words[0].bitcast(I32))
             elif what == "wus":
-                load_scales(wu_sc_in[:], wu_scales)
+                load_scales(wu_sc_in[:], wu_scales, nc.sync)
             elif what == "wa":
                 nc.sync.dma_start(wgt_sb[:, 0:HALF], wgt[:, 0:HALF])
             elif what == "wb":
@@ -113,9 +116,6 @@ def tile_list_silu_mix_res_kernel(
             elif what == "wd":
                 nc.sync.dma_start(wd8_sb[:].bitcast(I32), wd8_words[0].rearrange("p n t -> p (n t)").bitcast(I32))
                 nc.sync.dma_start(wd4_sb[:].bitcast(I32), wd4_words[0].bitcast(I32))
-            elif what == "wds":
-                load_scales(wd_sc[:, 0:N], wd8_scales)
-                load_scales(wd_sc[:, N : 2 * N], wd4_scales)
             elif what[0] == "r":
                 a = int(what[1])
                 nc.sync.dma_start(res_sb[a][:], res_rows[:, :, HALF * a : HALF * (a + 1)])
@@ -130,14 +130,17 @@ def tile_list_silu_mix_res_kernel(
             wu_sc[:].rearrange("p (b t m) -> p b t m", b=2, t=PACK),
             wu_sc_in[:].rearrange("p (b m t) -> p b t m", b=2, t=PACK),
         )
+        wd_sc = wu_sc_in
+        load_scales(wd_sc[:, 0:N], wd8_scales, nc.gpsimd)
+        load_scales(wd_sc[:, N : 2 * N], wd4_scales, nc.gpsimd)
 
         picked = keep.tile([P, PACK, J], F32, name="picked")
         xg_bf = keep.tile([P, J, PACK], BF16, name="xg_bf", align_bytes=64)
-        xg_codes = keep.tile([P, J], U32, name="xg_codes", align_bytes=64)
-        xg_sc = keep.tile([P, J], U8, name="xg_sc", align_bytes=64)
         wg_bf = [keep.tile([P, PACK, P, PACK], BF16, name=f"wg_bf{b}", tag=("wg_bf0", "stage0" if ALIAS else "wg_bf1")[b], align_bytes=64) for b in range(2)]
         wg_codes = [keep.tile([P, HALF], U32, name=f"wg_codes{b}", align_bytes=64) for b in range(2)]
         wg_sc = [keep.tile([P, HALF], U8, name=f"wg_sc{b}", align_bytes=64) for b in range(2)]
+        xg_codes = [keep.tile([P, HALF], U32, name=f"xg_codes{a}", tag=("xc0", "wg_bf0" if HOLD else "xc1")[a], align_bytes=64) for a in range(2)]
+        xg_sc = [keep.tile([P, HALF], U8, name=f"xg_sc{a}", align_bytes=64) for a in range(2)]
         h_bf = [keep.tile([P, 2, 2 * TOK, PACK], BF16, name=f"h_bf{n}", tag=f"stage{n}", align_bytes=64) for n in range(4)]
         h_codes = [keep.tile([P, 2, 2 * TOK], U32, name=f"h_codes{n}", align_bytes=64) for n in range(4)]
         h_sc = [keep.tile([P, 2, 2 * TOK], U8, name=f"h_sc{n}", align_bytes=64) for n in range(4)]
@@ -176,9 +179,10 @@ def tile_list_silu_mix_res_kernel(
             )
 
         def quant_x(j0, n):
+            a, c = divmod(j0, HALF)
             nc.vector.quantize_mx(
-                out=xg_codes[:, j0 : j0 + n].bitcast(FP8X4),
-                scales=xg_sc[:, j0 : j0 + n],
+                out=xg_codes[a][:, c : c + n].bitcast(FP8X4),
+                scales=xg_sc[a][:, c : c + n],
                 in_=xg_bf[:, j0 : j0 + n, :].rearrange("p j i -> p (j i)"),
             )
 
@@ -204,24 +208,24 @@ def tile_list_silu_mix_res_kernel(
                 out=dst,
                 lhsT=wg_codes[b][:, P * t : P * (t + 1)].bitcast(FP8X4),
                 lhsT_scale=wg_sc[b][:, P * t : P * (t + 1)],
-                rhs=xg_codes[:, cols].bitcast(FP8X4),
-                rhs_scale=xg_sc[:, cols],
+                rhs=xg_codes[cols.start // HALF][:, cols.start % HALF : cols.start % HALF + cols.stop - cols.start].bitcast(FP8X4),
+                rhs_scale=xg_sc[cols.start // HALF][:, cols.start % HALF : cols.start % HALF + cols.stop - cols.start],
                 start=True,
                 stop=True,
             )
 
-        def gate_single(b, c):
-            ga = next_bank()[:].rearrange("p (t j) -> p t j", t=PACK)
+        def gate_single(b, c, bank):
+            ga = bank()[:].rearrange("p (t j) -> p t j", t=PACK)
             for t in range(PACK):
                 gate_pass(ga[:, t, :], b, t, slice(TOK * c, TOK * (c + 1)))
             gate = next_gate()[:, 0:HALF].rearrange("p (j t) -> p j t", t=PACK)
             nc.scalar.activation(gate, ga.rearrange("p t j -> p j t"), ACT.Silu, bias=zero[:])
             gate_of[b, c] = gate.rearrange("p j (u e) -> p j u e", u=2)
 
-        def gate_pair(b, c):
+        def gate_pair(b, c, bank):
             gate = next_gate()[:].rearrange("p (u j e) -> p u j e", u=2, e=2)
             for u in range(2):
-                ga = next_bank()[:].rearrange("p (e j) -> p e j", e=2)
+                ga = bank()[:].rearrange("p (e j) -> p e j", e=2)
                 for e in range(2):
                     gate_pass(ga[:, e, :], b, 2 * u + e, slice(TOK * c, TOK * (c + 2)))
                 nc.scalar.activation(gate[:, u, :, :], ga.rearrange("p e j -> p j e"), ACT.Silu, bias=zero[:])
@@ -237,8 +241,8 @@ def tile_list_silu_mix_res_kernel(
                     out=ub[:, t, :],
                     lhsT=wu_codes[:, 2 * P * s : 2 * P * (s + 1)].bitcast(FP4X4),
                     lhsT_scale=wu_sc[:, P * s : P * (s + 1)],
-                    rhs=xg_codes[:, cols].bitcast(FP8X4),
-                    rhs_scale=xg_sc[:, cols],
+                    rhs=xg_codes[c // 4][:, TOK * (c % 4) : TOK * (c % 4 + 1)].bitcast(FP8X4),
+                    rhs_scale=xg_sc[c // 4][:, TOK * (c % 4) : TOK * (c % 4 + 1)],
                     start=True,
                     stop=True,
                 )
@@ -310,7 +314,7 @@ def tile_list_silu_mix_res_kernel(
             y_of[n, u] = (y_sb, src, dst)
 
         def finish_gpsimd(n, us):
-            result = keep.tile([P, 2, 2, 2 * TOK], F32, name=f"result{n}", tag=f"stage{n + 1}" if LAG[n] else f"res{n}", align_bytes=64)
+            result = keep.tile([P, 2, 2, 2 * TOK], F32, name=f"result{n}", tag=f"stage{n + 1}" if LAG[n] else f"late{n}", align_bytes=64)
             for u in us:
                 y_sb, src, dst = y_of[n, u]
                 if GW == HALF:
@@ -330,14 +334,18 @@ def tile_list_silu_mix_res_kernel(
                         round_x(HALF * a, HALF, 0)
         j0 = 0
         for k, n in enumerate(XCH):
-            if k == RW0AT:
+            if k == RW0AT and RW0 > 0:
                 round_wg(0, 0, RW0, False)
             gather(3, j0, n)
             round_x(j0, n, 2)
-            quant_x(j0, n)
+            if j0 < HALF or not MERGE:
+                quant_x(j0, n)
+            elif j0 + n == J:
+                quant_x(HALF, HALF)
             j0 += n
             if k == QW0AT:
                 round_wg(0, RW0, P - RW0, True)
+            if k == QW0AT + QD:
                 quant_wg(0)
         round_wg(1, 0, RW1, False)
         round_wg(1, RW1, P - RW1, True)
@@ -348,9 +356,11 @@ def tile_list_silu_mix_res_kernel(
             if k < len(units):
                 b, c = units[k]
                 if k < SINGLE:
-                    gate_single(b, c)
-                elif c % 2 == 0:
-                    gate_pair(b, c)
+                    gate_single(b, c, next_bank)
+                elif c % 2 == 0 and (b, c) not in gate_of:
+                    gate_pair(b, c, next_bank)
+                if k == 1 and AHEAD:
+                    gate_pair(0, 2, next_y_bank)
                 up(b, c)
             if k >= 1:
                 product(*units[k - 1])
@@ -373,7 +383,10 @@ def tile_list_silu_mix_res_kernel(
                 quant_h(3, 0, 2 * TOK)
                 open_narrow(0)
                 open_narrow(1)
-        for d in range(2):
+                if Q6:
+                    quant_h(3, 2 * TOK, TOK)
+                    close_narrow(0)
+        for d in range(Q6, 2):
             quant_h(3, (2 + d) * TOK, TOK)
             close_narrow(d)
         if LAG[2]:

@@ -35,7 +35,7 @@ MERGE = 1
 Q6 = 1
 AHEAD = 0
 QD = 1
-LAG = (0, 0, 0)
+LAG = (1, 1, 0)
 DLAG = 1
 SPLIT = 1
 VLAG = 1

@@ -69,7 +69,7 @@ def tile_list_silu_mix_res_kernel(
         offsets = keep.tile([P, J // 16], U16, name="offsets")
         nc.sync.dma_start(offsets[:], offs)
 
-        wu_sc_in = keep.tile([P, R], U8, name="wu_sc_in", align_bytes=64)
+        wu_sc_in = keep.tile([P, R], U8, name="wu_sc_in", align_bytes=256)
         nc.vector.memset(wu_sc_in[:].bitcast(I32), 0)
         zero_in = keep.tile([P, 1], F32, name="zero_in")
         nc.vector.memset(zero_in[:], 0.0)
@@ -80,14 +80,14 @@ def tile_list_silu_mix_res_kernel(
             for q in range(4):
                 queue.dma_start(dst[32 * q : 32 * q + 4, :].bitcast(I32), src[0, 4 * q : 4 * q + 4, :].bitcast(I32))
 
-        wu_in = keep.tile([P, 2 * R], U8, name="wu_in", align_bytes=64)
+        wu_in = keep.tile([P, 2 * R], U8, name="wu_in", align_bytes=256)
         x_rows = xT.rearrange("(p i) t -> i p t", i=PACK)
         wgt_sb = keep.tile([P, J], F32, name="wgt_sb")
         planes = [keep.tile([P, T], F32, name=f"plane{i}") for i in range(PACK)]
         wg_rows = wg.rearrange("(p i) r -> p i r", i=PACK)
         wg_in = [keep.tile([P, PACK, HALF], F32, name=f"wg_in{c}") for c in range(2)]
-        wd8_sb = keep.tile([P, N], U32, name="wd8_sb", align_bytes=64)
-        wd4_sb = keep.tile([P, 2 * N], U8, name="wd4_sb", align_bytes=64)
+        wd8_sb = keep.tile([P, N], U32, name="wd8_sb", align_bytes=256)
+        wd4_sb = keep.tile([P, 2 * N], U8, name="wd4_sb", align_bytes=256)
         res_rows = res.rearrange("(a p) j -> p a j", p=P)
         out_rows = out.rearrange("(a p) j -> p a j", p=P)
         res_sb = [keep.tile([P, 4, HALF], F32, name=f"res{a}") for a in range(2)]
@@ -120,8 +120,8 @@ def tile_list_silu_mix_res_kernel(
                 a = int(what[1])
                 nc.sync.dma_start(res_sb[a][:], res_rows[:, :, HALF * a : HALF * (a + 1)])
 
-        wu_codes = keep.tile([P, 2 * R], U8, name="wu_codes", align_bytes=64)
-        wu_sc = keep.tile([P, R], U8, name="wu_sc", align_bytes=64)
+        wu_codes = keep.tile([P, 2 * R], U8, name="wu_codes", align_bytes=256)
+        wu_sc = keep.tile([P, R], U8, name="wu_sc", align_bytes=256)
         nc.vector.tensor_copy(
             wu_codes[:].bitcast(U16).rearrange("p (b t m) -> p b t m", b=2, t=PACK),
             wu_in[:].bitcast(U16).rearrange("p (b m t) -> p b t m", b=2, t=PACK),
@@ -135,15 +135,15 @@ def tile_list_silu_mix_res_kernel(
         load_scales(wd_sc[:, N : 2 * N], wd4_scales, nc.gpsimd)
 
         picked = keep.tile([P, PACK, J], F32, name="picked")
-        xg_bf = keep.tile([P, J, PACK], BF16, name="xg_bf", align_bytes=64)
-        wg_bf = [keep.tile([P, PACK, P, PACK], BF16, name=f"wg_bf{b}", tag=("wg_bf0", "stage0" if ALIAS else "wg_bf1")[b], align_bytes=64) for b in range(2)]
-        wg_codes = [keep.tile([P, HALF], U32, name=f"wg_codes{b}", align_bytes=64) for b in range(2)]
-        wg_sc = [keep.tile([P, HALF], U8, name=f"wg_sc{b}", align_bytes=64) for b in range(2)]
-        xg_codes = [keep.tile([P, HALF], U32, name=f"xg_codes{a}", tag=("xc0", "wg_bf0" if HOLD else "xc1")[a], align_bytes=64) for a in range(2)]
-        xg_sc = [keep.tile([P, HALF], U8, name=f"xg_sc{a}", align_bytes=64) for a in range(2)]
-        h_bf = [keep.tile([P, 2, 2 * TOK, PACK], BF16, name=f"h_bf{n}", tag=f"stage{n}", align_bytes=64) for n in range(4)]
-        h_codes = [keep.tile([P, 2, 2 * TOK], U32, name=f"h_codes{n}", align_bytes=64) for n in range(4)]
-        h_sc = [keep.tile([P, 2, 2 * TOK], U8, name=f"h_sc{n}", align_bytes=64) for n in range(4)]
+        xg_bf = keep.tile([P, J, PACK], BF16, name="xg_bf", align_bytes=256)
+        wg_bf = [keep.tile([P, PACK, P, PACK], BF16, name=f"wg_bf{b}", tag=("wg_bf0", "stage0" if ALIAS else "wg_bf1")[b], align_bytes=256) for b in range(2)]
+        wg_codes = [keep.tile([P, HALF], U32, name=f"wg_codes{b}", align_bytes=256) for b in range(2)]
+        wg_sc = [keep.tile([P, HALF], U8, name=f"wg_sc{b}", align_bytes=256) for b in range(2)]
+        xg_codes = [keep.tile([P, HALF], U32, name=f"xg_codes{a}", tag=("xc0", "wg_bf0" if HOLD else "xc1")[a], align_bytes=256) for a in range(2)]
+        xg_sc = [keep.tile([P, HALF], U8, name=f"xg_sc{a}", align_bytes=256) for a in range(2)]
+        h_bf = [keep.tile([P, 2, 2 * TOK, PACK], BF16, name=f"h_bf{n}", tag=f"stage{n}", align_bytes=256) for n in range(4)]
+        h_codes = [keep.tile([P, 2, 2 * TOK], U32, name=f"h_codes{n}", align_bytes=256) for n in range(4)]
+        h_sc = [keep.tile([P, 2, 2 * TOK], U8, name=f"h_sc{n}", align_bytes=256) for n in range(4)]
         banks = [psum.tile([P, HALF], F32, name=f"bank{k}") for k in range(8)]
         gates = [keep.tile([P, 2 * HALF], F32, name=f"gate{k}") for k in range(NGATE)]
         up_uses, other_uses, gate_uses, y_uses = [], [], [], []
@@ -314,7 +314,7 @@ def tile_list_silu_mix_res_kernel(
             y_of[n, u] = (y_sb, src, dst)
 
         def finish_gpsimd(n, us):
-            result = keep.tile([P, 2, 2, 2 * TOK], F32, name=f"result{n}", tag=f"stage{n + 1}" if LAG[n] else f"late{n}", align_bytes=64)
+            result = keep.tile([P, 2, 2, 2 * TOK], F32, name=f"result{n}", tag=f"stage{n + 1}" if LAG[n] else f"late{n}", align_bytes=256)
             for u in us:
                 y_sb, src, dst = y_of[n, u]
                 if GW == HALF:

@@ -15,46 +15,21 @@ FP8X4 = mybir.dt.float8_e4m3fn_x4
 FP4X4 = mybir.dt.float4_e2m1fn_x4
 MULT = mybir.AluOpType.mult
 ADD = mybir.AluOpType.add
-ACT = mybir.ActivationFunctionType
+SILU = mybir.ActivationFunctionType.Silu
 
 P = 128
 PACK = 4
 HALF = 512
-TOK = 128
-LOADS = "wu wa wus x0 wb x1 x2 x3 g0 g1 wd r0 r1"
-GSPLIT = 64
-RW0AT = 0
-QW0AT = 2
-EARLY = 1
-Q01 = 1
-GG = ((0,), (0,), ())
-QLAG = 1
-ALIAS = 1
-HOLD = 0
-MERGE = 1
-Q6 = 1
-AHEAD = 0
-QD = 1
-LAG = (1, 1, 0)
-DLAG = 1
-SPLIT = 1
-VLAG = 1
-VEARLY = 1
-GFULL = 1
-GW = 512
-RW0 = 32
-RW1 = 80
-LEAD = 4
-XCH = (128, 128, 256, 256, 256)
-NG = 4
-NUB = 3
-RW1AT = 0
-YPER = 1
-TAILG = 0
-SINGLE = 4
-NGATE = 8
-NGA = 3
-YLAG = 0
+CHUNK = 128
+GROUP = 2 * CHUNK
+GROUPS = J // GROUP
+ALIGN = 256
+LAST_PLANE_PIECES = (128, 128, 256, 256, 256)
+SCALAR_SHARE = (32, 96)
+QUAD = 32
+HEAD = 16
+UP_BANKS, GATE_BANKS, OUT_BANKS = 3, 3, 2
+GATE_TILES = 8
 
 
 def tile_list_silu_mix_res_kernel(
@@ -67,102 +42,107 @@ def tile_list_silu_mix_res_kernel(
         psum = ctx.enter_context(tc.psum_pool(name="psum", bufs=1))
 
         offsets = keep.tile([P, J // 16], U16, name="offsets")
-        nc.sync.dma_start(offsets[:], offs)
 
-        wu_sc_in = keep.tile([P, R], U8, name="wu_sc_in", align_bytes=256)
-        nc.vector.memset(wu_sc_in[:].bitcast(I32), 0)
+        scales_in = keep.tile([P, R], U8, name="scales_in", align_bytes=ALIGN)
+        nc.vector.memset(scales_in[:].bitcast(I32), 0)
         zero_in = keep.tile([P, 1], F32, name="zero_in")
         nc.vector.memset(zero_in[:], 0.0)
         zero = keep.tile([P, 1], F32, name="zero")
-        nc.scalar.activation(zero[:], zero_in[:], ACT.Silu)
 
-        def load_scales(dst, src, queue):
+        def load_scales(queue, dst, src):
             for q in range(4):
                 queue.dma_start(dst[32 * q : 32 * q + 4, :].bitcast(I32), src[0, 4 * q : 4 * q + 4, :].bitcast(I32))
 
-        wu_in = keep.tile([P, 2 * R], U8, name="wu_in", align_bytes=256)
-        x_rows = xT.rearrange("(p i) t -> i p t", i=PACK)
-        wgt_sb = keep.tile([P, J], F32, name="wgt_sb")
+        wu_in = keep.tile([P, 2 * R], U8, name="wu_in", align_bytes=ALIGN)
+        wgt_sb = keep.tile([P, J], F32, name="wgt_sb", align_bytes=ALIGN)
         planes = [keep.tile([P, T], F32, name=f"plane{i}") for i in range(PACK)]
+        wg_in = [keep.tile([P, PACK, HALF], F32, name=f"wg_in{b}") for b in range(2)]
+        wd8_sb = keep.tile([P, N], U32, name="wd8_sb", align_bytes=ALIGN)
+        wd4_sb = keep.tile([P, 2 * N], U8, name="wd4_sb", align_bytes=ALIGN)
+        res_sb = [keep.tile([P, N // P, HALF], F32, name=f"res{s}") for s in range(2)]
+        x_rows = xT.rearrange("(p i) t -> i p t", i=PACK)
         wg_rows = wg.rearrange("(p i) r -> p i r", i=PACK)
-        wg_in = [keep.tile([P, PACK, HALF], F32, name=f"wg_in{c}") for c in range(2)]
-        wd8_sb = keep.tile([P, N], U32, name="wd8_sb", align_bytes=256)
-        wd4_sb = keep.tile([P, 2 * N], U8, name="wd4_sb", align_bytes=256)
         res_rows = res.rearrange("(a p) j -> p a j", p=P)
         out_rows = out.rearrange("(a p) j -> p a j", p=P)
-        res_sb = [keep.tile([P, 4, HALF], F32, name=f"res{a}") for a in range(2)]
-        for what in LOADS.split():
-            if what == "wu":
-                nc.sync.dma_start(wu_in[:].bitcast(I32), wu_words[0].bitcast(I32))
-            elif what == "wus":
-                load_scales(wu_sc_in[:], wu_scales, nc.sync)
-            elif what == "wa":
-                nc.sync.dma_start(wgt_sb[:, 0:HALF], wgt[:, 0:HALF])
-            elif what == "wb":
-                nc.sync.dma_start(wgt_sb[:, HALF:J], wgt[:, HALF:J])
-            elif what[0] == "x":
-                nc.sync.dma_start(planes[int(what[1])][:], x_rows[int(what[1])])
-            elif what == "ga":
-                nc.sync.dma_start(wg_in[0][:, :, 0 : 4 * RW0], wg_rows[:, :, 0 : 4 * RW0])
-            elif what == "gb":
-                nc.sync.dma_start(wg_in[0][:, :, 4 * RW0 : HALF], wg_rows[:, :, 4 * RW0 : HALF])
-            elif what == "gc":
-                nc.sync.dma_start(wg_in[1][:, :, 0 : 4 * RW1], wg_rows[:, :, HALF : HALF + 4 * RW1])
-            elif what == "gd":
-                nc.sync.dma_start(wg_in[1][:, :, 4 * RW1 : HALF], wg_rows[:, :, HALF + 4 * RW1 : R])
-            elif what[0] == "g":
-                c = int(what[1])
-                nc.sync.dma_start(wg_in[c][:], wg_rows[:, :, HALF * c : HALF * (c + 1)])
-            elif what == "wd":
-                nc.sync.dma_start(wd8_sb[:].bitcast(I32), wd8_words[0].rearrange("p n t -> p (n t)").bitcast(I32))
-                nc.sync.dma_start(wd4_sb[:].bitcast(I32), wd4_words[0].bitcast(I32))
-            elif what[0] == "r":
-                a = int(what[1])
-                nc.sync.dma_start(res_sb[a][:], res_rows[:, :, HALF * a : HALF * (a + 1)])
-
-        wu_codes = keep.tile([P, 2 * R], U8, name="wu_codes", align_bytes=256)
-        wu_sc = keep.tile([P, R], U8, name="wu_sc", align_bytes=256)
+        wgt_in = keep.tile([P, 2, QUAD], F32, name="wgt_in", align_bytes=ALIGN)
+        wgt_turned = keep.tile([P, 2, QUAD], F32, name="wgt_turned", align_bytes=ALIGN)
+        wgt_wide = keep.tile([P, QUAD, 2, HEAD], F32, name="wgt_wide", align_bytes=ALIGN)
+        wu_codes = keep.tile([P, 2 * R], U8, name="wu_codes", align_bytes=ALIGN)
+        wu_sc = keep.tile([P, R], U8, name="wu_sc", align_bytes=ALIGN)
+        head_rows = wgt.rearrange("(g c) (a b) -> c g a b", c=HEAD, b=QUAD)[0]
+        for q in range(4):
+            (nc.sync, nc.scalar)[q % 2].dma_start(
+                wgt_in[QUAD * q : QUAD * (q + 1)],
+                head_rows[2 * q : 2 * q + 2].rearrange("h a b -> a h b"),
+            )
+        nc.sync.dma_start(wu_in[:].bitcast(I32), wu_words[0].bitcast(I32))
+        nc.sync.dma_start(scales_in[0:16, :].bitcast(I32), wu_scales[0].bitcast(I32))
+        nc.scalar.activation(zero[:], zero_in[:], SILU)
+        for h in range(2):
+            nc.vector.transpose(wgt_turned[:, h, :], wgt_in[:, h, :])
+        nc.vector.tensor_copy(
+            wu_sc[:].rearrange("p (b t m) -> p b t m", b=2, t=PACK),
+            scales_in[:].rearrange("p (b m t) -> p b t m", b=2, t=PACK),
+        )
         nc.vector.tensor_copy(
             wu_codes[:].bitcast(U16).rearrange("p (b t m) -> p b t m", b=2, t=PACK),
             wu_in[:].bitcast(U16).rearrange("p (b m t) -> p b t m", b=2, t=PACK),
         )
-        nc.vector.tensor_copy(
-            wu_sc[:].rearrange("p (b t m) -> p b t m", b=2, t=PACK),
-            wu_sc_in[:].rearrange("p (b m t) -> p b t m", b=2, t=PACK),
-        )
-        wd_sc = wu_sc_in
-        load_scales(wd_sc[:, 0:N], wd8_scales, nc.gpsimd)
-        load_scales(wd_sc[:, N : 2 * N], wd4_scales, nc.gpsimd)
+        for s in range(2):
+            part = slice(HEAD * s, HEAD * (s + 1))
+            nc.scalar.copy(
+                wgt_wide[:, part],
+                wgt_turned[:, :, part].rearrange("p h a -> p a h").unsqueeze(3).to_broadcast([P, HEAD, 2, HEAD]),
+            )
+            nc.vector.transpose(wgt_sb[:, HALF * s : HALF * (s + 1)], wgt_wide[:, part].rearrange("p a h q -> p (a h q)"))
+        for i in range(PACK):
+            nc.sync.dma_start(planes[i][:], x_rows[i])
+            if i == 0:
+                nc.sync.dma_start(offsets[:], offs)
+            if i == 2:
+                for q in range(1, 4):
+                    nc.sync.dma_start(
+                        wu_sc[QUAD * q : QUAD * q + 4, :].bitcast(I32), wu_sc[4 * q : 4 * q + 4, :].bitcast(I32)
+                    )
+        for b in range(2):
+            nc.sync.dma_start(wg_in[b][:], wg_rows[:, :, HALF * b : HALF * (b + 1)])
+        nc.sync.dma_start(wd8_sb[:].bitcast(I32), wd8_words[0].rearrange("p n t -> p (n t)").bitcast(I32))
+        nc.sync.dma_start(wd4_sb[:].bitcast(I32), wd4_words[0].bitcast(I32))
+        for s in range(2):
+            nc.sync.dma_start(res_sb[s][:], res_rows[:, :, HALF * s : HALF * (s + 1)])
+
+        load_scales(nc.gpsimd, scales_in[:, 0:N], wd8_scales)
+        load_scales(nc.gpsimd, scales_in[:, N : 2 * N], wd4_scales)
 
         picked = keep.tile([P, PACK, J], F32, name="picked")
-        xg_bf = keep.tile([P, J, PACK], BF16, name="xg_bf", align_bytes=256)
-        wg_bf = [keep.tile([P, PACK, P, PACK], BF16, name=f"wg_bf{b}", tag=("wg_bf0", "stage0" if ALIAS else "wg_bf1")[b], align_bytes=256) for b in range(2)]
-        wg_codes = [keep.tile([P, HALF], U32, name=f"wg_codes{b}", align_bytes=256) for b in range(2)]
-        wg_sc = [keep.tile([P, HALF], U8, name=f"wg_sc{b}", align_bytes=256) for b in range(2)]
-        xg_codes = [keep.tile([P, HALF], U32, name=f"xg_codes{a}", tag=("xc0", "wg_bf0" if HOLD else "xc1")[a], align_bytes=256) for a in range(2)]
-        xg_sc = [keep.tile([P, HALF], U8, name=f"xg_sc{a}", align_bytes=256) for a in range(2)]
-        h_bf = [keep.tile([P, 2, 2 * TOK, PACK], BF16, name=f"h_bf{n}", tag=f"stage{n}", align_bytes=256) for n in range(4)]
-        h_codes = [keep.tile([P, 2, 2 * TOK], U32, name=f"h_codes{n}", align_bytes=256) for n in range(4)]
-        h_sc = [keep.tile([P, 2, 2 * TOK], U8, name=f"h_sc{n}", align_bytes=256) for n in range(4)]
+        xg_bf = keep.tile([P, J, PACK], BF16, name="xg_bf", align_bytes=ALIGN)
+        wg_bf = [
+            keep.tile([P, PACK, P, PACK], BF16, name=f"wg_bf{b}", tag=("wg_bf0", "stage0")[b], align_bytes=ALIGN)
+            for b in range(2)
+        ]
+        wg_codes = [keep.tile([P, HALF], U32, name=f"wg_codes{b}", align_bytes=ALIGN) for b in range(2)]
+        wg_sc = [keep.tile([P, HALF], U8, name=f"wg_sc{b}", align_bytes=ALIGN) for b in range(2)]
+        xg_codes = [keep.tile([P, HALF], U32, name=f"xg_codes{s}", align_bytes=ALIGN) for s in range(2)]
+        xg_sc = [keep.tile([P, HALF], U8, name=f"xg_sc{s}", align_bytes=ALIGN) for s in range(2)]
+        h_bf = [
+            keep.tile([P, 2, GROUP, PACK], BF16, name=f"h_bf{n}", tag=f"stage{n}", align_bytes=ALIGN)
+            for n in range(GROUPS)
+        ]
+        h_codes = [keep.tile([P, 2, GROUP], U32, name=f"h_codes{n}", align_bytes=ALIGN) for n in range(GROUPS)]
+        h_sc = [keep.tile([P, 2, GROUP], U8, name=f"h_sc{n}", align_bytes=ALIGN) for n in range(GROUPS)]
         banks = [psum.tile([P, HALF], F32, name=f"bank{k}") for k in range(8)]
-        gates = [keep.tile([P, 2 * HALF], F32, name=f"gate{k}") for k in range(NGATE)]
-        up_uses, other_uses, gate_uses, y_uses = [], [], [], []
+        gates = [keep.tile([P, 2 * HALF], F32, name=f"gate{k}") for k in range(GATE_TILES)]
 
-        def next_up_bank():
-            up_uses.append(0)
-            return banks[(len(up_uses) - 1) % NUB]
+        rings = {
+            "up": banks[:UP_BANKS],
+            "gate": banks[UP_BANKS : UP_BANKS + GATE_BANKS],
+            "out": banks[UP_BANKS + GATE_BANKS :],
+            "silu": gates,
+        }
 
-        def next_bank():
-            other_uses.append(0)
-            return banks[NUB + (len(other_uses) - 1) % NGA]
-
-        def next_y_bank():
-            y_uses.append(0)
-            return banks[NUB + NGA + (len(y_uses) - 1) % (8 - NUB - NGA)]
-
-        def next_gate():
-            gate_uses.append(0)
-            return gates[(len(gate_uses) - 1) % NGATE]
+        def take(name):
+            rings[name] = rings[name][1:] + rings[name][:1]
+            return rings[name][-1][:]
 
         def gather(i, j0, n):
             nc.vector.tensor_tensor(
@@ -179,20 +159,18 @@ def tile_list_silu_mix_res_kernel(
             )
 
         def quant_x(j0, n):
-            a, c = divmod(j0, HALF)
+            s, c = divmod(j0, HALF)
             nc.vector.quantize_mx(
-                out=xg_codes[a][:, c : c + n].bitcast(FP8X4),
-                scales=xg_sc[a][:, c : c + n],
+                out=xg_codes[s][:, c : c + n].bitcast(FP8X4),
+                scales=xg_sc[s][:, c : c + n],
                 in_=xg_bf[:, j0 : j0 + n, :].rearrange("p j i -> p (j i)"),
             )
 
-        def round_wg(b, m0, n, on_vector):
-            dst = wg_bf[b][:, :, m0 : m0 + n, :].rearrange("p t m i -> p m i t")
-            src = wg_in[b][:, :, 4 * m0 : 4 * (m0 + n)].rearrange("p i (m t) -> p m i t", t=PACK)
-            if on_vector:
-                nc.vector.tensor_copy(dst, src)
-            else:
-                nc.scalar.copy(dst, src)
+        def round_wg(copy, b, m0, m1):
+            copy(
+                wg_bf[b][:, :, m0:m1, :].rearrange("p t m i -> p m i t"),
+                wg_in[b][:, :, PACK * m0 : PACK * m1].rearrange("p i (m t) -> p m i t", t=PACK),
+            )
 
         def quant_wg(b):
             nc.vector.quantize_mx(
@@ -201,202 +179,178 @@ def tile_list_silu_mix_res_kernel(
                 in_=wg_bf[b][:].rearrange("p t m i -> p (t m i)"),
             )
 
-        ub_of, gate_of, y_of = {}, {}, {}
-
-        def gate_pass(dst, b, t, cols):
+        def first_stage(dst, codes, scales, j0, n):
+            s, c = divmod(j0, HALF)
             nc.tensor.matmul_mx(
                 out=dst,
-                lhsT=wg_codes[b][:, P * t : P * (t + 1)].bitcast(FP8X4),
-                lhsT_scale=wg_sc[b][:, P * t : P * (t + 1)],
-                rhs=xg_codes[cols.start // HALF][:, cols.start % HALF : cols.start % HALF + cols.stop - cols.start].bitcast(FP8X4),
-                rhs_scale=xg_sc[cols.start // HALF][:, cols.start % HALF : cols.start % HALF + cols.stop - cols.start],
+                lhsT=codes,
+                lhsT_scale=scales,
+                rhs=xg_codes[s][:, c : c + n].bitcast(FP8X4),
+                rhs_scale=xg_sc[s][:, c : c + n],
                 start=True,
                 stop=True,
             )
 
-        def gate_single(b, c, bank):
-            ga = bank()[:].rearrange("p (t j) -> p t j", t=PACK)
+        def gate_pass(dst, b, t, j0, n):
+            cols = slice(P * t, P * (t + 1))
+            first_stage(dst, wg_codes[b][:, cols].bitcast(FP8X4), wg_sc[b][:, cols], j0, n)
+
+        gate_of, up_of = {}, {}
+
+        def gate_chunk(b, c):
+            bank = take("gate").rearrange("p (t j) -> p t j", t=PACK)
             for t in range(PACK):
-                gate_pass(ga[:, t, :], b, t, slice(TOK * c, TOK * (c + 1)))
-            gate = next_gate()[:, 0:HALF].rearrange("p (j t) -> p j t", t=PACK)
-            nc.scalar.activation(gate, ga.rearrange("p t j -> p j t"), ACT.Silu, bias=zero[:])
+                gate_pass(bank[:, t, :], b, t, CHUNK * c, CHUNK)
+            gate = take("silu")[:, 0:HALF].rearrange("p (j t) -> p j t", t=PACK)
+            nc.scalar.activation(gate, bank.rearrange("p t j -> p j t"), SILU, bias=zero[:])
             gate_of[b, c] = gate.rearrange("p j (u e) -> p j u e", u=2)
 
-        def gate_pair(b, c, bank):
-            gate = next_gate()[:].rearrange("p (u j e) -> p u j e", u=2, e=2)
+        def gate_group(b, c):
+            gate = take("silu").rearrange("p (u j e) -> p u j e", u=2, e=2)
             for u in range(2):
-                ga = bank()[:].rearrange("p (e j) -> p e j", e=2)
+                bank = take("gate").rearrange("p (e j) -> p e j", e=2)
                 for e in range(2):
-                    gate_pass(ga[:, e, :], b, 2 * u + e, slice(TOK * c, TOK * (c + 2)))
-                nc.scalar.activation(gate[:, u, :, :], ga.rearrange("p e j -> p j e"), ACT.Silu, bias=zero[:])
+                    gate_pass(bank[:, e, :], b, 2 * u + e, CHUNK * c, GROUP)
+                nc.scalar.activation(gate[:, u, :, :], bank.rearrange("p e j -> p j e"), SILU, bias=zero[:])
             for d in range(2):
-                gate_of[b, c + d] = gate[:, :, TOK * d : TOK * (d + 1), :].rearrange("p u j e -> p j u e")
+                gate_of[b, c + d] = gate[:, :, CHUNK * d : CHUNK * (d + 1), :].rearrange("p u j e -> p j u e")
 
         def up(b, c):
-            cols = slice(TOK * c, TOK * (c + 1))
-            ub = next_up_bank()[:].rearrange("p (t j) -> p t j", t=PACK)
+            bank = take("up").rearrange("p (t j) -> p t j", t=PACK)
             for t in range(PACK):
-                s = PACK * b + t
-                nc.tensor.matmul_mx(
-                    out=ub[:, t, :],
-                    lhsT=wu_codes[:, 2 * P * s : 2 * P * (s + 1)].bitcast(FP4X4),
-                    lhsT_scale=wu_sc[:, P * s : P * (s + 1)],
-                    rhs=xg_codes[c // 4][:, TOK * (c % 4) : TOK * (c % 4 + 1)].bitcast(FP8X4),
-                    rhs_scale=xg_sc[c // 4][:, TOK * (c % 4) : TOK * (c % 4 + 1)],
-                    start=True,
-                    stop=True,
+                c0 = HALF * b + P * t
+                first_stage(
+                    bank[:, t, :], wu_codes[:, 2 * c0 : 2 * (c0 + P)].bitcast(FP4X4), wu_sc[:, c0 : c0 + P], CHUNK * c, CHUNK
                 )
-            ub_of[b, c] = ub
+            up_of[b, c] = bank.rearrange("p (u e) j -> p j u e", u=2)
 
         def product(b, c):
+            n, d = divmod(c, 2)
             nc.vector.tensor_tensor(
-                h_bf[c // 2][:, b, TOK * (c % 2) : TOK * (c % 2 + 1), :].rearrange("p j (u e) -> p j u e", u=2),
-                ub_of[b, c].rearrange("p (u e) j -> p j u e", u=2),
+                h_bf[n][:, b, CHUNK * d : CHUNK * (d + 1), :].rearrange("p j (u e) -> p j u e", u=2),
+                up_of[b, c],
                 gate_of[b, c],
                 MULT,
             )
 
-        def quant_h(n, c0, w):
+        def quant_h(n, c0, width):
             nc.vector.quantize_mx(
-                out=h_codes[n][:].rearrange("p b j -> p (b j)")[:, c0 : c0 + w].bitcast(FP8X4),
-                scales=h_sc[n][:].rearrange("p b j -> p (b j)")[:, c0 : c0 + w],
-                in_=h_bf[n][:].rearrange("p b j t -> p (b j t)")[:, PACK * c0 : PACK * (c0 + w)],
+                out=h_codes[n][:].rearrange("p b j -> p (b j)")[:, c0 : c0 + width].bitcast(FP8X4),
+                scales=h_sc[n][:].rearrange("p b j -> p (b j)")[:, c0 : c0 + width],
+                in_=h_bf[n][:].rearrange("p b j t -> p (b j t)")[:, PACK * c0 : PACK * (c0 + width)],
             )
 
-        def down_pass(y, a, b, n, c0, w, start, stop):
+        def down_pass(dst, a, b, n, j0, width, start, stop):
             if b == 0:
-                lhsT = wd8_sb[:, P * a : P * (a + 1)].bitcast(FP8X4)
+                codes = wd8_sb[:, P * a : P * (a + 1)].bitcast(FP8X4)
             else:
-                lhsT = wd4_sb[:, 2 * P * a : 2 * P * (a + 1)].bitcast(FP4X4)
+                codes = wd4_sb[:, 2 * P * a : 2 * P * (a + 1)].bitcast(FP4X4)
             nc.tensor.matmul_mx(
-                out=y,
-                lhsT=lhsT,
-                lhsT_scale=wd_sc[:, N * b + P * a : N * b + P * (a + 1)],
-                rhs=h_codes[n][:, b, c0 : c0 + w].bitcast(FP8X4),
-                rhs_scale=h_sc[n][:, b, c0 : c0 + w],
+                out=dst,
+                lhsT=codes,
+                lhsT_scale=scales_in[:, N * b + P * a : N * b + P * (a + 1)],
+                rhs=h_codes[n][:, b, j0 : j0 + width].bitcast(FP8X4),
+                rhs_scale=h_sc[n][:, b, j0 : j0 + width],
                 start=start,
                 stop=stop,
             )
 
-        def down_pair(n, u):
-            y = next_y_bank()[:]
+        def operands(bank, a0, a1, j0, width):
+            s, c = divmod(j0, HALF)
+            y = bank.rearrange("p (a j) -> p a j", j=width)
+            return y, res_sb[s][:, a0:a1, c : c + width], out_rows[:, a0:a1, j0 : j0 + width]
+
+        def down_group(n, u):
+            bank = take("out")
             for e in range(2):
-                c0 = 2 * TOK * e
-                down_pass(y[:, c0 : c0 + 2 * TOK], 2 * u + e, 0, n, 0, 2 * TOK, True, False)
+                c0 = GROUP * e
+                down_pass(bank[:, c0 : c0 + GROUP], 2 * u + e, 0, n, 0, GROUP, True, False)
                 for d in range(2):
-                    down_pass(y[:, c0 + TOK * d : c0 + TOK * (d + 1)], 2 * u + e, 1, n, TOK * d, TOK, False, d == 1)
-            cols = slice(2 * TOK * n, 2 * TOK * (n + 1))
-            c0 = 2 * TOK * (n % 2)
-            y_of[n, u] = (y, res_sb[n // 2][:, 2 * u : 2 * u + 2, c0 : c0 + 2 * TOK], out_rows[:, 2 * u : 2 * u + 2, cols])
+                    dst = bank[:, c0 + CHUNK * d : c0 + CHUNK * (d + 1)]
+                    down_pass(dst, 2 * u + e, 1, n, CHUNK * d, CHUNK, False, d == 1)
+            return operands(bank, 2 * u, 2 * u + 2, GROUP * n, GROUP)
 
-        def open_narrow(d):
-            y = next_bank()[:]
-            for a in range(4):
-                down_pass(y[:, TOK * a : TOK * (a + 1)], a, 0, 3, TOK * d, TOK, a == 0, False)
-            c0 = TOK * (2 + d)
-            y_of[3, d] = (y, res_sb[1][:, :, c0 : c0 + TOK], out_rows[:, :, HALF + c0 : HALF + c0 + TOK])
+        def down_chunk(bank, b, n, d):
+            for a in range(N // P):
+                first, last = (b, a) == (0, 0), (b, a) == (1, N // P - 1)
+                down_pass(bank[:, CHUNK * a : CHUNK * (a + 1)], a, b, n, CHUNK * d, CHUNK, first, last)
 
-        def close_narrow(d):
-            y = y_of[3, d][0]
-            for a in range(4):
-                down_pass(y[:, TOK * a : TOK * (a + 1)], a, 1, 3, TOK * d, TOK, False, a == 3)
+        def add_on_vector(y, res_part, out_part):
+            result = ring.tile(list(res_part.shape), F32, name="result")
+            nc.vector.tensor_tensor(result[:], y, res_part, ADD)
+            nc.sync.dma_start(out_part, result[:])
 
-        def finish_vector(n, u, a0, a1):
-            y, src, dst = y_of[n, u]
-            result = ring.tile([P, a1 - a0, src.shape[2]], F32, name="result")
-            nc.vector.tensor_tensor(result[:], y.rearrange("p (a j) -> p a j", a=src.shape[1])[:, a0:a1], src[:, a0:a1], ADD)
-            nc.sync.dma_start(dst[:, a0:a1], result[:])
+        def leave_psum(y, res_part, out_part):
+            y_sb = ring.tile(list(res_part.shape), F32, name="y_sb")
+            nc.scalar.copy(y_sb[:], y)
+            return y_sb[:], res_part, out_part
 
-        def evacuate(n, u):
-            y, src, dst = y_of[n, u]
-            y_sb = ring.tile(list(src.shape), F32, name="y_sb")
-            nc.scalar.copy(y_sb[:], y.rearrange("p (a j) -> p a j", a=src.shape[1]))
-            y_of[n, u] = (y_sb, src, dst)
+        def add_on_gpsimd(n, y, res_part, out_part):
+            result = keep.tile([P, 2, 2, GROUP], F32, name=f"result{n}", tag=f"stage{n + 1}", align_bytes=ALIGN)
+            nc.gpsimd.tensor_tensor(result[:, 0], y, res_part, ADD)
+            nc.sync.dma_start(out_part, result[:, 0])
 
-        def finish_gpsimd(n, us):
-            result = keep.tile([P, 2, 2, 2 * TOK], F32, name=f"result{n}", tag=f"stage{n + 1}" if LAG[n] else f"late{n}", align_bytes=256)
-            for u in us:
-                y_sb, src, dst = y_of[n, u]
-                if GW == HALF:
-                    nc.gpsimd.tensor_tensor(result[:, u], y_sb[:], src, ADD)
-                else:
-                    for e in range(2):
-                        nc.gpsimd.tensor_tensor(result[:, u, e], y_sb[:, e], src[:, e], ADD)
-                nc.sync.dma_start(dst, result[:, u])
-
-        for i in range(3):
-            if GFULL and i != 1 and i != 0:
-                gather(i, 0, J)
-            else:
-                for a in range(2):
-                    gather(i, HALF * a, HALF)
-                    if i == 1:
-                        round_x(HALF * a, HALF, 0)
+        for i in range(2):
+            for j0 in (0, HALF):
+                gather(i, j0, HALF)
+                if i == 1:
+                    round_x(j0, HALF, 0)
+        gather(2, 0, J)
+        round_wg(nc.scalar.copy, 0, 0, SCALAR_SHARE[0])
         j0 = 0
-        for k, n in enumerate(XCH):
-            if k == RW0AT and RW0 > 0:
-                round_wg(0, 0, RW0, False)
-            gather(3, j0, n)
+        for n in LAST_PLANE_PIECES:
+            gather(PACK - 1, j0, n)
             round_x(j0, n, 2)
-            if j0 < HALF or not MERGE:
+            if j0 < HALF:
                 quant_x(j0, n)
-            elif j0 + n == J:
+            j0 = j0 + n
+            if j0 == HALF:
+                round_wg(nc.vector.tensor_copy, 0, SCALAR_SHARE[0], P)
+            elif j0 == J:
                 quant_x(HALF, HALF)
-            j0 += n
-            if k == QW0AT:
-                round_wg(0, RW0, P - RW0, True)
-            if k == QW0AT + QD:
+            elif j0 > HALF:
                 quant_wg(0)
-        round_wg(1, 0, RW1, False)
-        round_wg(1, RW1, P - RW1, True)
+        round_wg(nc.scalar.copy, 1, 0, SCALAR_SHARE[1])
+        round_wg(nc.vector.tensor_copy, 1, SCALAR_SHARE[1], P)
         quant_wg(1)
-        units = [(b, c + d) for c in range(0, 8, 2) for b in range(2) for d in range(2)]
-        for k in range(len(units) + 1):
+
+        products = [(b, 2 * n + d) for n in range(GROUPS) for b in range(2) for d in range(2)]
+        last = GROUPS - 1
+        waiting, for_gpsimd = {}, {}
+        tail_banks = []
+        for k in range(len(products) + 1):
             n, step = divmod(k, 4)
-            if k < len(units):
-                b, c = units[k]
-                if k < SINGLE:
-                    gate_single(b, c, next_bank)
-                elif c % 2 == 0 and (b, c) not in gate_of:
-                    gate_pair(b, c, next_bank)
-                if k == 1 and AHEAD:
-                    gate_pair(0, 2, next_y_bank)
+            if k < len(products):
+                b, c = products[k]
+                if n == 0:
+                    gate_chunk(b, c)
+                elif c % 2 == 0:
+                    gate_group(b, c)
                 up(b, c)
             if k >= 1:
-                product(*units[k - 1])
-            if n >= 1 and step == QLAG and n < 4:
-                quant_h(n - 1, 0, HALF)
-                if n >= 2 and LAG[n - 2]:
-                    finish_gpsimd(n - 2, GG[n - 2])
-            for m in range(3):
-                for u in range(2):
-                    at = 4 * (m + 1) + QLAG + DLAG + u
-                    if k == at:
-                        down_pair(m, u)
-                        if u in GG[m]:
-                            evacuate(m, u)
-                            if not LAG[m] and u == GG[m][-1]:
-                                finish_gpsimd(m, GG[m])
-                    if k == min(at + VLAG, len(units)) and u not in GG[m] and (m < 2 or VEARLY):
-                        finish_vector(m, u, 0, 2)
-            if k == len(units) - 1:
-                quant_h(3, 0, 2 * TOK)
-                open_narrow(0)
-                open_narrow(1)
-                if Q6:
-                    quant_h(3, 2 * TOK, TOK)
-                    close_narrow(0)
-        for d in range(Q6, 2):
-            quant_h(3, (2 + d) * TOK, TOK)
-            close_narrow(d)
-        if LAG[2]:
-            finish_gpsimd(2, GG[2])
-        for u in range(2):
-            if u not in GG[2] and not VEARLY:
-                finish_vector(2, u, 0, 2)
-        finish_vector(3, 0, 0, 4)
-        if SPLIT:
-            finish_vector(3, 1, 0, 2)
-            finish_vector(3, 1, 2, 4)
-        else:
-            finish_vector(3, 1, 0, 4)
+                product(*products[k - 1])
+            if 1 <= n <= last and step == 1:
+                quant_h(n - 1, 0, 2 * GROUP)
+                if n - 2 in for_gpsimd:
+                    add_on_gpsimd(n - 2, *for_gpsimd[n - 2])
+            if 1 <= n <= last and step == 2:
+                waiting[k + 1] = down_group(n - 1, 0)
+                if n < last:
+                    for_gpsimd[n - 1] = leave_psum(*waiting.pop(k + 1))
+            if k in waiting:
+                add_on_vector(*waiting.pop(k))
+            if 1 <= n <= last and step == 3:
+                waiting[k + 1] = down_group(n - 1, 1)
+            if k == len(products) - 1:
+                quant_h(last, 0, GROUP)
+                for d in range(2):
+                    tail_banks.append(take("gate"))
+                    down_chunk(tail_banks[d], 0, last, d)
+                quant_h(last, GROUP, CHUNK)
+                down_chunk(tail_banks[0], 1, last, 0)
+        quant_h(last, GROUP + CHUNK, CHUNK)
+        down_chunk(tail_banks[1], 1, last, 1)
+        add_on_vector(*operands(tail_banks[0], 0, 4, J - GROUP, CHUNK))
+        y, res_part, out_part = operands(tail_banks[1], 0, 4, J - CHUNK, CHUNK)
+        for a0 in (0, 2):
+            add_on_vector(y[:, a0 : a0 + 2], res_part[:, a0 : a0 + 2], out_part[:, a0 : a0 + 2])

@@ -24,8 +24,7 @@ CHUNK = 128
 GROUP = 2 * CHUNK
 GROUPS = J // GROUP
 ALIGN = 256
-LAST_PLANE_PIECES = (128, 128, 256, 256, 256)
-SCALAR_SHARE = (32, 96)
+SCALAR_SHARE = (40, 108)
 QUAD = 32
 HEAD = 16
 UP_BANKS, GATE_BANKS, OUT_BANKS = 3, 3, 2
@@ -56,7 +55,10 @@ def tile_list_silu_mix_res_kernel(
         wu_in = keep.tile([P, 2 * R], U8, name="wu_in", align_bytes=ALIGN)
         wgt_sb = keep.tile([P, J], F32, name="wgt_sb", align_bytes=ALIGN)
         planes = [keep.tile([P, T], F32, name=f"plane{i}") for i in range(PACK)]
-        wg_in = [keep.tile([P, PACK, HALF], F32, name=f"wg_in{b}") for b in range(2)]
+        early = PACK * SCALAR_SHARE[0]
+        wg_early = keep.tile([P, PACK, early], F32, name="wg_early")
+        wg_rest = keep.tile([P, PACK, HALF - early], F32, name="wg_rest")
+        wg_second = keep.tile([P, PACK, HALF], F32, name="wg_second")
         wd8_sb = keep.tile([P, N], U32, name="wd8_sb", align_bytes=ALIGN)
         wd4_sb = keep.tile([P, 2 * N], U8, name="wd4_sb", align_bytes=ALIGN)
         res_sb = [keep.tile([P, N // P, HALF], F32, name=f"res{s}") for s in range(2)]
@@ -100,12 +102,13 @@ def tile_list_silu_mix_res_kernel(
             if i == 0:
                 nc.sync.dma_start(offsets[:], offs)
             if i == 2:
+                nc.sync.dma_start(wg_early[:], wg_rows[:, :, 0:early])
                 for q in range(1, 4):
                     nc.sync.dma_start(
                         wu_sc[QUAD * q : QUAD * q + 4, :].bitcast(I32), wu_sc[4 * q : 4 * q + 4, :].bitcast(I32)
                     )
-        for b in range(2):
-            nc.sync.dma_start(wg_in[b][:], wg_rows[:, :, HALF * b : HALF * (b + 1)])
+        nc.sync.dma_start(wg_rest[:], wg_rows[:, :, early:HALF])
+        nc.sync.dma_start(wg_second[:], wg_rows[:, :, HALF:R])
         nc.sync.dma_start(wd8_sb[:].bitcast(I32), wd8_words[0].rearrange("p n t -> p (n t)").bitcast(I32))
         nc.sync.dma_start(wd4_sb[:].bitcast(I32), wd4_words[0].bitcast(I32))
         for s in range(2):
@@ -117,7 +120,7 @@ def tile_list_silu_mix_res_kernel(
         picked = keep.tile([P, PACK, J], F32, name="picked")
         xg_bf = keep.tile([P, J, PACK], BF16, name="xg_bf", align_bytes=ALIGN)
         wg_bf = [
-            keep.tile([P, PACK, P, PACK], BF16, name=f"wg_bf{b}", tag=("wg_bf0", "stage0")[b], align_bytes=ALIGN)
+            keep.tile([P, PACK, P, PACK], BF16, name=f"wg_bf{b}", align_bytes=ALIGN)
             for b in range(2)
         ]
         wg_codes = [keep.tile([P, HALF], U32, name=f"wg_codes{b}", align_bytes=ALIGN) for b in range(2)]
@@ -132,6 +135,7 @@ def tile_list_silu_mix_res_kernel(
         h_sc = [keep.tile([P, 2, GROUP], U8, name=f"h_sc{n}", align_bytes=ALIGN) for n in range(GROUPS)]
         banks = [psum.tile([P, HALF], F32, name=f"bank{k}") for k in range(8)]
         gates = [keep.tile([P, 2 * HALF], F32, name=f"gate{k}") for k in range(GATE_TILES)]
+        first_gates = keep.tile([P, PACK, HALF], F32, name="first_gates", tag="wg_second")
 
         rings = {
             "up": banks[:UP_BANKS],
@@ -166,10 +170,10 @@ def tile_list_silu_mix_res_kernel(
                 in_=xg_bf[:, j0 : j0 + n, :].rearrange("p j i -> p (j i)"),
             )
 
-        def round_wg(copy, b, m0, m1):
+        def round_wg(copy, b, m0, m1, src):
             copy(
                 wg_bf[b][:, :, m0:m1, :].rearrange("p t m i -> p m i t"),
-                wg_in[b][:, :, PACK * m0 : PACK * m1].rearrange("p i (m t) -> p m i t", t=PACK),
+                src.rearrange("p i (m t) -> p m i t", t=PACK),
             )
 
         def quant_wg(b):
@@ -197,11 +201,11 @@ def tile_list_silu_mix_res_kernel(
 
         gate_of, up_of = {}, {}
 
-        def gate_chunk(b, c):
+        def gate_chunk(b, c, tile):
             bank = take("gate").rearrange("p (t j) -> p t j", t=PACK)
             for t in range(PACK):
                 gate_pass(bank[:, t, :], b, t, CHUNK * c, CHUNK)
-            gate = take("silu")[:, 0:HALF].rearrange("p (j t) -> p j t", t=PACK)
+            gate = tile.rearrange("p (j t) -> p j t", t=PACK)
             nc.scalar.activation(gate, bank.rearrange("p t j -> p j t"), SILU, bias=zero[:])
             gate_of[b, c] = gate.rearrange("p j (u e) -> p j u e", u=2)
 
@@ -296,51 +300,54 @@ def tile_list_silu_mix_res_kernel(
                 if i == 1:
                     round_x(j0, HALF, 0)
         gather(2, 0, J)
-        round_wg(nc.scalar.copy, 0, 0, SCALAR_SHARE[0])
-        j0 = 0
-        for n in LAST_PLANE_PIECES:
-            gather(PACK - 1, j0, n)
-            round_x(j0, n, 2)
-            if j0 < HALF:
-                quant_x(j0, n)
-            j0 = j0 + n
-            if j0 == HALF:
-                round_wg(nc.vector.tensor_copy, 0, SCALAR_SHARE[0], P)
-            elif j0 == J:
-                quant_x(HALF, HALF)
-            elif j0 > HALF:
+        round_wg(nc.scalar.copy, 0, 0, SCALAR_SHARE[0], wg_early[:])
+        for n in range(GROUPS):
+            gather(PACK - 1, GROUP * n, GROUP)
+            round_x(GROUP * n, GROUP, 2)
+            if n < 2:
+                quant_x(GROUP * n, GROUP)
+            if n == 1:
+                round_wg(nc.vector.tensor_copy, 0, SCALAR_SHARE[0], P, wg_rest[:])
+            if n == 2:
                 quant_wg(0)
-        round_wg(nc.scalar.copy, 1, 0, SCALAR_SHARE[1])
-        round_wg(nc.vector.tensor_copy, 1, SCALAR_SHARE[1], P)
+        quant_x(HALF, HALF)
+        split = PACK * SCALAR_SHARE[1]
+        round_wg(nc.scalar.copy, 1, 0, SCALAR_SHARE[1], wg_second[:, :, 0:split])
+        round_wg(nc.vector.tensor_copy, 1, SCALAR_SHARE[1], P, wg_second[:, :, split:HALF])
         quant_wg(1)
 
         products = [(b, 2 * n + d) for n in range(GROUPS) for b in range(2) for d in range(2)]
+        products = products[:2] + [products[4]] + products[2:4] + products[5:]
         last = GROUPS - 1
+        quantise_at = {6: 0, 9: 1, 13: 2}
         waiting, for_gpsimd = {}, {}
         tail_banks = []
         for k in range(len(products) + 1):
             n, step = divmod(k, 4)
             if k < len(products):
                 b, c = products[k]
-                if n == 0:
-                    gate_chunk(b, c)
+                if k < 3:
+                    gate_chunk(b, c, first_gates[:, k])
+                elif k < 6:
+                    gate_chunk(b, c, take("silu")[:, 0:HALF])
                 elif c % 2 == 0:
                     gate_group(b, c)
                 up(b, c)
             if k >= 1:
                 product(*products[k - 1])
-            if 1 <= n <= last and step == 1:
-                quant_h(n - 1, 0, 2 * GROUP)
-                if n - 2 in for_gpsimd:
-                    add_on_gpsimd(n - 2, *for_gpsimd[n - 2])
-            if 1 <= n <= last and step == 2:
-                waiting[k + 1] = down_group(n - 1, 0)
-                if n < last:
-                    for_gpsimd[n - 1] = leave_psum(*waiting.pop(k + 1))
+            if k in quantise_at:
+                quant_h(quantise_at[k], 0, 2 * GROUP)
+            if k - 1 in quantise_at:
+                g = quantise_at[k - 1]
+                waiting[k + 1] = down_group(g, 0)
+                if g < 2:
+                    for_gpsimd[g] = leave_psum(*waiting.pop(k + 1))
             if k in waiting:
                 add_on_vector(*waiting.pop(k))
-            if 1 <= n <= last and step == 3:
-                waiting[k + 1] = down_group(n - 1, 1)
+            if k - 2 in quantise_at:
+                waiting[k + 1] = down_group(quantise_at[k - 2], 1)
+            if quantise_at.get(k, 0) > 0:
+                add_on_gpsimd(quantise_at[k] - 1, *for_gpsimd[quantise_at[k] - 1])
             if k == len(products) - 1:
                 quant_h(last, 0, GROUP)
                 for d in range(2):

@@ -24,7 +24,8 @@ CHUNK = 128
 GROUP = 2 * CHUNK
 GROUPS = J // GROUP
 ALIGN = 256
-SCALAR_SHARE = (40, 108)
+SCALAR_SHARE = (40, 80)
+LAST_PLANE_PIECES = (128, 128, 256, 256, 256)
 QUAD = 32
 HEAD = 16
 UP_BANKS, GATE_BANKS, OUT_BANKS = 3, 3, 2
@@ -55,10 +56,7 @@ def tile_list_silu_mix_res_kernel(
         wu_in = keep.tile([P, 2 * R], U8, name="wu_in", align_bytes=ALIGN)
         wgt_sb = keep.tile([P, J], F32, name="wgt_sb", align_bytes=ALIGN)
         planes = [keep.tile([P, T], F32, name=f"plane{i}") for i in range(PACK)]
-        early = PACK * SCALAR_SHARE[0]
-        wg_early = keep.tile([P, PACK, early], F32, name="wg_early")
-        wg_rest = keep.tile([P, PACK, HALF - early], F32, name="wg_rest")
-        wg_second = keep.tile([P, PACK, HALF], F32, name="wg_second")
+        wg_in = [keep.tile([P, PACK, HALF], F32, name=f"wg_in{b}") for b in range(2)]
         wd8_sb = keep.tile([P, N], U32, name="wd8_sb", align_bytes=ALIGN)
         wd4_sb = keep.tile([P, 2 * N], U8, name="wd4_sb", align_bytes=ALIGN)
         res_sb = [keep.tile([P, N // P, HALF], F32, name=f"res{s}") for s in range(2)]
@@ -102,13 +100,12 @@ def tile_list_silu_mix_res_kernel(
             if i == 0:
                 nc.sync.dma_start(offsets[:], offs)
             if i == 2:
-                nc.sync.dma_start(wg_early[:], wg_rows[:, :, 0:early])
                 for q in range(1, 4):
                     nc.sync.dma_start(
                         wu_sc[QUAD * q : QUAD * q + 4, :].bitcast(I32), wu_sc[4 * q : 4 * q + 4, :].bitcast(I32)
                     )
-        nc.sync.dma_start(wg_rest[:], wg_rows[:, :, early:HALF])
-        nc.sync.dma_start(wg_second[:], wg_rows[:, :, HALF:R])
+        for b in range(2):
+            nc.sync.dma_start(wg_in[b][:], wg_rows[:, :, HALF * b : HALF * (b + 1)])
         nc.sync.dma_start(wd8_sb[:].bitcast(I32), wd8_words[0].rearrange("p n t -> p (n t)").bitcast(I32))
         nc.sync.dma_start(wd4_sb[:].bitcast(I32), wd4_words[0].bitcast(I32))
         for s in range(2):
@@ -135,7 +132,7 @@ def tile_list_silu_mix_res_kernel(
         h_sc = [keep.tile([P, 2, GROUP], U8, name=f"h_sc{n}", align_bytes=ALIGN) for n in range(GROUPS)]
         banks = [psum.tile([P, HALF], F32, name=f"bank{k}") for k in range(8)]
         gates = [keep.tile([P, 2 * HALF], F32, name=f"gate{k}") for k in range(GATE_TILES)]
-        first_gates = keep.tile([P, PACK, HALF], F32, name="first_gates", tag="wg_second")
+        first_gates = keep.tile([P, PACK, HALF], F32, name="first_gates", tag="wg_in1")
 
         rings = {
             "up": banks[:UP_BANKS],
@@ -170,10 +167,10 @@ def tile_list_silu_mix_res_kernel(
                 in_=xg_bf[:, j0 : j0 + n, :].rearrange("p j i -> p (j i)"),
             )
 
-        def round_wg(copy, b, m0, m1, src):
+        def round_wg(copy, b, m0, m1):
             copy(
                 wg_bf[b][:, :, m0:m1, :].rearrange("p t m i -> p m i t"),
-                src.rearrange("p i (m t) -> p m i t", t=PACK),
+                wg_in[b][:, :, PACK * m0 : PACK * m1].rearrange("p i (m t) -> p m i t", t=PACK),
             )
 
         def quant_wg(b):
@@ -300,20 +297,22 @@ def tile_list_silu_mix_res_kernel(
                 if i == 1:
                     round_x(j0, HALF, 0)
         gather(2, 0, J)
-        round_wg(nc.scalar.copy, 0, 0, SCALAR_SHARE[0], wg_early[:])
-        for n in range(GROUPS):
-            gather(PACK - 1, GROUP * n, GROUP)
-            round_x(GROUP * n, GROUP, 2)
-            if n < 2:
-                quant_x(GROUP * n, GROUP)
-            if n == 1:
-                round_wg(nc.vector.tensor_copy, 0, SCALAR_SHARE[0], P, wg_rest[:])
-            if n == 2:
+        round_wg(nc.scalar.copy, 0, 0, SCALAR_SHARE[0])
+        j0 = 0
+        for n in LAST_PLANE_PIECES:
+            gather(PACK - 1, j0, n)
+            round_x(j0, n, 2)
+            if j0 < HALF:
+                quant_x(j0, n)
+            j0 = j0 + n
+            if j0 == HALF:
+                round_wg(nc.vector.tensor_copy, 0, SCALAR_SHARE[0], P)
+            elif j0 == J:
+                quant_x(HALF, HALF)
+            elif j0 > HALF:
                 quant_wg(0)
-        quant_x(HALF, HALF)
-        split = PACK * SCALAR_SHARE[1]
-        round_wg(nc.scalar.copy, 1, 0, SCALAR_SHARE[1], wg_second[:, :, 0:split])
-        round_wg(nc.vector.tensor_copy, 1, SCALAR_SHARE[1], P, wg_second[:, :, split:HALF])
+        round_wg(nc.scalar.copy, 1, 0, SCALAR_SHARE[1])
+        round_wg(nc.vector.tensor_copy, 1, SCALAR_SHARE[1], P)
         quant_wg(1)
 
         products = [(b, 2 * n + d) for n in range(GROUPS) for b in range(2) for d in range(2)]

@@ -48,10 +48,9 @@ def tile_list_silu_mix_res_kernel(
         zero_in = keep.tile([P, 1], F32, name="zero_in")
         nc.vector.memset(zero_in[:], 0.0)
         zero = keep.tile([P, 1], F32, name="zero")
-
-        def load_scales(queue, dst, src):
-            for q in range(4):
-                queue.dma_start(dst[32 * q : 32 * q + 4, :].bitcast(I32), src[0, 4 * q : 4 * q + 4, :].bitcast(I32))
+        scales = keep.tile([P, R + 2 * N], U8, name="scales", align_bytes=ALIGN)
+        nc.vector.memset(scales[:, R:].bitcast(I32), 0)
+        wu_sc, wd_sc = scales[:, 0:R], scales[:, R:]
 
         wu_in = keep.tile([P, 2 * R], U8, name="wu_in", align_bytes=ALIGN)
         wgt_sb = keep.tile([P, J], F32, name="wgt_sb", align_bytes=ALIGN)
@@ -68,7 +67,6 @@ def tile_list_silu_mix_res_kernel(
         wgt_turned = keep.tile([P, 2, QUAD], F32, name="wgt_turned", align_bytes=ALIGN)
         wgt_wide = keep.tile([P, QUAD, 2, HEAD], F32, name="wgt_wide", align_bytes=ALIGN)
         wu_codes = keep.tile([P, 2 * R], U8, name="wu_codes", align_bytes=ALIGN)
-        wu_sc = keep.tile([P, R], U8, name="wu_sc", align_bytes=ALIGN)
         head_rows = wgt.rearrange("(g c) (a b) -> c g a b", c=HEAD, b=QUAD)[0]
         for q in range(4):
             (nc.sync, nc.scalar)[q % 2].dma_start(
@@ -81,7 +79,7 @@ def tile_list_silu_mix_res_kernel(
         for h in range(2):
             nc.vector.transpose(wgt_turned[:, h, :], wgt_in[:, h, :])
         nc.vector.tensor_copy(
-            wu_sc[:].rearrange("p (b t m) -> p b t m", b=2, t=PACK),
+            wu_sc.rearrange("p (b t m) -> p b t m", b=2, t=PACK),
             scales_in[:].rearrange("p (b m t) -> p b t m", b=2, t=PACK),
         )
         nc.vector.tensor_copy(
@@ -99,10 +97,12 @@ def tile_list_silu_mix_res_kernel(
             nc.sync.dma_start(planes[i][:], x_rows[i])
             if i == 0:
                 nc.sync.dma_start(offsets[:], offs)
+                nc.sync.dma_start(wd_sc[0:16, 0:N].bitcast(I32), wd8_scales[0].bitcast(I32))
+                nc.sync.dma_start(wd_sc[0:16, N:].bitcast(I32), wd4_scales[0].bitcast(I32))
             if i == 2:
                 for q in range(1, 4):
                     nc.sync.dma_start(
-                        wu_sc[QUAD * q : QUAD * q + 4, :].bitcast(I32), wu_sc[4 * q : 4 * q + 4, :].bitcast(I32)
+                        scales[QUAD * q : QUAD * q + 4, :].bitcast(I32), scales[4 * q : 4 * q + 4, :].bitcast(I32)
                     )
         for b in range(2):
             nc.sync.dma_start(wg_in[b][:], wg_rows[:, :, HALF * b : HALF * (b + 1)])
@@ -110,9 +110,6 @@ def tile_list_silu_mix_res_kernel(
         nc.sync.dma_start(wd4_sb[:].bitcast(I32), wd4_words[0].bitcast(I32))
         for s in range(2):
             nc.sync.dma_start(res_sb[s][:], res_rows[:, :, HALF * s : HALF * (s + 1)])
-
-        load_scales(nc.gpsimd, scales_in[:, 0:N], wd8_scales)
-        load_scales(nc.gpsimd, scales_in[:, N : 2 * N], wd4_scales)
 
         picked = keep.tile([P, PACK, J], F32, name="picked")
         xg_bf = keep.tile([P, J, PACK], BF16, name="xg_bf", align_bytes=ALIGN)
@@ -249,7 +246,7 @@ def tile_list_silu_mix_res_kernel(
             nc.tensor.matmul_mx(
                 out=dst,
                 lhsT=codes,
-                lhsT_scale=scales_in[:, N * b + P * a : N * b + P * (a + 1)],
+                lhsT_scale=wd_sc[:, N * b + P * a : N * b + P * (a + 1)],
                 rhs=h_codes[n][:, b, j0 : j0 + width].bitcast(FP8X4),
                 rhs_scale=h_sc[n][:, b, j0 : j0 + width],
                 start=start,

@@ -48,9 +48,7 @@ def tile_list_silu_mix_res_kernel(
         zero_in = keep.tile([P, 1], F32, name="zero_in")
         nc.vector.memset(zero_in[:], 0.0)
         zero = keep.tile([P, 1], F32, name="zero")
-        scales = keep.tile([P, R + 2 * N], U8, name="scales", align_bytes=ALIGN)
-        nc.vector.memset(scales[:, R:].bitcast(I32), 0)
-        wu_sc, wd_sc = scales[:, 0:R], scales[:, R:]
+        wu_sc = keep.tile([P, R], U8, name="wu_sc", align_bytes=ALIGN)
 
         wu_in = keep.tile([P, 2 * R], U8, name="wu_in", align_bytes=ALIGN)
         wgt_sb = keep.tile([P, J], F32, name="wgt_sb", align_bytes=ALIGN)
@@ -63,23 +61,19 @@ def tile_list_silu_mix_res_kernel(
         wg_rows = wg.rearrange("(p i) r -> p i r", i=PACK)
         res_rows = res.rearrange("(a p) j -> p a j", p=P)
         out_rows = out.rearrange("(a p) j -> p a j", p=P)
-        wgt_in = keep.tile([P, 2, QUAD], F32, name="wgt_in", align_bytes=ALIGN)
-        wgt_turned = keep.tile([P, 2, QUAD], F32, name="wgt_turned", align_bytes=ALIGN)
-        wgt_wide = keep.tile([P, QUAD, 2, HEAD], F32, name="wgt_wide", align_bytes=ALIGN)
+        wgt_in = keep.tile([P, 2 * QUAD], F32, name="wgt_in", align_bytes=ALIGN)
+        wgt_turned = keep.tile([P, 2, 2, HEAD], F32, name="wgt_turned", align_bytes=ALIGN)
+        wgt_wide = keep.tile([P, HEAD, 2, 2, HEAD], F32, name="wgt_wide", align_bytes=ALIGN)
         wu_codes = keep.tile([P, 2 * R], U8, name="wu_codes", align_bytes=ALIGN)
-        head_rows = wgt.rearrange("(g c) (a b) -> c g a b", c=HEAD, b=QUAD)[0]
-        for q in range(4):
-            (nc.sync, nc.scalar)[q % 2].dma_start(
-                wgt_in[QUAD * q : QUAD * (q + 1)],
-                head_rows[2 * q : 2 * q + 2].rearrange("h a b -> a h b"),
-            )
+        head_rows = wgt.rearrange("(g c) (a s) -> c g a s", c=HEAD, a=HEAD)[0]
+        nc.sync.dma_start(wgt_in[:], head_rows)
         nc.sync.dma_start(wu_in[:].bitcast(I32), wu_words[0].bitcast(I32))
         nc.sync.dma_start(scales_in[0:16, :].bitcast(I32), wu_scales[0].bitcast(I32))
         nc.scalar.activation(zero[:], zero_in[:], SILU)
-        for h in range(2):
-            nc.vector.transpose(wgt_turned[:, h, :], wgt_in[:, h, :])
+        for u in range(2):
+            nc.vector.transpose(wgt_turned[:, u].rearrange("p h a -> p (h a)"), wgt_in[:, QUAD * u : QUAD * (u + 1)])
         nc.vector.tensor_copy(
-            wu_sc.rearrange("p (b t m) -> p b t m", b=2, t=PACK),
+            wu_sc[:].rearrange("p (b t m) -> p b t m", b=2, t=PACK),
             scales_in[:].rearrange("p (b m t) -> p b t m", b=2, t=PACK),
         )
         nc.vector.tensor_copy(
@@ -87,29 +81,35 @@ def tile_list_silu_mix_res_kernel(
             wu_in[:].bitcast(U16).rearrange("p (b m t) -> p b t m", b=2, t=PACK),
         )
         for s in range(2):
-            part = slice(HEAD * s, HEAD * (s + 1))
+            part = slice(8 * s, 8 * (s + 1))
             nc.scalar.copy(
-                wgt_wide[:, part],
-                wgt_turned[:, :, part].rearrange("p h a -> p a h").unsqueeze(3).to_broadcast([P, HEAD, 2, HEAD]),
+                wgt_wide[:, part].rearrange("p a u h c -> p a (u h) c"),
+                wgt_turned[:, :, :, part].rearrange("p u h a -> p a (u h)").unsqueeze(3).to_broadcast([P, 8, 4, HEAD]),
             )
-            nc.vector.transpose(wgt_sb[:, HALF * s : HALF * (s + 1)], wgt_wide[:, part].rearrange("p a h q -> p (a h q)"))
+            nc.vector.transpose(
+                wgt_sb[:, HALF * s : HALF * (s + 1)], wgt_wide[:, part].rearrange("p a u h c -> p (a u h c)")
+            )
+        def deal_scales(plane):
+            for q in range(1, 4):
+                nc.sync.dma_start(
+                    plane[QUAD * q : QUAD * q + 4, :].bitcast(I32), plane[4 * q : 4 * q + 4, :].bitcast(I32)
+                )
+
         for i in range(PACK):
             nc.sync.dma_start(planes[i][:], x_rows[i])
             if i == 0:
                 nc.sync.dma_start(offsets[:], offs)
-                nc.sync.dma_start(wd_sc[0:16, 0:N].bitcast(I32), wd8_scales[0].bitcast(I32))
-                nc.sync.dma_start(wd_sc[0:16, N:].bitcast(I32), wd4_scales[0].bitcast(I32))
             if i == 2:
-                for q in range(1, 4):
-                    nc.sync.dma_start(
-                        scales[QUAD * q : QUAD * q + 4, :].bitcast(I32), scales[4 * q : 4 * q + 4, :].bitcast(I32)
-                    )
+                deal_scales(wu_sc)
         for b in range(2):
             nc.sync.dma_start(wg_in[b][:], wg_rows[:, :, HALF * b : HALF * (b + 1)])
+        nc.sync.dma_start(scales_in[0:16, 0:N].bitcast(I32), wd8_scales[0].bitcast(I32))
+        nc.sync.dma_start(scales_in[0:16, N:].bitcast(I32), wd4_scales[0].bitcast(I32))
         nc.sync.dma_start(wd8_sb[:].bitcast(I32), wd8_words[0].rearrange("p n t -> p (n t)").bitcast(I32))
         nc.sync.dma_start(wd4_sb[:].bitcast(I32), wd4_words[0].bitcast(I32))
-        for s in range(2):
-            nc.sync.dma_start(res_sb[s][:], res_rows[:, :, HALF * s : HALF * (s + 1)])
+        nc.sync.dma_start(res_sb[0][:], res_rows[:, :, 0:HALF])
+        deal_scales(scales_in)
+        nc.sync.dma_start(res_sb[1][:], res_rows[:, :, HALF:J])
 
         picked = keep.tile([P, PACK, J], F32, name="picked")
         xg_bf = keep.tile([P, J, PACK], BF16, name="xg_bf", align_bytes=ALIGN)
@@ -246,7 +246,7 @@ def tile_list_silu_mix_res_kernel(
             nc.tensor.matmul_mx(
                 out=dst,
                 lhsT=codes,
-                lhsT_scale=wd_sc[:, N * b + P * a : N * b + P * (a + 1)],
+                lhsT_scale=scales_in[:, N * b + P * a : N * b + P * (a + 1)],
                 rhs=h_codes[n][:, b, j0 : j0 + width].bitcast(FP8X4),
                 rhs_scale=h_sc[n][:, b, j0 : j0 + width],
                 start=start,

@@ -24,11 +24,30 @@ CHUNK = 128
 GROUP = 2 * CHUNK
 GROUPS = J // GROUP
 ALIGN = 256
-SCALAR_SHARE = (40, 80)
+SCALAR_SHARE = (0, 100)
+FIRST = 3
+QUANT_AT = (6, 9, 13)
+HOLD = 3
+TAILC = 2
+PREFILL = 2
+ADD_LAG = 1
+COPY_LAG = 0
+DOWN_LAG = (1, 3)
+CHUNKWISE = 6
+GB = {(0, 0): 1, (0, 1): 1, (1, 1): 2}
+RING5 = 1
+QW1_AT = 1
+Q2_AT = 0
+Q34_AT = 0
+DEALQ = 0
+DEFER = 1
+EARLYQ = 1
+R1FIRST = 0
 LAST_PLANE_PIECES = (128, 128, 256, 256, 256)
 QUAD = 32
 HEAD = 16
-UP_BANKS, GATE_BANKS, OUT_BANKS = 3, 3, 2
+BANKS = (3, 3, 2)
+UP_BANKS, GATE_BANKS, OUT_BANKS = BANKS
 GATE_TILES = 8
 
 
@@ -53,7 +72,7 @@ def tile_list_silu_mix_res_kernel(
         wu_in = keep.tile([P, 2 * R], U8, name="wu_in", align_bytes=ALIGN)
         wgt_sb = keep.tile([P, J], F32, name="wgt_sb", align_bytes=ALIGN)
         planes = [keep.tile([P, T], F32, name=f"plane{i}") for i in range(PACK)]
-        wg_in = [keep.tile([P, PACK, HALF], F32, name=f"wg_in{b}") for b in range(2)]
+        wg_in = [keep.tile([P, PACK, HALF], F32, name=f"wg_in{b}", align_bytes=ALIGN) for b in range(2)]
         wd8_sb = keep.tile([P, N], U32, name="wd8_sb", align_bytes=ALIGN)
         wd4_sb = keep.tile([P, 2 * N], U8, name="wd4_sb", align_bytes=ALIGN)
         res_sb = [keep.tile([P, N // P, HALF], F32, name=f"res{s}") for s in range(2)]
@@ -89,9 +108,9 @@ def tile_list_silu_mix_res_kernel(
             nc.vector.transpose(
                 wgt_sb[:, HALF * s : HALF * (s + 1)], wgt_wide[:, part].rearrange("p a u h c -> p (a u h c)")
             )
-        def deal_scales(plane):
+        def deal_scales(plane, queue):
             for q in range(1, 4):
-                nc.sync.dma_start(
+                queue.dma_start(
                     plane[QUAD * q : QUAD * q + 4, :].bitcast(I32), plane[4 * q : 4 * q + 4, :].bitcast(I32)
                 )
 
@@ -100,7 +119,7 @@ def tile_list_silu_mix_res_kernel(
             if i == 0:
                 nc.sync.dma_start(offsets[:], offs)
             if i == 2:
-                deal_scales(wu_sc)
+                deal_scales(wu_sc, nc.scalar if DEALQ else nc.sync)
         for b in range(2):
             nc.sync.dma_start(wg_in[b][:], wg_rows[:, :, HALF * b : HALF * (b + 1)])
         nc.sync.dma_start(scales_in[0:16, 0:N].bitcast(I32), wd8_scales[0].bitcast(I32))
@@ -108,19 +127,29 @@ def tile_list_silu_mix_res_kernel(
         nc.sync.dma_start(wd8_sb[:].bitcast(I32), wd8_words[0].rearrange("p n t -> p (n t)").bitcast(I32))
         nc.sync.dma_start(wd4_sb[:].bitcast(I32), wd4_words[0].bitcast(I32))
         nc.sync.dma_start(res_sb[0][:], res_rows[:, :, 0:HALF])
-        deal_scales(scales_in)
+        deal_scales(scales_in, nc.sync)
         nc.sync.dma_start(res_sb[1][:], res_rows[:, :, HALF:J])
 
-        picked = keep.tile([P, PACK, J], F32, name="picked")
+        picked_flat = keep.tile([P, PACK * J], F32, name="picked", align_bytes=ALIGN)
+        picked = picked_flat[:].rearrange("p (i j) -> p i j", i=PACK)
         xg_bf = keep.tile([P, J, PACK], BF16, name="xg_bf", align_bytes=ALIGN)
+        xg_first = picked_flat[:, PACK * J - GROUP :].bitcast(BF16).rearrange("p (j i) -> p j i", i=PACK) if EARLYQ else xg_bf
         wg_bf = [
             keep.tile([P, PACK, P, PACK], BF16, name=f"wg_bf{b}", align_bytes=ALIGN)
             for b in range(2)
         ]
         wg_codes = [keep.tile([P, HALF], U32, name=f"wg_codes{b}", align_bytes=ALIGN) for b in range(2)]
         wg_sc = [keep.tile([P, HALF], U8, name=f"wg_sc{b}", align_bytes=ALIGN) for b in range(2)]
-        xg_codes = [keep.tile([P, HALF], U32, name=f"xg_codes{s}", align_bytes=ALIGN) for s in range(2)]
-        xg_sc = [keep.tile([P, HALF], U8, name=f"xg_sc{s}", align_bytes=ALIGN) for s in range(2)]
+        codes_early = keep.tile([P, GROUP], U32, name="codes_early", align_bytes=ALIGN)
+        codes_late = keep.tile([P, J - GROUP], U32, name="codes_late", tag=("late", "wg_in0", "wg_in1")[DEFER], align_bytes=ALIGN)
+        xg_sc = keep.tile([P, J], U8, name="xg_sc", align_bytes=ALIGN)
+
+        def xg_codes(j0, n):
+            return (codes_early[:, j0 : j0 + n] if j0 < GROUP else codes_late[:, j0 - GROUP : j0 - GROUP + n]).bitcast(FP8X4)
+
+        def rounded(j0, n):
+            return xg_first[:, j0 : j0 + n] if j0 < CHUNK else xg_bf[:, j0 : j0 + n]
+
         h_bf = [
             keep.tile([P, 2, GROUP, PACK], BF16, name=f"h_bf{n}", tag=f"stage{n}", align_bytes=ALIGN)
             for n in range(GROUPS)
@@ -129,7 +158,9 @@ def tile_list_silu_mix_res_kernel(
         h_sc = [keep.tile([P, 2, GROUP], U8, name=f"h_sc{n}", align_bytes=ALIGN) for n in range(GROUPS)]
         banks = [psum.tile([P, HALF], F32, name=f"bank{k}") for k in range(8)]
         gates = [keep.tile([P, 2 * HALF], F32, name=f"gate{k}") for k in range(GATE_TILES)]
-        first_gates = keep.tile([P, PACK, HALF], F32, name="first_gates", tag="wg_in1")
+
+
+        first_gates = keep.tile([P, PACK, HALF], F32, name="first_gates", tag="wg_in1", align_bytes=ALIGN)
 
         rings = {
             "up": banks[:UP_BANKS],
@@ -151,40 +182,42 @@ def tile_list_silu_mix_res_kernel(
             )
 
         def round_x(j0, n, i0):
+            if EARLYQ and j0 < CHUNK < j0 + n:
+                round_x(j0, CHUNK, i0)
+                round_x(CHUNK, n - CHUNK, i0)
+                return
             nc.scalar.copy(
-                xg_bf[:, j0 : j0 + n, i0 : i0 + 2],
+                rounded(j0, n)[:, :, i0 : i0 + 2],
                 picked[:, i0 : i0 + 2, j0 : j0 + n].rearrange("p i j -> p j i"),
             )
 
         def quant_x(j0, n):
-            s, c = divmod(j0, HALF)
             nc.vector.quantize_mx(
-                out=xg_codes[s][:, c : c + n].bitcast(FP8X4),
-                scales=xg_sc[s][:, c : c + n],
-                in_=xg_bf[:, j0 : j0 + n, :].rearrange("p j i -> p (j i)"),
+                out=xg_codes(j0, n),
+                scales=xg_sc[:, j0 : j0 + n],
+                in_=rounded(j0, n).rearrange("p j i -> p (j i)"),
             )
 
-        def round_wg(copy, b, m0, m1):
+        def round_wg(copy, b, m0, m1, t0=0, t1=PACK):
             copy(
-                wg_bf[b][:, :, m0:m1, :].rearrange("p t m i -> p m i t"),
-                wg_in[b][:, :, PACK * m0 : PACK * m1].rearrange("p i (m t) -> p m i t", t=PACK),
+                wg_bf[b][:, t0:t1, m0:m1, :].rearrange("p t m i -> p m i t"),
+                wg_in[b][:, :, PACK * m0 : PACK * m1].rearrange("p i (m t) -> p m i t", t=PACK)[:, :, :, t0:t1],
             )
 
-        def quant_wg(b):
+        def quant_wg(b, t0=0, t1=PACK):
             nc.vector.quantize_mx(
-                out=wg_codes[b][:].bitcast(FP8X4),
-                scales=wg_sc[b][:],
-                in_=wg_bf[b][:].rearrange("p t m i -> p (t m i)"),
+                out=wg_codes[b][:, P * t0 : P * t1].bitcast(FP8X4),
+                scales=wg_sc[b][:, P * t0 : P * t1],
+                in_=wg_bf[b][:, t0:t1].rearrange("p t m i -> p (t m i)"),
             )
 
         def first_stage(dst, codes, scales, j0, n):
-            s, c = divmod(j0, HALF)
             nc.tensor.matmul_mx(
                 out=dst,
                 lhsT=codes,
                 lhsT_scale=scales,
-                rhs=xg_codes[s][:, c : c + n].bitcast(FP8X4),
-                rhs_scale=xg_sc[s][:, c : c + n],
+                rhs=xg_codes(j0, n),
+                rhs_scale=xg_sc[:, j0 : j0 + n],
                 start=True,
                 stop=True,
             )
@@ -213,8 +246,8 @@ def tile_list_silu_mix_res_kernel(
             for d in range(2):
                 gate_of[b, c + d] = gate[:, :, CHUNK * d : CHUNK * (d + 1), :].rearrange("p u j e -> p j u e")
 
-        def up(b, c):
-            bank = take("up").rearrange("p (t j) -> p t j", t=PACK)
+        def up(b, c, ring_name):
+            bank = take(ring_name).rearrange("p (t j) -> p t j", t=PACK)
             for t in range(PACK):
                 c0 = HALF * b + P * t
                 first_stage(
@@ -222,10 +255,18 @@ def tile_list_silu_mix_res_kernel(
                 )
             up_of[b, c] = bank.rearrange("p (u e) j -> p j u e", u=2)
 
+        def place(n, b, j0):
+            if TAILC and n == GROUPS - 1:
+                return GROUP * (j0 // CHUNK) + CHUNK * b
+            return GROUP * b + j0
+
+        def quant_tail(d, b0, nb):
+            quant_h(GROUPS - 1, GROUP * d + CHUNK * b0, CHUNK * nb)
+
         def product(b, c):
             n, d = divmod(c, 2)
             nc.vector.tensor_tensor(
-                h_bf[n][:, b, CHUNK * d : CHUNK * (d + 1), :].rearrange("p j (u e) -> p j u e", u=2),
+                h_bf[n][:].rearrange("p b j t -> p (b j) t")[:, place(n, b, CHUNK * d) : place(n, b, CHUNK * d) + CHUNK, :].rearrange("p j (u e) -> p j u e", u=2),
                 up_of[b, c],
                 gate_of[b, c],
                 MULT,
@@ -247,8 +288,8 @@ def tile_list_silu_mix_res_kernel(
                 out=dst,
                 lhsT=codes,
                 lhsT_scale=scales_in[:, N * b + P * a : N * b + P * (a + 1)],
-                rhs=h_codes[n][:, b, j0 : j0 + width].bitcast(FP8X4),
-                rhs_scale=h_sc[n][:, b, j0 : j0 + width],
+                rhs=h_codes[n][:].rearrange("p b j -> p (b j)")[:, place(n, b, j0) : place(n, b, j0) + width].bitcast(FP8X4),
+                rhs_scale=h_sc[n][:].rearrange("p b j -> p (b j)")[:, place(n, b, j0) : place(n, b, j0) + width],
                 start=start,
                 stop=stop,
             )
@@ -273,8 +314,11 @@ def tile_list_silu_mix_res_kernel(
                 first, last = (b, a) == (0, 0), (b, a) == (1, N // P - 1)
                 down_pass(bank[:, CHUNK * a : CHUNK * (a + 1)], a, b, n, CHUNK * d, CHUNK, first, last)
 
-        def add_on_vector(y, res_part, out_part):
-            result = ring.tile(list(res_part.shape), F32, name="result")
+        def add_on_vector(y, res_part, out_part, held=False):
+            if held:
+                result = keep.tile(list(res_part.shape), F32, name="result_held", tag=f"stage{GROUPS - 1}", align_bytes=ALIGN)
+            else:
+                result = ring.tile(list(res_part.shape), F32, name="result")
             nc.vector.tensor_tensor(result[:], y, res_part, ADD)
             nc.sync.dma_start(out_part, result[:])
 
@@ -283,10 +327,15 @@ def tile_list_silu_mix_res_kernel(
             nc.scalar.copy(y_sb[:], y)
             return y_sb[:], res_part, out_part
 
+        sums = {}
+
         def add_on_gpsimd(n, y, res_part, out_part):
-            result = keep.tile([P, 2, 2, GROUP], F32, name=f"result{n}", tag=f"stage{n + 1}", align_bytes=ALIGN)
-            nc.gpsimd.tensor_tensor(result[:, 0], y, res_part, ADD)
-            nc.sync.dma_start(out_part, result[:, 0])
+            if n not in sums:
+                sums[n] = [keep.tile([P, 2, 2, GROUP], F32, name=f"result{n}", tag=f"stage{n}", align_bytes=ALIGN), 0]
+            result = sums[n][0][:, sums[n][1]]
+            sums[n][1] = sums[n][1] + 1
+            nc.gpsimd.tensor_tensor(result, y, res_part, ADD)
+            nc.sync.dma_start(out_part, result)
 
         for i in range(2):
             for j0 in (0, HALF):
@@ -294,66 +343,108 @@ def tile_list_silu_mix_res_kernel(
                 if i == 1:
                     round_x(j0, HALF, 0)
         gather(2, 0, J)
-        round_wg(nc.scalar.copy, 0, 0, SCALAR_SHARE[0])
-        j0 = 0
-        for n in LAST_PLANE_PIECES:
+        if SCALAR_SHARE[0]:
+            round_wg(nc.scalar.copy, 0, 0, SCALAR_SHARE[0])
+        pieces = [(sum(LAST_PLANE_PIECES[:n]), LAST_PLANE_PIECES[n]) for n in range(len(LAST_PLANE_PIECES))]
+        for j0, n in pieces:
             gather(PACK - 1, j0, n)
             round_x(j0, n, 2)
-            if j0 < HALF:
+            if j0 < GROUP:
                 quant_x(j0, n)
-            j0 = j0 + n
-            if j0 == HALF:
-                round_wg(nc.vector.tensor_copy, 0, SCALAR_SHARE[0], P)
-            elif j0 == J:
-                quant_x(HALF, HALF)
-            elif j0 > HALF:
-                quant_wg(0)
-        round_wg(nc.scalar.copy, 1, 0, SCALAR_SHARE[1])
-        round_wg(nc.vector.tensor_copy, 1, SCALAR_SHARE[1], P)
-        quant_wg(1)
+        round_wg(nc.vector.tensor_copy, 0, SCALAR_SHARE[0], P)
+        quant_wg(0)
+        if SCALAR_SHARE[1]:
+            round_wg(nc.scalar.copy, 1, 0, SCALAR_SHARE[1])
+        if R1FIRST:
+            round_wg(nc.vector.tensor_copy, 1, SCALAR_SHARE[1], P)
+        if not Q2_AT:
+            quant_x(GROUP, GROUP)
+        if R1FIRST == 2:
+            quant_wg(1)
+        if not Q34_AT:
+            quant_x(HALF, HALF)
+        if not R1FIRST and SCALAR_SHARE[1] < P:
+            round_wg(nc.vector.tensor_copy, 1, SCALAR_SHARE[1], P)
+        if R1FIRST < 2 and not QW1_AT:
+            quant_wg(1)
 
         products = [(b, 2 * n + d) for n in range(GROUPS) for b in range(2) for d in range(2)]
-        products = products[:2] + [products[4]] + products[2:4] + products[5:]
+        early = [(0, c) for c in range(FIRST)]
+        products = early + [u for u in products if u not in early]
         last = GROUPS - 1
-        quantise_at = {6: 0, 9: 1, 13: 2}
-        waiting, for_gpsimd = {}, {}
+        if TAILC:
+            products = products[:-3] + [products[-2], products[-3], products[-1]]
+        quantise_at = {QUANT_AT[g]: g for g in range(last)}
+        quantise_steps = [(QUANT_AT[g], g) for g in range(last)]
+        to_add, to_copy, for_gpsimd, quantised = [], [], [], set()
         tail_banks = []
         for k in range(len(products) + 1):
-            n, step = divmod(k, 4)
             if k < len(products):
                 b, c = products[k]
-                if k < 3:
+                if k < HOLD:
                     gate_chunk(b, c, first_gates[:, k])
-                elif k < 6:
+                elif k < CHUNKWISE or (TAILC and k >= len(products) - 4) or (c % 2 == 1 and (b, c) not in gate_of):
                     gate_chunk(b, c, take("silu")[:, 0:HALF])
                 elif c % 2 == 0:
                     gate_group(b, c)
-                up(b, c)
+                up(b, c, "out" if (b == 1 and c < PREFILL) or k in range(8, 8 + RING5) else "up")
             if k >= 1:
                 product(*products[k - 1])
+            if Q2_AT and k == Q2_AT:
+                quant_x(GROUP, GROUP)
+            if Q34_AT and k == Q34_AT:
+                quant_x(HALF, HALF)
+            if QW1_AT and k == QW1_AT:
+                quant_wg(1)
             if k in quantise_at:
                 quant_h(quantise_at[k], 0, 2 * GROUP)
-            if k - 1 in quantise_at:
-                g = quantise_at[k - 1]
-                waiting[k + 1] = down_group(g, 0)
-                if g < 2:
-                    for_gpsimd[g] = leave_psum(*waiting.pop(k + 1))
-            if k in waiting:
-                add_on_vector(*waiting.pop(k))
-            if k - 2 in quantise_at:
-                waiting[k + 1] = down_group(quantise_at[k - 2], 1)
-            if quantise_at.get(k, 0) > 0:
-                add_on_gpsimd(quantise_at[k] - 1, *for_gpsimd[quantise_at[k] - 1])
-            if k == len(products) - 1:
+                quantised.add(quantise_at[k])
+            for u in range(2):
+                for g in [g for kq, g in quantise_steps if min(kq + DOWN_LAG[u], len(products)) == k]:
+                    while len(to_add) + len(to_copy) >= 2:
+                        if to_copy and (not to_add or to_copy[0][3] < to_add[0][2]):
+                            first = to_copy.pop(0)
+                            for_gpsimd.append((first[1], leave_psum(*first[2])))
+                        else:
+                            add_on_vector(*to_add.pop(0)[1])
+                    if (g, u) in GB:
+                        to_copy.append((k + COPY_LAG, GB[g, u], down_group(g, u), 2 * g + u))
+                    else:
+                        to_add.append((k + ADD_LAG, down_group(g, u), 2 * g + u))
+            while to_copy and (to_copy[0][0] <= k or k == len(products)):
+                first = to_copy.pop(0)
+                for_gpsimd.append((first[1], leave_psum(*first[2])))
+            while for_gpsimd and for_gpsimd[0][0] in quantised:
+                first = for_gpsimd.pop(0)
+                add_on_gpsimd(first[0], *first[1])
+            if TAILC and k == len(products) - 1:
+                quant_tail(0, 0, 2)
+                tail_banks.append(take("gate"))
+                for b in range(2):
+                    down_chunk(tail_banks[0], b, last, 0)
+                quant_tail(1, 0, 1)
+                tail_banks.append(take("gate"))
+                down_chunk(tail_banks[1], 0, last, 1)
+            while to_add and (to_add[0][0] <= k or k == len(products)) and not (TAILC == 2 and to_add[0][2] == 5):
+                add_on_vector(*to_add.pop(0)[1])
+            if not TAILC and k == len(products) - 1:
                 quant_h(last, 0, GROUP)
                 for d in range(2):
                     tail_banks.append(take("gate"))
                     down_chunk(tail_banks[d], 0, last, d)
                 quant_h(last, GROUP, CHUNK)
                 down_chunk(tail_banks[0], 1, last, 0)
-        quant_h(last, GROUP + CHUNK, CHUNK)
+        if TAILC == 2:
+            add_on_vector(*operands(tail_banks[0], 0, 4, J - GROUP, CHUNK))
+        if TAILC:
+            quant_tail(1, 1, 1)
+        else:
+            quant_h(last, GROUP + CHUNK, CHUNK)
         down_chunk(tail_banks[1], 1, last, 1)
-        add_on_vector(*operands(tail_banks[0], 0, 4, J - GROUP, CHUNK))
+        if TAILC == 2:
+            add_on_vector(*to_add.pop(0)[1], held=True)
+        else:
+            add_on_vector(*operands(tail_banks[0], 0, 4, J - GROUP, CHUNK))
         y, res_part, out_part = operands(tail_banks[1], 0, 4, J - CHUNK, CHUNK)
         for a0 in (0, 2):
             add_on_vector(y[:, a0 : a0 + 2], res_part[:, a0 : a0 + 2], out_part[:, a0 : a0 + 2])

@@ -37,9 +37,14 @@ CHUNKWISE = 6
 GB = {(0, 0): 1, (0, 1): 1, (1, 1): 2}
 RING5 = 1
 QW1_AT = 1
+EARLY = 256
+QFIRST = (128, 128)
+SCFIRST = 0
+BIAS_N = 1
+LASTSPLIT = 1
 Q2_AT = 0
 Q34_AT = 0
-DEALQ = 0
+DEALQ = 1
 DEFER = 1
 EARLYQ = 1
 R1FIRST = 0
@@ -86,8 +91,11 @@ def tile_list_silu_mix_res_kernel(
         wu_codes = keep.tile([P, 2 * R], U8, name="wu_codes", align_bytes=ALIGN)
         head_rows = wgt.rearrange("(g c) (a s) -> c g a s", c=HEAD, a=HEAD)[0]
         nc.sync.dma_start(wgt_in[:], head_rows)
+        if SCFIRST:
+            nc.sync.dma_start(scales_in[0:16, :].bitcast(I32), wu_scales[0].bitcast(I32))
         nc.sync.dma_start(wu_in[:].bitcast(I32), wu_words[0].bitcast(I32))
-        nc.sync.dma_start(scales_in[0:16, :].bitcast(I32), wu_scales[0].bitcast(I32))
+        if not SCFIRST:
+            nc.sync.dma_start(scales_in[0:16, :].bitcast(I32), wu_scales[0].bitcast(I32))
         nc.scalar.activation(zero[:], zero_in[:], SILU)
         for u in range(2):
             nc.vector.transpose(wgt_turned[:, u].rearrange("p h a -> p (h a)"), wgt_in[:, QUAD * u : QUAD * (u + 1)])
@@ -140,12 +148,12 @@ def tile_list_silu_mix_res_kernel(
         ]
         wg_codes = [keep.tile([P, HALF], U32, name=f"wg_codes{b}", align_bytes=ALIGN) for b in range(2)]
         wg_sc = [keep.tile([P, HALF], U8, name=f"wg_sc{b}", align_bytes=ALIGN) for b in range(2)]
-        codes_early = keep.tile([P, GROUP], U32, name="codes_early", align_bytes=ALIGN)
-        codes_late = keep.tile([P, J - GROUP], U32, name="codes_late", tag=("late", "wg_in0", "wg_in1")[DEFER], align_bytes=ALIGN)
+        codes_early = keep.tile([P, EARLY], U32, name="codes_early", align_bytes=ALIGN)
+        codes_late = keep.tile([P, J - EARLY], U32, name="codes_late", tag=("late", "wg_in0", "wg_in1")[DEFER], align_bytes=ALIGN)
         xg_sc = keep.tile([P, J], U8, name="xg_sc", align_bytes=ALIGN)
 
         def xg_codes(j0, n):
-            return (codes_early[:, j0 : j0 + n] if j0 < GROUP else codes_late[:, j0 - GROUP : j0 - GROUP + n]).bitcast(FP8X4)
+            return (codes_early[:, j0 : j0 + n] if j0 < EARLY else codes_late[:, j0 - EARLY : j0 - EARLY + n]).bitcast(FP8X4)
 
         def rounded(j0, n):
             return xg_first[:, j0 : j0 + n] if j0 < CHUNK else xg_bf[:, j0 : j0 + n]
@@ -228,12 +236,21 @@ def tile_list_silu_mix_res_kernel(
 
         gate_of, up_of = {}, {}
 
+        made = []
+
+        def silu(dst, bank):
+            if len(made) < BIAS_N:
+                nc.scalar.activation(dst, bank, SILU, bias=zero[:])
+            else:
+                nc.scalar.activation(dst, bank, SILU)
+            made.append(dst)
+
         def gate_chunk(b, c, tile):
             bank = take("gate").rearrange("p (t j) -> p t j", t=PACK)
             for t in range(PACK):
                 gate_pass(bank[:, t, :], b, t, CHUNK * c, CHUNK)
             gate = tile.rearrange("p (j t) -> p j t", t=PACK)
-            nc.scalar.activation(gate, bank.rearrange("p t j -> p j t"), SILU, bias=zero[:])
+            silu(gate, bank.rearrange("p t j -> p j t"))
             gate_of[b, c] = gate.rearrange("p j (u e) -> p j u e", u=2)
 
         def gate_group(b, c):
@@ -242,7 +259,7 @@ def tile_list_silu_mix_res_kernel(
                 bank = take("gate").rearrange("p (e j) -> p e j", e=2)
                 for e in range(2):
                     gate_pass(bank[:, e, :], b, 2 * u + e, CHUNK * c, GROUP)
-                nc.scalar.activation(gate[:, u, :, :], bank.rearrange("p e j -> p j e"), SILU, bias=zero[:])
+                silu(gate[:, u, :, :], bank.rearrange("p e j -> p j e"))
             for d in range(2):
                 gate_of[b, c + d] = gate[:, :, CHUNK * d : CHUNK * (d + 1), :].rearrange("p u j e -> p j u e")
 
@@ -256,7 +273,7 @@ def tile_list_silu_mix_res_kernel(
             up_of[b, c] = bank.rearrange("p (u e) j -> p j u e", u=2)
 
         def place(n, b, j0):
-            if TAILC and n == GROUPS - 1:
+            if TAILC in (1, 2) and n == GROUPS - 1:
                 return GROUP * (j0 // CHUNK) + CHUNK * b
             return GROUP * b + j0
 
@@ -299,8 +316,8 @@ def tile_list_silu_mix_res_kernel(
             y = bank.rearrange("p (a j) -> p a j", j=width)
             return y, res_sb[s][:, a0:a1, c : c + width], out_rows[:, a0:a1, j0 : j0 + width]
 
-        def down_group(n, u):
-            bank = take("out")
+        def down_group(n, u, ring_name="out"):
+            bank = take(ring_name)
             for e in range(2):
                 c0 = GROUP * e
                 down_pass(bank[:, c0 : c0 + GROUP], 2 * u + e, 0, n, 0, GROUP, True, False)
@@ -346,18 +363,20 @@ def tile_list_silu_mix_res_kernel(
         if SCALAR_SHARE[0]:
             round_wg(nc.scalar.copy, 0, 0, SCALAR_SHARE[0])
         pieces = [(sum(LAST_PLANE_PIECES[:n]), LAST_PLANE_PIECES[n]) for n in range(len(LAST_PLANE_PIECES))]
+        left = list(QFIRST)
         for j0, n in pieces:
             gather(PACK - 1, j0, n)
             round_x(j0, n, 2)
-            if j0 < GROUP:
-                quant_x(j0, n)
+            while left and EARLY - sum(left) + left[0] <= j0 + n:
+                quant_x(EARLY - sum(left), left[0])
+                left.pop(0)
         round_wg(nc.vector.tensor_copy, 0, SCALAR_SHARE[0], P)
         quant_wg(0)
         if SCALAR_SHARE[1]:
             round_wg(nc.scalar.copy, 1, 0, SCALAR_SHARE[1])
         if R1FIRST:
             round_wg(nc.vector.tensor_copy, 1, SCALAR_SHARE[1], P)
-        if not Q2_AT:
+        if not Q2_AT and EARLY < HALF:
             quant_x(GROUP, GROUP)
         if R1FIRST == 2:
             quant_wg(1)
@@ -372,7 +391,7 @@ def tile_list_silu_mix_res_kernel(
         early = [(0, c) for c in range(FIRST)]
         products = early + [u for u in products if u not in early]
         last = GROUPS - 1
-        if TAILC:
+        if TAILC in (1, 2):
             products = products[:-3] + [products[-2], products[-3], products[-1]]
         quantise_at = {QUANT_AT[g]: g for g in range(last)}
         quantise_steps = [(QUANT_AT[g], g) for g in range(last)]
@@ -383,7 +402,7 @@ def tile_list_silu_mix_res_kernel(
                 b, c = products[k]
                 if k < HOLD:
                     gate_chunk(b, c, first_gates[:, k])
-                elif k < CHUNKWISE or (TAILC and k >= len(products) - 4) or (c % 2 == 1 and (b, c) not in gate_of):
+                elif k < CHUNKWISE or (TAILC in (1, 2) and k >= len(products) - 4) or (c % 2 == 1 and (b, c) not in gate_of):
                     gate_chunk(b, c, take("silu")[:, 0:HALF])
                 elif c % 2 == 0:
                     gate_group(b, c)
@@ -417,7 +436,7 @@ def tile_list_silu_mix_res_kernel(
             while for_gpsimd and for_gpsimd[0][0] in quantised:
                 first = for_gpsimd.pop(0)
                 add_on_gpsimd(first[0], *first[1])
-            if TAILC and k == len(products) - 1:
+            if TAILC in (1, 2) and k == len(products) - 1:
                 quant_tail(0, 0, 2)
                 tail_banks.append(take("gate"))
                 for b in range(2):
@@ -425,7 +444,7 @@ def tile_list_silu_mix_res_kernel(
                 quant_tail(1, 0, 1)
                 tail_banks.append(take("gate"))
                 down_chunk(tail_banks[1], 0, last, 1)
-            while to_add and (to_add[0][0] <= k or k == len(products)) and not (TAILC == 2 and to_add[0][2] == 5):
+            while to_add and (to_add[0][0] <= k or k == len(products)) and not (TAILC >= 2 and to_add[0][2] == 5) and not (TAILC == 3 and to_add[0][2] == 4 and k < len(products)):
                 add_on_vector(*to_add.pop(0)[1])
             if not TAILC and k == len(products) - 1:
                 quant_h(last, 0, GROUP)
@@ -434,17 +453,28 @@ def tile_list_silu_mix_res_kernel(
                     down_chunk(tail_banks[d], 0, last, d)
                 quant_h(last, GROUP, CHUNK)
                 down_chunk(tail_banks[0], 1, last, 0)
-        if TAILC == 2:
-            add_on_vector(*operands(tail_banks[0], 0, 4, J - GROUP, CHUNK))
-        if TAILC:
-            quant_tail(1, 1, 1)
-        else:
-            quant_h(last, GROUP + CHUNK, CHUNK)
-        down_chunk(tail_banks[1], 1, last, 1)
-        if TAILC == 2:
+        if TAILC == 3:
+            quant_h(last, 0, 2 * GROUP)
+            ends = [down_group(last, u, "gate") for u in range(2)]
             add_on_vector(*to_add.pop(0)[1], held=True)
+            add_on_vector(*ends[0])
+            if LASTSPLIT:
+                for e in range(2):
+                    add_on_vector(*[a[:, e : e + 1] for a in ends[1]])
+            else:
+                add_on_vector(*ends[1])
         else:
-            add_on_vector(*operands(tail_banks[0], 0, 4, J - GROUP, CHUNK))
-        y, res_part, out_part = operands(tail_banks[1], 0, 4, J - CHUNK, CHUNK)
-        for a0 in (0, 2):
-            add_on_vector(y[:, a0 : a0 + 2], res_part[:, a0 : a0 + 2], out_part[:, a0 : a0 + 2])
+            if TAILC == 2:
+                add_on_vector(*operands(tail_banks[0], 0, 4, J - GROUP, CHUNK))
+            if TAILC:
+                quant_tail(1, 1, 1)
+            else:
+                quant_h(last, GROUP + CHUNK, CHUNK)
+            down_chunk(tail_banks[1], 1, last, 1)
+            if TAILC == 2:
+                add_on_vector(*to_add.pop(0)[1], held=True)
+            else:
+                add_on_vector(*operands(tail_banks[0], 0, 4, J - GROUP, CHUNK))
+            y, res_part, out_part = operands(tail_banks[1], 0, 4, J - CHUNK, CHUNK)
+            for a0 in (0, 2):
+                add_on_vector(y[:, a0 : a0 + 2], res_part[:, a0 : a0 + 2], out_part[:, a0 : a0 + 2])

@@ -41,6 +41,7 @@ EARLY = 256
 QFIRST = (128, 128)
 SCFIRST = 0
 BIAS_N = 1
+VSHARE = 28
 LASTSPLIT = 1
 Q2_AT = 0
 Q34_AT = 0
@@ -77,7 +78,9 @@ def tile_list_silu_mix_res_kernel(
         wu_in = keep.tile([P, 2 * R], U8, name="wu_in", align_bytes=ALIGN)
         wgt_sb = keep.tile([P, J], F32, name="wgt_sb", align_bytes=ALIGN)
         planes = [keep.tile([P, T], F32, name=f"plane{i}") for i in range(PACK)]
-        wg_in = [keep.tile([P, PACK, HALF], F32, name=f"wg_in{b}", align_bytes=ALIGN) for b in range(2)]
+        edge = HALF + PACK * VSHARE
+        wg_in = [keep.tile([P, PACK, edge], F32, name="wg_in0", align_bytes=ALIGN)]
+        wg_in.append(keep.tile([P, PACK, R - edge], F32, name="wg_in1", align_bytes=ALIGN))
         wd8_sb = keep.tile([P, N], U32, name="wd8_sb", align_bytes=ALIGN)
         wd4_sb = keep.tile([P, 2 * N], U8, name="wd4_sb", align_bytes=ALIGN)
         res_sb = [keep.tile([P, N // P, HALF], F32, name=f"res{s}") for s in range(2)]
@@ -128,8 +131,8 @@ def tile_list_silu_mix_res_kernel(
                 nc.sync.dma_start(offsets[:], offs)
             if i == 2:
                 deal_scales(wu_sc, nc.scalar if DEALQ else nc.sync)
-        for b in range(2):
-            nc.sync.dma_start(wg_in[b][:], wg_rows[:, :, HALF * b : HALF * (b + 1)])
+        nc.sync.dma_start(wg_in[0][:], wg_rows[:, :, 0:edge])
+        nc.sync.dma_start(wg_in[1][:], wg_rows[:, :, edge:R])
         nc.sync.dma_start(scales_in[0:16, 0:N].bitcast(I32), wd8_scales[0].bitcast(I32))
         nc.sync.dma_start(scales_in[0:16, N:].bitcast(I32), wd4_scales[0].bitcast(I32))
         nc.sync.dma_start(wd8_sb[:].bitcast(I32), wd8_words[0].rearrange("p n t -> p (n t)").bitcast(I32))
@@ -207,9 +210,11 @@ def tile_list_silu_mix_res_kernel(
             )
 
         def round_wg(copy, b, m0, m1, t0=0, t1=PACK):
+            c0, c1 = HALF * b + PACK * m0, HALF * b + PACK * m1
+            rows = wg_in[0][:, :, c0:c1] if c1 <= edge else wg_in[1][:, :, c0 - edge : c1 - edge]
             copy(
                 wg_bf[b][:, t0:t1, m0:m1, :].rearrange("p t m i -> p m i t"),
-                wg_in[b][:, :, PACK * m0 : PACK * m1].rearrange("p i (m t) -> p m i t", t=PACK)[:, :, :, t0:t1],
+                rows.rearrange("p i (m t) -> p m i t", t=PACK)[:, :, :, t0:t1],
             )
 
         def quant_wg(b, t0=0, t1=PACK):
@@ -370,22 +375,12 @@ def tile_list_silu_mix_res_kernel(
             while left and EARLY - sum(left) + left[0] <= j0 + n:
                 quant_x(EARLY - sum(left), left[0])
                 left.pop(0)
-        round_wg(nc.vector.tensor_copy, 0, SCALAR_SHARE[0], P)
+        round_wg(nc.vector.tensor_copy, 0, 0, P)
+        round_wg(nc.vector.tensor_copy, 1, 0, VSHARE)
         quant_wg(0)
-        if SCALAR_SHARE[1]:
-            round_wg(nc.scalar.copy, 1, 0, SCALAR_SHARE[1])
-        if R1FIRST:
-            round_wg(nc.vector.tensor_copy, 1, SCALAR_SHARE[1], P)
-        if not Q2_AT and EARLY < HALF:
-            quant_x(GROUP, GROUP)
-        if R1FIRST == 2:
-            quant_wg(1)
-        if not Q34_AT:
-            quant_x(HALF, HALF)
-        if not R1FIRST and SCALAR_SHARE[1] < P:
-            round_wg(nc.vector.tensor_copy, 1, SCALAR_SHARE[1], P)
-        if R1FIRST < 2 and not QW1_AT:
-            quant_wg(1)
+        round_wg(nc.scalar.copy, 1, VSHARE, P)
+        quant_x(GROUP, GROUP)
+        quant_x(HALF, HALF)
 
         products = [(b, 2 * n + d) for n in range(GROUPS) for b in range(2) for d in range(2)]
         early = [(0, c) for c in range(FIRST)]

@@ -24,37 +24,23 @@ CHUNK = 128
 GROUP = 2 * CHUNK
 GROUPS = J // GROUP
 ALIGN = 256
-SCALAR_SHARE = (0, 100)
-FIRST = 3
-QUANT_AT = (6, 9, 13)
-HOLD = 3
-TAILC = 2
-PREFILL = 2
-ADD_LAG = 1
-COPY_LAG = 0
-DOWN_LAG = (1, 3)
-CHUNKWISE = 6
-GB = {(0, 0): 1, (0, 1): 1, (1, 1): 2}
-RING5 = 1
-QW1_AT = 1
-EARLY = 256
-QFIRST = (128, 128)
-SCFIRST = 0
-BIAS_N = 1
-VSHARE = 28
-LASTSPLIT = 1
-Q2_AT = 0
-Q34_AT = 0
-DEALQ = 1
-DEFER = 1
-EARLYQ = 1
-R1FIRST = 0
 LAST_PLANE_PIECES = (128, 128, 256, 256, 256)
+EARLY = 256
 QUAD = 32
 HEAD = 16
-BANKS = (3, 3, 2)
-UP_BANKS, GATE_BANKS, OUT_BANKS = BANKS
-GATE_TILES = 8
+UP_BANKS, GATE_BANKS = 3, 3
+VSHARE = 32
+ORDER = ((0, 0), (0, 1), (0, 2), (1, 0), (1, 1), (0, 3), (1, 2), (1, 3), (0, 4), (0, 5), (1, 4), (1, 5), (0, 6), (1, 6), (0, 7), (1, 7))
+GATES = ((0, 0, 0, 1), (0, 0, 1, 1), (0, 0, 2, 1), (0, 1, 0, 1), (1, 1, 1, 1), (2, 0, 3, 1), (3, 1, 2, 2), (5, 0, 4, 2), (7, 1, 4, 2),
+         (9, 0, 6, 1), (10, 1, 6, 1), (11, 0, 7, 1), (12, 1, 7, 1))
+ON_GPSIMD = ()
+SCALES_BEHIND = 3
+PREFILL = 5
+COPY_LEAD = -1
+QUANT_AT = (6, 9, 13)
+DOWN_LAG = (0, 1)
+ADD_LAG = 2
+GB = {(0, 0): 1, (0, 1): 1, (1, 1): 2}
 
 
 def tile_list_silu_mix_res_kernel(
@@ -73,14 +59,17 @@ def tile_list_silu_mix_res_kernel(
         zero_in = keep.tile([P, 1], F32, name="zero_in")
         nc.vector.memset(zero_in[:], 0.0)
         zero = keep.tile([P, 1], F32, name="zero")
-        wu_sc = keep.tile([P, R], U8, name="wu_sc", align_bytes=ALIGN)
+        wu_tile = keep.tile([P, R], U8, name="wu_sc", align_bytes=ALIGN)
+        wu_sc = wu_tile[:]
+        wd_sc = scales_in[:]
 
         wu_in = keep.tile([P, 2 * R], U8, name="wu_in", align_bytes=ALIGN)
         wgt_sb = keep.tile([P, J], F32, name="wgt_sb", align_bytes=ALIGN)
         planes = [keep.tile([P, T], F32, name=f"plane{i}") for i in range(PACK)]
         edge = HALF + PACK * VSHARE
-        wg_in = [keep.tile([P, PACK, edge], F32, name="wg_in0", align_bytes=ALIGN)]
+        wg_in = [keep.tile([P, PACK, HALF], F32, name="wg_in0", align_bytes=ALIGN)]
         wg_in.append(keep.tile([P, PACK, R - edge], F32, name="wg_in1", align_bytes=ALIGN))
+        wg_in.append(keep.tile([P, PACK, edge - HALF], F32, name="wg_in2", align_bytes=ALIGN))
         wd8_sb = keep.tile([P, N], U32, name="wd8_sb", align_bytes=ALIGN)
         wd4_sb = keep.tile([P, 2 * N], U8, name="wd4_sb", align_bytes=ALIGN)
         res_sb = [keep.tile([P, N // P, HALF], F32, name=f"res{s}") for s in range(2)]
@@ -94,16 +83,13 @@ def tile_list_silu_mix_res_kernel(
         wu_codes = keep.tile([P, 2 * R], U8, name="wu_codes", align_bytes=ALIGN)
         head_rows = wgt.rearrange("(g c) (a s) -> c g a s", c=HEAD, a=HEAD)[0]
         nc.sync.dma_start(wgt_in[:], head_rows)
-        if SCFIRST:
-            nc.sync.dma_start(scales_in[0:16, :].bitcast(I32), wu_scales[0].bitcast(I32))
         nc.sync.dma_start(wu_in[:].bitcast(I32), wu_words[0].bitcast(I32))
-        if not SCFIRST:
-            nc.sync.dma_start(scales_in[0:16, :].bitcast(I32), wu_scales[0].bitcast(I32))
+        nc.sync.dma_start(scales_in[0:16, :].bitcast(I32), wu_scales[0].bitcast(I32))
         nc.scalar.activation(zero[:], zero_in[:], SILU)
         for u in range(2):
             nc.vector.transpose(wgt_turned[:, u].rearrange("p h a -> p (h a)"), wgt_in[:, QUAD * u : QUAD * (u + 1)])
         nc.vector.tensor_copy(
-            wu_sc[:].rearrange("p (b t m) -> p b t m", b=2, t=PACK),
+            wu_sc.rearrange("p (b t m) -> p b t m", b=2, t=PACK),
             scales_in[:].rearrange("p (b m t) -> p b t m", b=2, t=PACK),
         )
         nc.vector.tensor_copy(
@@ -130,21 +116,23 @@ def tile_list_silu_mix_res_kernel(
             if i == 0:
                 nc.sync.dma_start(offsets[:], offs)
             if i == 2:
-                deal_scales(wu_sc, nc.scalar if DEALQ else nc.sync)
-        nc.sync.dma_start(wg_in[0][:], wg_rows[:, :, 0:edge])
+                deal_scales(wu_sc, nc.scalar)
+            if i == SCALES_BEHIND:
+                nc.sync.dma_start(wd_sc[0:16, 0:N].bitcast(I32), wd8_scales[0].bitcast(I32))
+                nc.sync.dma_start(wd_sc[0:16, N:].bitcast(I32), wd4_scales[0].bitcast(I32))
+        nc.sync.dma_start(wg_in[0][:], wg_rows[:, :, 0:HALF])
         nc.sync.dma_start(wg_in[1][:], wg_rows[:, :, edge:R])
-        nc.sync.dma_start(scales_in[0:16, 0:N].bitcast(I32), wd8_scales[0].bitcast(I32))
-        nc.sync.dma_start(scales_in[0:16, N:].bitcast(I32), wd4_scales[0].bitcast(I32))
+        nc.sync.dma_start(wg_in[2][:], wg_rows[:, :, HALF:edge])
+        deal_scales(wd_sc, nc.sync)
         nc.sync.dma_start(wd8_sb[:].bitcast(I32), wd8_words[0].rearrange("p n t -> p (n t)").bitcast(I32))
         nc.sync.dma_start(wd4_sb[:].bitcast(I32), wd4_words[0].bitcast(I32))
         nc.sync.dma_start(res_sb[0][:], res_rows[:, :, 0:HALF])
-        deal_scales(scales_in, nc.sync)
         nc.sync.dma_start(res_sb[1][:], res_rows[:, :, HALF:J])
 
         picked_flat = keep.tile([P, PACK * J], F32, name="picked", align_bytes=ALIGN)
         picked = picked_flat[:].rearrange("p (i j) -> p i j", i=PACK)
         xg_bf = keep.tile([P, J, PACK], BF16, name="xg_bf", align_bytes=ALIGN)
-        xg_first = picked_flat[:, PACK * J - GROUP :].bitcast(BF16).rearrange("p (j i) -> p j i", i=PACK) if EARLYQ else xg_bf
+        xg_first = picked_flat[:, PACK * J - GROUP :].bitcast(BF16).rearrange("p (j i) -> p j i", i=PACK)
         wg_bf = [
             keep.tile([P, PACK, P, PACK], BF16, name=f"wg_bf{b}", align_bytes=ALIGN)
             for b in range(2)
@@ -152,7 +140,7 @@ def tile_list_silu_mix_res_kernel(
         wg_codes = [keep.tile([P, HALF], U32, name=f"wg_codes{b}", align_bytes=ALIGN) for b in range(2)]
         wg_sc = [keep.tile([P, HALF], U8, name=f"wg_sc{b}", align_bytes=ALIGN) for b in range(2)]
         codes_early = keep.tile([P, EARLY], U32, name="codes_early", align_bytes=ALIGN)
-        codes_late = keep.tile([P, J - EARLY], U32, name="codes_late", tag=("late", "wg_in0", "wg_in1")[DEFER], align_bytes=ALIGN)
+        codes_late = keep.tile([P, J - EARLY], U32, name="codes_late", tag="wg_in0", align_bytes=ALIGN)
         xg_sc = keep.tile([P, J], U8, name="xg_sc", align_bytes=ALIGN)
 
         def xg_codes(j0, n):
@@ -168,16 +156,12 @@ def tile_list_silu_mix_res_kernel(
         h_codes = [keep.tile([P, 2, GROUP], U32, name=f"h_codes{n}", align_bytes=ALIGN) for n in range(GROUPS)]
         h_sc = [keep.tile([P, 2, GROUP], U8, name=f"h_sc{n}", align_bytes=ALIGN) for n in range(GROUPS)]
         banks = [psum.tile([P, HALF], F32, name=f"bank{k}") for k in range(8)]
-        gates = [keep.tile([P, 2 * HALF], F32, name=f"gate{k}") for k in range(GATE_TILES)]
 
-
-        first_gates = keep.tile([P, PACK, HALF], F32, name="first_gates", tag="wg_in1", align_bytes=ALIGN)
 
         rings = {
             "up": banks[:UP_BANKS],
             "gate": banks[UP_BANKS : UP_BANKS + GATE_BANKS],
             "out": banks[UP_BANKS + GATE_BANKS :],
-            "silu": gates,
         }
 
         def take(name):
@@ -193,7 +177,7 @@ def tile_list_silu_mix_res_kernel(
             )
 
         def round_x(j0, n, i0):
-            if EARLYQ and j0 < CHUNK < j0 + n:
+            if j0 < CHUNK < j0 + n:
                 round_x(j0, CHUNK, i0)
                 round_x(CHUNK, n - CHUNK, i0)
                 return
@@ -211,7 +195,12 @@ def tile_list_silu_mix_res_kernel(
 
         def round_wg(copy, b, m0, m1, t0=0, t1=PACK):
             c0, c1 = HALF * b + PACK * m0, HALF * b + PACK * m1
-            rows = wg_in[0][:, :, c0:c1] if c1 <= edge else wg_in[1][:, :, c0 - edge : c1 - edge]
+            if b == 0:
+                rows = wg_in[0][:, :, c0:c1]
+            elif c1 <= edge:
+                rows = wg_in[2][:, :, c0 - HALF : c1 - HALF]
+            else:
+                rows = wg_in[1][:, :, c0 - edge : c1 - edge]
             copy(
                 wg_bf[b][:, t0:t1, m0:m1, :].rearrange("p t m i -> p m i t"),
                 rows.rearrange("p i (m t) -> p m i t", t=PACK)[:, :, :, t0:t1],
@@ -244,22 +233,26 @@ def tile_list_silu_mix_res_kernel(
         made = []
 
         def silu(dst, bank):
-            if len(made) < BIAS_N:
+            if not made:
                 nc.scalar.activation(dst, bank, SILU, bias=zero[:])
             else:
                 nc.scalar.activation(dst, bank, SILU)
             made.append(dst)
 
-        def gate_chunk(b, c, tile):
+        def gate_tile(b, c, shape):
+            tile = keep.tile(shape, F32, name=f"gate{b}{c}")
+            return tile[:]
+
+        def gate_chunk(b, c):
             bank = take("gate").rearrange("p (t j) -> p t j", t=PACK)
             for t in range(PACK):
                 gate_pass(bank[:, t, :], b, t, CHUNK * c, CHUNK)
-            gate = tile.rearrange("p (j t) -> p j t", t=PACK)
+            gate = gate_tile(b, c, [P, CHUNK, PACK])
             silu(gate, bank.rearrange("p t j -> p j t"))
             gate_of[b, c] = gate.rearrange("p j (u e) -> p j u e", u=2)
 
         def gate_group(b, c):
-            gate = take("silu").rearrange("p (u j e) -> p u j e", u=2, e=2)
+            gate = gate_tile(b, c, [P, 2, GROUP, 2])
             for u in range(2):
                 bank = take("gate").rearrange("p (e j) -> p e j", e=2)
                 for e in range(2):
@@ -278,7 +271,7 @@ def tile_list_silu_mix_res_kernel(
             up_of[b, c] = bank.rearrange("p (u e) j -> p j u e", u=2)
 
         def place(n, b, j0):
-            if TAILC in (1, 2) and n == GROUPS - 1:
+            if n == GROUPS - 1:
                 return GROUP * (j0 // CHUNK) + CHUNK * b
             return GROUP * b + j0
 
@@ -290,6 +283,18 @@ def tile_list_silu_mix_res_kernel(
             nc.vector.tensor_tensor(
                 h_bf[n][:].rearrange("p b j t -> p (b j) t")[:, place(n, b, CHUNK * d) : place(n, b, CHUNK * d) + CHUNK, :].rearrange("p j (u e) -> p j u e", u=2),
                 up_of[b, c],
+                gate_of[b, c],
+                MULT,
+            )
+
+        def product_on_gpsimd(b, c):
+            n, d = divmod(c, 2)
+            up_sb = keep.tile([P, CHUNK, 2, 2], F32, name=f"up{b}{c}", align_bytes=ALIGN)
+            nc.scalar.copy(up_sb[:], up_of[b, c])
+            c0 = place(n, b, CHUNK * d)
+            nc.gpsimd.tensor_tensor(
+                h_bf[n][:].rearrange("p b j t -> p (b j) t")[:, c0 : c0 + CHUNK, :].rearrange("p j (u e) -> p j u e", u=2),
+                up_sb[:],
                 gate_of[b, c],
                 MULT,
             )
@@ -309,7 +314,7 @@ def tile_list_silu_mix_res_kernel(
             nc.tensor.matmul_mx(
                 out=dst,
                 lhsT=codes,
-                lhsT_scale=scales_in[:, N * b + P * a : N * b + P * (a + 1)],
+                lhsT_scale=wd_sc[:, N * b + P * a : N * b + P * (a + 1)],
                 rhs=h_codes[n][:].rearrange("p b j -> p (b j)")[:, place(n, b, j0) : place(n, b, j0) + width].bitcast(FP8X4),
                 rhs_scale=h_sc[n][:].rearrange("p b j -> p (b j)")[:, place(n, b, j0) : place(n, b, j0) + width],
                 start=start,
@@ -365,73 +370,54 @@ def tile_list_silu_mix_res_kernel(
                 if i == 1:
                     round_x(j0, HALF, 0)
         gather(2, 0, J)
-        if SCALAR_SHARE[0]:
-            round_wg(nc.scalar.copy, 0, 0, SCALAR_SHARE[0])
-        pieces = [(sum(LAST_PLANE_PIECES[:n]), LAST_PLANE_PIECES[n]) for n in range(len(LAST_PLANE_PIECES))]
-        left = list(QFIRST)
-        for j0, n in pieces:
+        j0 = 0
+        for n in LAST_PLANE_PIECES:
             gather(PACK - 1, j0, n)
             round_x(j0, n, 2)
-            while left and EARLY - sum(left) + left[0] <= j0 + n:
-                quant_x(EARLY - sum(left), left[0])
-                left.pop(0)
-        round_wg(nc.vector.tensor_copy, 0, 0, P)
-        round_wg(nc.vector.tensor_copy, 1, 0, VSHARE)
-        quant_wg(0)
+            if j0 < EARLY:
+                quant_x(j0, n)
+            j0 = j0 + n
+        for t0 in (0, 2):
+            round_wg(nc.vector.tensor_copy, 0, 0, P, t0, t0 + 2)
+        for t0 in (0, 2):
+            quant_wg(0, t0, t0 + 2)
         round_wg(nc.scalar.copy, 1, VSHARE, P)
         quant_x(GROUP, GROUP)
         quant_x(HALF, HALF)
+        round_wg(nc.vector.tensor_copy, 1, 0, VSHARE)
+        quant_wg(1)
 
-        products = [(b, 2 * n + d) for n in range(GROUPS) for b in range(2) for d in range(2)]
-        early = [(0, c) for c in range(FIRST)]
-        products = early + [u for u in products if u not in early]
         last = GROUPS - 1
-        if TAILC in (1, 2):
-            products = products[:-3] + [products[-2], products[-3], products[-1]]
-        quantise_at = {QUANT_AT[g]: g for g in range(last)}
-        quantise_steps = [(QUANT_AT[g], g) for g in range(last)]
-        to_add, to_copy, for_gpsimd, quantised = [], [], [], set()
-        tail_banks = []
-        for k in range(len(products) + 1):
-            if k < len(products):
-                b, c = products[k]
-                if k < HOLD:
-                    gate_chunk(b, c, first_gates[:, k])
-                elif k < CHUNKWISE or (TAILC in (1, 2) and k >= len(products) - 4) or (c % 2 == 1 and (b, c) not in gate_of):
-                    gate_chunk(b, c, take("silu")[:, 0:HALF])
-                elif c % 2 == 0:
-                    gate_group(b, c)
-                up(b, c, "out" if (b == 1 and c < PREFILL) or k in range(8, 8 + RING5) else "up")
-            if k >= 1:
-                product(*products[k - 1])
-            if Q2_AT and k == Q2_AT:
-                quant_x(GROUP, GROUP)
-            if Q34_AT and k == Q34_AT:
-                quant_x(HALF, HALF)
-            if QW1_AT and k == QW1_AT:
-                quant_wg(1)
-            if k in quantise_at:
-                quant_h(quantise_at[k], 0, 2 * GROUP)
-                quantised.add(quantise_at[k])
-            for u in range(2):
-                for g in [g for kq, g in quantise_steps if min(kq + DOWN_LAG[u], len(products)) == k]:
-                    while len(to_add) + len(to_copy) >= 2:
-                        if to_copy and (not to_add or to_copy[0][3] < to_add[0][2]):
-                            first = to_copy.pop(0)
-                            for_gpsimd.append((first[1], leave_psum(*first[2])))
+        waiting, to_add, tail_banks, ups = [], [], [], PREFILL
+        for k in range(len(ORDER) + 1):
+            for step, b, c, chunks in GATES:
+                if step == k:
+                    (gate_chunk if chunks == 1 else gate_group)(b, c)
+            if k == 0:
+                for m in range(PREFILL):
+                    up(*ORDER[m], "up" if m < UP_BANKS else "out")
+            if k + COPY_LEAD in ON_GPSIMD:
+                product_on_gpsimd(*ORDER[k + COPY_LEAD])
+            if k >= 1 and k - 1 not in ON_GPSIMD:
+                product(*ORDER[k - 1])
+            if k >= 1 and not UP_BANKS <= k - 1 < PREFILL and ups < len(ORDER):
+                up(*ORDER[ups], "up")
+                ups = ups + 1
+            for n in range(last):
+                if k == QUANT_AT[n]:
+                    quant_h(n, 0, 2 * GROUP)
+                    for held in [w for w in waiting if w[0] == n]:
+                        add_on_gpsimd(*held)
+                for u in range(2):
+                    if k == QUANT_AT[n] + DOWN_LAG[u]:
+                        bank = down_group(n, u)
+                        if (n, u) not in GB:
+                            to_add.append((k + ADD_LAG, bank))
+                        elif QUANT_AT[GB[n, u]] <= k:
+                            add_on_gpsimd(GB[n, u], *leave_psum(*bank))
                         else:
-                            add_on_vector(*to_add.pop(0)[1])
-                    if (g, u) in GB:
-                        to_copy.append((k + COPY_LAG, GB[g, u], down_group(g, u), 2 * g + u))
-                    else:
-                        to_add.append((k + ADD_LAG, down_group(g, u), 2 * g + u))
-            while to_copy and (to_copy[0][0] <= k or k == len(products)):
-                first = to_copy.pop(0)
-                for_gpsimd.append((first[1], leave_psum(*first[2])))
-            while for_gpsimd and for_gpsimd[0][0] in quantised:
-                first = for_gpsimd.pop(0)
-                add_on_gpsimd(first[0], *first[1])
-            if TAILC in (1, 2) and k == len(products) - 1:
+                            waiting.append((GB[n, u], *leave_psum(*bank)))
+            if k == len(ORDER) - 1:
                 quant_tail(0, 0, 2)
                 tail_banks.append(take("gate"))
                 for b in range(2):
@@ -439,37 +425,14 @@ def tile_list_silu_mix_res_kernel(
                 quant_tail(1, 0, 1)
                 tail_banks.append(take("gate"))
                 down_chunk(tail_banks[1], 0, last, 1)
-            while to_add and (to_add[0][0] <= k or k == len(products)) and not (TAILC >= 2 and to_add[0][2] == 5) and not (TAILC == 3 and to_add[0][2] == 4 and k < len(products)):
+            while len(to_add) > (1 if k > QUANT_AT[last - 1] else 0) and to_add[0][0] <= k:
                 add_on_vector(*to_add.pop(0)[1])
-            if not TAILC and k == len(products) - 1:
-                quant_h(last, 0, GROUP)
-                for d in range(2):
-                    tail_banks.append(take("gate"))
-                    down_chunk(tail_banks[d], 0, last, d)
-                quant_h(last, GROUP, CHUNK)
-                down_chunk(tail_banks[0], 1, last, 0)
-        if TAILC == 3:
-            quant_h(last, 0, 2 * GROUP)
-            ends = [down_group(last, u, "gate") for u in range(2)]
-            add_on_vector(*to_add.pop(0)[1], held=True)
-            add_on_vector(*ends[0])
-            if LASTSPLIT:
-                for e in range(2):
-                    add_on_vector(*[a[:, e : e + 1] for a in ends[1]])
-            else:
-                add_on_vector(*ends[1])
-        else:
-            if TAILC == 2:
-                add_on_vector(*operands(tail_banks[0], 0, 4, J - GROUP, CHUNK))
-            if TAILC:
-                quant_tail(1, 1, 1)
-            else:
-                quant_h(last, GROUP + CHUNK, CHUNK)
-            down_chunk(tail_banks[1], 1, last, 1)
-            if TAILC == 2:
-                add_on_vector(*to_add.pop(0)[1], held=True)
-            else:
-                add_on_vector(*operands(tail_banks[0], 0, 4, J - GROUP, CHUNK))
-            y, res_part, out_part = operands(tail_banks[1], 0, 4, J - CHUNK, CHUNK)
-            for a0 in (0, 2):
-                add_on_vector(y[:, a0 : a0 + 2], res_part[:, a0 : a0 + 2], out_part[:, a0 : a0 + 2])
+        while len(to_add) > 1:
+            add_on_vector(*to_add.pop(0)[1])
+        add_on_vector(*operands(tail_banks[0], 0, 4, J - GROUP, CHUNK))
+        quant_tail(1, 1, 1)
+        down_chunk(tail_banks[1], 1, last, 1)
+        add_on_vector(*to_add.pop(0)[1], held=True)
+        y, res_part, out_part = operands(tail_banks[1], 0, 4, J - CHUNK, CHUNK)
+        for a0 in (0, 2):
+            add_on_vector(y[:, a0 : a0 + 2], res_part[:, a0 : a0 + 2], out_part[:, a0 : a0 + 2])

@@ -31,10 +31,11 @@ HEAD = 16
 UP_BANKS, GATE_BANKS = 3, 3
 VSHARE = 32
 ORDER = ((0, 0), (0, 1), (0, 2), (1, 0), (1, 1), (0, 3), (1, 2), (1, 3), (0, 4), (0, 5), (1, 4), (1, 5), (0, 6), (1, 6), (0, 7), (1, 7))
-GATES = ((0, 0, 0, 1), (0, 0, 1, 1), (0, 0, 2, 1), (0, 1, 0, 1), (1, 1, 1, 1), (2, 0, 3, 1), (3, 1, 2, 2), (5, 0, 4, 2), (7, 1, 4, 2),
+GATES = ((0, 0, 0, 1), (0, 0, 1, 1), (0, 0, 2, 1), (0, 1, 0, 1), (1, 1, 1, 1), (2, 0, 3, 1), (3, 1, 2, 2), (5, 0, 4, 1), (6, 0, 5, 1), (7, 1, 4, 2),
          (9, 0, 6, 1), (10, 1, 6, 1), (11, 0, 7, 1), (12, 1, 7, 1))
 ON_GPSIMD = ()
 SCALES_BEHIND = 3
+HOLD = 3
 PREFILL = 5
 COPY_LEAD = -1
 QUANT_AT = (6, 9, 13)
@@ -67,9 +68,8 @@ def tile_list_silu_mix_res_kernel(
         wgt_sb = keep.tile([P, J], F32, name="wgt_sb", align_bytes=ALIGN)
         planes = [keep.tile([P, T], F32, name=f"plane{i}") for i in range(PACK)]
         edge = HALF + PACK * VSHARE
-        wg_in = [keep.tile([P, PACK, HALF], F32, name="wg_in0", align_bytes=ALIGN)]
+        wg_in = [keep.tile([P, PACK, edge], F32, name="wg_in0", align_bytes=ALIGN)]
         wg_in.append(keep.tile([P, PACK, R - edge], F32, name="wg_in1", align_bytes=ALIGN))
-        wg_in.append(keep.tile([P, PACK, edge - HALF], F32, name="wg_in2", align_bytes=ALIGN))
         wd8_sb = keep.tile([P, N], U32, name="wd8_sb", align_bytes=ALIGN)
         wd4_sb = keep.tile([P, 2 * N], U8, name="wd4_sb", align_bytes=ALIGN)
         res_sb = [keep.tile([P, N // P, HALF], F32, name=f"res{s}") for s in range(2)]
@@ -120,9 +120,8 @@ def tile_list_silu_mix_res_kernel(
             if i == SCALES_BEHIND:
                 nc.sync.dma_start(wd_sc[0:16, 0:N].bitcast(I32), wd8_scales[0].bitcast(I32))
                 nc.sync.dma_start(wd_sc[0:16, N:].bitcast(I32), wd4_scales[0].bitcast(I32))
-        nc.sync.dma_start(wg_in[0][:], wg_rows[:, :, 0:HALF])
+        nc.sync.dma_start(wg_in[0][:], wg_rows[:, :, 0:edge])
         nc.sync.dma_start(wg_in[1][:], wg_rows[:, :, edge:R])
-        nc.sync.dma_start(wg_in[2][:], wg_rows[:, :, HALF:edge])
         deal_scales(wd_sc, nc.sync)
         nc.sync.dma_start(wd8_sb[:].bitcast(I32), wd8_words[0].rearrange("p n t -> p (n t)").bitcast(I32))
         nc.sync.dma_start(wd4_sb[:].bitcast(I32), wd4_words[0].bitcast(I32))
@@ -155,6 +154,7 @@ def tile_list_silu_mix_res_kernel(
         ]
         h_codes = [keep.tile([P, 2, GROUP], U32, name=f"h_codes{n}", align_bytes=ALIGN) for n in range(GROUPS)]
         h_sc = [keep.tile([P, 2, GROUP], U8, name=f"h_sc{n}", align_bytes=ALIGN) for n in range(GROUPS)]
+        first_gates = keep.tile([P, 3, HALF], F32, name="first_gates", tag="wg_in1", align_bytes=ALIGN)
         banks = [psum.tile([P, HALF], F32, name=f"bank{k}") for k in range(8)]
 
 
@@ -195,12 +195,7 @@ def tile_list_silu_mix_res_kernel(
 
         def round_wg(copy, b, m0, m1, t0=0, t1=PACK):
             c0, c1 = HALF * b + PACK * m0, HALF * b + PACK * m1
-            if b == 0:
-                rows = wg_in[0][:, :, c0:c1]
-            elif c1 <= edge:
-                rows = wg_in[2][:, :, c0 - HALF : c1 - HALF]
-            else:
-                rows = wg_in[1][:, :, c0 - edge : c1 - edge]
+            rows = wg_in[0][:, :, c0:c1] if c1 <= edge else wg_in[1][:, :, c0 - edge : c1 - edge]
             copy(
                 wg_bf[b][:, t0:t1, m0:m1, :].rearrange("p t m i -> p m i t"),
                 rows.rearrange("p i (m t) -> p m i t", t=PACK)[:, :, :, t0:t1],
@@ -240,6 +235,8 @@ def tile_list_silu_mix_res_kernel(
             made.append(dst)
 
         def gate_tile(b, c, shape):
+            if (b, c) in ORDER[:HOLD]:
+                return first_gates[:, c].rearrange("p (j t) -> p j t", t=PACK)
             tile = keep.tile(shape, F32, name=f"gate{b}{c}")
             return tile[:]
 
@@ -358,7 +355,7 @@ def tile_list_silu_mix_res_kernel(
 
         def add_on_gpsimd(n, y, res_part, out_part):
             if n not in sums:
-                sums[n] = [keep.tile([P, 2, 2, GROUP], F32, name=f"result{n}", tag=f"stage{n}", align_bytes=ALIGN), 0]
+                sums[n] = [keep.tile([P, 2, 2, GROUP], F32, name=f"result{n}", tag="gate%d%d" % ORDER[QUANT_AT[n] - 1]), 0]
             result = sums[n][0][:, sums[n][1]]
             sums[n][1] = sums[n][1] + 1
             nc.gpsimd.tensor_tensor(result, y, res_part, ADD)
@@ -377,14 +374,12 @@ def tile_list_silu_mix_res_kernel(
             if j0 < EARLY:
                 quant_x(j0, n)
             j0 = j0 + n
-        for t0 in (0, 2):
-            round_wg(nc.vector.tensor_copy, 0, 0, P, t0, t0 + 2)
-        for t0 in (0, 2):
-            quant_wg(0, t0, t0 + 2)
+        round_wg(nc.vector.tensor_copy, 0, 0, P)
+        round_wg(nc.vector.tensor_copy, 1, 0, VSHARE)
+        quant_wg(0)
         round_wg(nc.scalar.copy, 1, VSHARE, P)
         quant_x(GROUP, GROUP)
         quant_x(HALF, HALF)
-        round_wg(nc.vector.tensor_copy, 1, 0, VSHARE)
         quant_wg(1)
 
         last = GROUPS - 1

@@ -16,6 +16,7 @@ FP4X4 = mybir.dt.float4_e2m1fn_x4
 MULT = mybir.AluOpType.mult
 ADD = mybir.AluOpType.add
 SILU = mybir.ActivationFunctionType.Silu
+IDENTITY = mybir.ActivationFunctionType.Identity
 
 P = 128
 PACK = 4
@@ -28,16 +29,19 @@ LAST_PLANE_PIECES = (128, 128, 256, 256, 256)
 EARLY = 256
 QUAD = 32
 HEAD = 16
-UP_BANKS, GATE_BANKS = 3, 3
+GATE_BANKS = 3
 VSHARE = 32
-ORDER = ((0, 0), (0, 1), (0, 2), (1, 0), (1, 1), (0, 3), (1, 2), (1, 3), (0, 4), (0, 5), (1, 4), (1, 5), (0, 6), (1, 6), (0, 7), (1, 7))
-GATES = ((0, 0, 0, 1), (0, 0, 1, 1), (0, 0, 2, 1), (0, 1, 0, 1), (1, 1, 1, 1), (2, 0, 3, 1), (3, 1, 2, 2), (5, 0, 4, 1), (6, 0, 5, 1), (7, 1, 4, 2),
-         (9, 0, 6, 1), (10, 1, 6, 1), (11, 0, 7, 1), (12, 1, 7, 1))
+ORDER = ((0, 0), (0, 1), (0, 2), (1, 0), (1, 1), (0, 3), (1, 2), (1, 3), (0, 4), (0, 5), (1, 4), (1, 5), (0, 6), (0, 7), (1, 6), (1, 7))
+GATES = ((0, 0, 0, 1), (0, 0, 1, 1), (0, 0, 2, 1), (0, 1, 0, 1), (1, 1, 1, 1), (2, 0, 3, 1), (3, 1, 2, 2), (5, 0, 4, 2),
+         (7, 1, 4, 2), (9, 0, 6, 2), (11, 1, 6, 1), (12, 1, 7, 1))
 ON_GPSIMD = ()
 SCALES_BEHIND = 3
+EARLY_RELEASE = (0, 0, 0)
 HOLD = 3
-PREFILL = 5
-COPY_LEAD = -1
+LEAD = 5
+LEAST = 3
+RETURN = 3
+SHARE = 1
 QUANT_AT = (6, 9, 13)
 DOWN_LAG = (0, 1)
 ADD_LAG = 2
@@ -50,7 +54,7 @@ def tile_list_silu_mix_res_kernel(
     nc = tc.nc
     with ExitStack() as ctx:
         keep = ctx.enter_context(tc.tile_pool(name="keep", bufs=1))
-        ring = ctx.enter_context(tc.tile_pool(name="ring", bufs=4))
+        ring = ctx.enter_context(tc.tile_pool(name="ring", bufs=6))
         psum = ctx.enter_context(tc.psum_pool(name="psum", bufs=1))
 
         offsets = keep.tile([P, J // 16], U16, name="offsets")
@@ -152,16 +156,14 @@ def tile_list_silu_mix_res_kernel(
             keep.tile([P, 2, GROUP, PACK], BF16, name=f"h_bf{n}", tag=f"stage{n}", align_bytes=ALIGN)
             for n in range(GROUPS)
         ]
-        h_codes = [keep.tile([P, 2, GROUP], U32, name=f"h_codes{n}", align_bytes=ALIGN) for n in range(GROUPS)]
+        h_codes = [keep.tile([P, 2, GROUP], U32, name=f"h_codes{n}", align_bytes=ALIGN) for n in range(GROUPS - 1)]
         h_sc = [keep.tile([P, 2, GROUP], U8, name=f"h_sc{n}", align_bytes=ALIGN) for n in range(GROUPS)]
-        first_gates = keep.tile([P, 3, HALF], F32, name="first_gates", tag="wg_in1", align_bytes=ALIGN)
+        zero_late = keep.tile([P, 1], F32, name="zero_late")
         banks = [psum.tile([P, HALF], F32, name=f"bank{k}") for k in range(8)]
 
 
         rings = {
-            "up": banks[:UP_BANKS],
-            "gate": banks[UP_BANKS : UP_BANKS + GATE_BANKS],
-            "out": banks[UP_BANKS + GATE_BANKS :],
+            "gate": banks[:GATE_BANKS],
         }
 
         def take(name):
@@ -228,16 +230,14 @@ def tile_list_silu_mix_res_kernel(
         made = []
 
         def silu(dst, bank):
-            if not made:
-                nc.scalar.activation(dst, bank, SILU, bias=zero[:])
+            if len(made) < HOLD:
+                nc.scalar.activation(dst, bank, SILU, bias=zero_late[:])
             else:
                 nc.scalar.activation(dst, bank, SILU)
             made.append(dst)
 
         def gate_tile(b, c, shape):
-            if (b, c) in ORDER[:HOLD]:
-                return first_gates[:, c].rearrange("p (j t) -> p j t", t=PACK)
-            tile = keep.tile(shape, F32, name=f"gate{b}{c}")
+            tile = keep.tile(shape, F32, name=f"gate{b}{c}", align_bytes=ALIGN)
             return tile[:]
 
         def gate_chunk(b, c):
@@ -258,8 +258,8 @@ def tile_list_silu_mix_res_kernel(
             for d in range(2):
                 gate_of[b, c + d] = gate[:, :, CHUNK * d : CHUNK * (d + 1), :].rearrange("p u j e -> p j u e")
 
-        def up(b, c, ring_name):
-            bank = take(ring_name).rearrange("p (t j) -> p t j", t=PACK)
+        def up(b, c, whole):
+            bank = whole.rearrange("p (t j) -> p t j", t=PACK)
             for t in range(PACK):
                 c0 = HALF * b + P * t
                 first_stage(
@@ -268,12 +268,7 @@ def tile_list_silu_mix_res_kernel(
             up_of[b, c] = bank.rearrange("p (u e) j -> p j u e", u=2)
 
         def place(n, b, j0):
-            if n == GROUPS - 1:
-                return GROUP * (j0 // CHUNK) + CHUNK * b
             return GROUP * b + j0
-
-        def quant_tail(d, b0, nb):
-            quant_h(GROUPS - 1, GROUP * d + CHUNK * b0, CHUNK * nb)
 
         def product(b, c):
             n, d = divmod(c, 2)
@@ -323,8 +318,7 @@ def tile_list_silu_mix_res_kernel(
             y = bank.rearrange("p (a j) -> p a j", j=width)
             return y, res_sb[s][:, a0:a1, c : c + width], out_rows[:, a0:a1, j0 : j0 + width]
 
-        def down_group(n, u, ring_name="out"):
-            bank = take(ring_name)
+        def down_group(n, u, bank):
             for e in range(2):
                 c0 = GROUP * e
                 down_pass(bank[:, c0 : c0 + GROUP], 2 * u + e, 0, n, 0, GROUP, True, False)
@@ -333,10 +327,12 @@ def tile_list_silu_mix_res_kernel(
                     down_pass(dst, 2 * u + e, 1, n, CHUNK * d, CHUNK, False, d == 1)
             return operands(bank, 2 * u, 2 * u + 2, GROUP * n, GROUP)
 
-        def down_chunk(bank, b, n, d):
-            for a in range(N // P):
-                first, last = (b, a) == (0, 0), (b, a) == (1, N // P - 1)
-                down_pass(bank[:, CHUNK * a : CHUNK * (a + 1)], a, b, n, CHUNK * d, CHUNK, first, last)
+        def down_half(bank, u, b, n):
+            width = CHUNK if b else GROUP
+            for e in range(2):
+                for j0 in range(0, GROUP, width):
+                    c0 = GROUP * e + j0
+                    down_pass(bank[:, c0 : c0 + width], 2 * u + e, b, n, j0, width, b == 0 and c0 == 0, c0 + width == HALF and b == 1)
 
         def add_on_vector(y, res_part, out_part, held=False):
             if held:
@@ -355,7 +351,7 @@ def tile_list_silu_mix_res_kernel(
 
         def add_on_gpsimd(n, y, res_part, out_part):
             if n not in sums:
-                sums[n] = [keep.tile([P, 2, 2, GROUP], F32, name=f"result{n}", tag="gate%d%d" % ORDER[QUANT_AT[n] - 1]), 0]
+                sums[n] = [keep.tile([P, 2, 2, GROUP], F32, name=f"result{n}", tag="gate%d%d" % ORDER[QUANT_AT[n] - 1], align_bytes=ALIGN) if EARLY_RELEASE[n] else keep.tile([P, 2, 2, GROUP], F32, name=f"result{n}", tag=f"stage{n}", align_bytes=ALIGN), 0]
             result = sums[n][0][:, sums[n][1]]
             sums[n][1] = sums[n][1] + 1
             nc.gpsimd.tensor_tensor(result, y, res_part, ADD)
@@ -377,57 +373,61 @@ def tile_list_silu_mix_res_kernel(
         round_wg(nc.vector.tensor_copy, 0, 0, P)
         round_wg(nc.vector.tensor_copy, 1, 0, VSHARE)
         quant_wg(0)
+        nc.scalar.activation(zero_late[:], wg_in[1][:, 0, 0:1], IDENTITY, bias=zero[:], scale=0.0)
         round_wg(nc.scalar.copy, 1, VSHARE, P)
         quant_x(GROUP, GROUP)
         quant_x(HALF, HALF)
         quant_wg(1)
 
         last = GROUPS - 1
-        waiting, to_add, tail_banks, ups = [], [], [], PREFILL
+        waiting, to_add, tail_banks = [], [], []
+        free = [(0, bank[:]) for bank in banks[GATE_BANKS:]]
+        bank_of, downs, ups = {}, [], 0
         for k in range(len(ORDER) + 1):
             for step, b, c, chunks in GATES:
                 if step == k:
                     (gate_chunk if chunks == 1 else gate_group)(b, c)
-            if k == 0:
-                for m in range(PREFILL):
-                    up(*ORDER[m], "up" if m < UP_BANKS else "out")
-            if k + COPY_LEAD in ON_GPSIMD:
-                product_on_gpsimd(*ORDER[k + COPY_LEAD])
-            if k >= 1 and k - 1 not in ON_GPSIMD:
+            if k >= 1:
                 product(*ORDER[k - 1])
-            if k >= 1 and not UP_BANKS <= k - 1 < PREFILL and ups < len(ORDER):
-                up(*ORDER[ups], "up")
-                ups = ups + 1
+                free.append((k, bank_of[k - 1]))
             for n in range(last):
                 if k == QUANT_AT[n]:
                     quant_h(n, 0, 2 * GROUP)
                     for held in [w for w in waiting if w[0] == n]:
                         add_on_gpsimd(*held)
-                for u in range(2):
-                    if k == QUANT_AT[n] + DOWN_LAG[u]:
-                        bank = down_group(n, u)
-                        if (n, u) not in GB:
-                            to_add.append((k + ADD_LAG, bank))
-                        elif QUANT_AT[GB[n, u]] <= k:
-                            add_on_gpsimd(GB[n, u], *leave_psum(*bank))
-                        else:
-                            waiting.append((GB[n, u], *leave_psum(*bank)))
-            if k == len(ORDER) - 1:
-                quant_tail(0, 0, 2)
-                tail_banks.append(take("gate"))
-                for b in range(2):
-                    down_chunk(tail_banks[0], b, last, 0)
-                quant_tail(1, 0, 1)
-                tail_banks.append(take("gate"))
-                down_chunk(tail_banks[1], 0, last, 1)
-            while len(to_add) > (1 if k > QUANT_AT[last - 1] else 0) and to_add[0][0] <= k:
+                downs.extend((n, u) for u in range(2) if k == QUANT_AT[n] + DOWN_LAG[u])
+            free.sort(key=lambda f: f[0])
+            while free and free[0][0] <= k and (downs or ups < min(len(ORDER), k + LEAD)):
+                bank = free.pop(0)[1]
+                if downs and ups >= min(len(ORDER), k + LEAST):
+                    n, u = downs.pop(0)
+                    sums_in = down_group(n, u, bank)
+                    if (n, u) not in GB:
+                        to_add.append((k + ADD_LAG, sums_in, bank))
+                        continue
+                    if QUANT_AT[GB[n, u]] <= k:
+                        add_on_gpsimd(GB[n, u], *leave_psum(*sums_in))
+                    else:
+                        waiting.append((GB[n, u], *leave_psum(*sums_in)))
+                    free.append((k + RETURN, bank))
+                else:
+                    up(*ORDER[ups], bank)
+                    bank_of[ups] = bank
+                    ups = ups + 1
+            while to_add and to_add[0][0] <= k and k <= QUANT_AT[last - 1]:
+                free.append((k + 1, to_add[0][2]))
                 add_on_vector(*to_add.pop(0)[1])
-        while len(to_add) > 1:
-            add_on_vector(*to_add.pop(0)[1])
-        add_on_vector(*operands(tail_banks[0], 0, 4, J - GROUP, CHUNK))
-        quant_tail(1, 1, 1)
-        down_chunk(tail_banks[1], 1, last, 1)
-        add_on_vector(*to_add.pop(0)[1], held=True)
-        y, res_part, out_part = operands(tail_banks[1], 0, 4, J - CHUNK, CHUNK)
-        for a0 in (0, 2):
-            add_on_vector(y[:, a0 : a0 + 2], res_part[:, a0 : a0 + 2], out_part[:, a0 : a0 + 2])
+        spare = [take("gate") for u in range(GATE_BANKS)] + [bank for step, bank in free]
+        ends = [spare[a // SHARE][:, GROUP * (a % SHARE) : GROUP * (a % SHARE + 1)] for a in range(N // P)]
+        h_codes.append(keep.tile([P, 2, GROUP], U32, name="h_codes_last", tag="gate%d%d" % ORDER[-2], align_bytes=ALIGN))
+        quant_h(last, 0, GROUP)
+        quant_h(last, GROUP, GROUP)
+        for a in range(N // P):
+            down_pass(ends[a], a, 0, last, 0, GROUP, a % SHARE == 0, False)
+        for a in range(N // P):
+            for d in range(2):
+                down_pass(ends[a][:, CHUNK * d : CHUNK * (d + 1)], a, 1, last, CHUNK * d, CHUNK, False, d == 1 and a % SHARE == SHARE - 1)
+        for step, sums_in, bank in to_add:
+            add_on_vector(*sums_in)
+        for a in range(N // P):
+            add_on_vector(*operands(ends[a], a, a + 1, J - GROUP, GROUP))

@@ -25,27 +25,18 @@ CHUNK = 128
 GROUP = 2 * CHUNK
 GROUPS = J // GROUP
 ALIGN = 256
-LAST_PLANE_PIECES = (128, 128, 256, 256, 256)
-EARLY = 256
 QUAD = 32
 HEAD = 16
+BLOCKS = N // P
+LAST_PLANE_PIECES = (CHUNK, CHUNK, GROUP, GROUP, GROUP)
+VECTOR_SHARE = 48
 GATE_BANKS = 3
-VSHARE = 32
-ORDER = ((0, 0), (0, 1), (0, 2), (1, 0), (1, 1), (0, 3), (1, 2), (1, 3), (0, 4), (0, 5), (1, 4), (1, 5), (0, 6), (0, 7), (1, 6), (1, 7))
-GATES = ((0, 0, 0, 1), (0, 0, 1, 1), (0, 0, 2, 1), (0, 1, 0, 1), (1, 1, 1, 1), (2, 0, 3, 1), (3, 1, 2, 2), (5, 0, 4, 2),
-         (7, 1, 4, 2), (9, 0, 6, 2), (11, 1, 6, 1), (12, 1, 7, 1))
-ON_GPSIMD = ()
-SCALES_BEHIND = 3
-EARLY_RELEASE = (0, 0, 0)
-HOLD = 3
-LEAD = 5
-LEAST = 3
-RETURN = 3
-SHARE = 1
-QUANT_AT = (6, 9, 13)
-DOWN_LAG = (0, 1)
-ADD_LAG = 2
-GB = {(0, 0): 1, (0, 1): 1, (1, 1): 2}
+AHEAD = 3
+SINGLES = 6
+COPIED_AFTER = 3
+ADDED_AFTER = 2
+RESULT_TILES = 6
+ON_GPSIMD = {(0, 0): 1, (0, 1): 1, (1, 1): 2}
 
 
 def tile_list_silu_mix_res_kernel(
@@ -54,46 +45,48 @@ def tile_list_silu_mix_res_kernel(
     nc = tc.nc
     with ExitStack() as ctx:
         keep = ctx.enter_context(tc.tile_pool(name="keep", bufs=1))
-        ring = ctx.enter_context(tc.tile_pool(name="ring", bufs=6))
+        ring = ctx.enter_context(tc.tile_pool(name="ring", bufs=RESULT_TILES))
         psum = ctx.enter_context(tc.psum_pool(name="psum", bufs=1))
-
-        offsets = keep.tile([P, J // 16], U16, name="offsets")
 
         scales_in = keep.tile([P, R], U8, name="scales_in", align_bytes=ALIGN)
         nc.vector.memset(scales_in[:].bitcast(I32), 0)
         zero_in = keep.tile([P, 1], F32, name="zero_in")
         nc.vector.memset(zero_in[:], 0.0)
         zero = keep.tile([P, 1], F32, name="zero")
-        wu_tile = keep.tile([P, R], U8, name="wu_sc", align_bytes=ALIGN)
-        wu_sc = wu_tile[:]
-        wd_sc = scales_in[:]
+        first_bias = keep.tile([P, 1], F32, name="first_bias")
 
+        offsets = keep.tile([P, J // HEAD], U16, name="offsets")
         wu_in = keep.tile([P, 2 * R], U8, name="wu_in", align_bytes=ALIGN)
+        wu_codes = keep.tile([P, 2 * R], U8, name="wu_codes", align_bytes=ALIGN)
+        wu_sc = keep.tile([P, R], U8, name="wu_sc", align_bytes=ALIGN)
+        wgt_in = keep.tile([P, 2 * QUAD], F32, name="wgt_in", align_bytes=ALIGN)
+        wgt_turned = keep.tile([P, 2, 2, HEAD], F32, name="wgt_turned", align_bytes=ALIGN)
+        wgt_wide = keep.tile([P, HEAD, 2, 2, HEAD], F32, name="wgt_wide", align_bytes=ALIGN)
         wgt_sb = keep.tile([P, J], F32, name="wgt_sb", align_bytes=ALIGN)
         planes = [keep.tile([P, T], F32, name=f"plane{i}") for i in range(PACK)]
-        edge = HALF + PACK * VSHARE
-        wg_in = [keep.tile([P, PACK, edge], F32, name="wg_in0", align_bytes=ALIGN)]
-        wg_in.append(keep.tile([P, PACK, R - edge], F32, name="wg_in1", align_bytes=ALIGN))
+        edge = HALF + PACK * VECTOR_SHARE
+        wg_vector = keep.tile([P, PACK, edge], F32, name="wg_vector", align_bytes=ALIGN)
+        wg_scalar = keep.tile([P, PACK, R - edge], F32, name="wg_scalar", align_bytes=ALIGN)
         wd8_sb = keep.tile([P, N], U32, name="wd8_sb", align_bytes=ALIGN)
         wd4_sb = keep.tile([P, 2 * N], U8, name="wd4_sb", align_bytes=ALIGN)
-        res_sb = [keep.tile([P, N // P, HALF], F32, name=f"res{s}") for s in range(2)]
+        res_sb = [keep.tile([P, BLOCKS, HALF], F32, name=f"res{s}") for s in range(2)]
         x_rows = xT.rearrange("(p i) t -> i p t", i=PACK)
         wg_rows = wg.rearrange("(p i) r -> p i r", i=PACK)
         res_rows = res.rearrange("(a p) j -> p a j", p=P)
         out_rows = out.rearrange("(a p) j -> p a j", p=P)
-        wgt_in = keep.tile([P, 2 * QUAD], F32, name="wgt_in", align_bytes=ALIGN)
-        wgt_turned = keep.tile([P, 2, 2, HEAD], F32, name="wgt_turned", align_bytes=ALIGN)
-        wgt_wide = keep.tile([P, HEAD, 2, 2, HEAD], F32, name="wgt_wide", align_bytes=ALIGN)
-        wu_codes = keep.tile([P, 2 * R], U8, name="wu_codes", align_bytes=ALIGN)
-        head_rows = wgt.rearrange("(g c) (a s) -> c g a s", c=HEAD, a=HEAD)[0]
-        nc.sync.dma_start(wgt_in[:], head_rows)
+
+        def deal_scales(plane, queue):
+            for q in range(1, P // QUAD):
+                queue.dma_start(plane[QUAD * q : QUAD * q + 4, :].bitcast(I32), plane[4 * q : 4 * q + 4, :].bitcast(I32))
+
+        nc.sync.dma_start(wgt_in[:], wgt.rearrange("(g c) (a s) -> c g a s", c=HEAD, a=HEAD)[0])
         nc.sync.dma_start(wu_in[:].bitcast(I32), wu_words[0].bitcast(I32))
-        nc.sync.dma_start(scales_in[0:16, :].bitcast(I32), wu_scales[0].bitcast(I32))
+        nc.sync.dma_start(scales_in[0:HEAD, :].bitcast(I32), wu_scales[0].bitcast(I32))
         nc.scalar.activation(zero[:], zero_in[:], SILU)
         for u in range(2):
             nc.vector.transpose(wgt_turned[:, u].rearrange("p h a -> p (h a)"), wgt_in[:, QUAD * u : QUAD * (u + 1)])
         nc.vector.tensor_copy(
-            wu_sc.rearrange("p (b t m) -> p b t m", b=2, t=PACK),
+            wu_sc[:].rearrange("p (b t m) -> p b t m", b=2, t=PACK),
             scales_in[:].rearrange("p (b m t) -> p b t m", b=2, t=PACK),
         )
         nc.vector.tensor_copy(
@@ -101,82 +94,67 @@ def tile_list_silu_mix_res_kernel(
             wu_in[:].bitcast(U16).rearrange("p (b m t) -> p b t m", b=2, t=PACK),
         )
         for s in range(2):
-            part = slice(8 * s, 8 * (s + 1))
+            part = slice(HEAD // 2 * s, HEAD // 2 * (s + 1))
             nc.scalar.copy(
                 wgt_wide[:, part].rearrange("p a u h c -> p a (u h) c"),
-                wgt_turned[:, :, :, part].rearrange("p u h a -> p a (u h)").unsqueeze(3).to_broadcast([P, 8, 4, HEAD]),
+                wgt_turned[:, :, :, part].rearrange("p u h a -> p a (u h)").unsqueeze(3).to_broadcast([P, HEAD // 2, 4, HEAD]),
             )
             nc.vector.transpose(
                 wgt_sb[:, HALF * s : HALF * (s + 1)], wgt_wide[:, part].rearrange("p a u h c -> p (a u h c)")
             )
-        def deal_scales(plane, queue):
-            for q in range(1, 4):
-                queue.dma_start(
-                    plane[QUAD * q : QUAD * q + 4, :].bitcast(I32), plane[4 * q : 4 * q + 4, :].bitcast(I32)
-                )
 
         for i in range(PACK):
             nc.sync.dma_start(planes[i][:], x_rows[i])
             if i == 0:
                 nc.sync.dma_start(offsets[:], offs)
-            if i == 2:
+            if i == PACK - 2:
                 deal_scales(wu_sc, nc.scalar)
-            if i == SCALES_BEHIND:
-                nc.sync.dma_start(wd_sc[0:16, 0:N].bitcast(I32), wd8_scales[0].bitcast(I32))
-                nc.sync.dma_start(wd_sc[0:16, N:].bitcast(I32), wd4_scales[0].bitcast(I32))
-        nc.sync.dma_start(wg_in[0][:], wg_rows[:, :, 0:edge])
-        nc.sync.dma_start(wg_in[1][:], wg_rows[:, :, edge:R])
-        deal_scales(wd_sc, nc.sync)
+        nc.sync.dma_start(wg_vector[:], wg_rows[:, :, 0:edge])
+        nc.sync.dma_start(wg_scalar[:], wg_rows[:, :, edge:R])
+        nc.sync.dma_start(scales_in[0:HEAD, 0:N].bitcast(I32), wd8_scales[0].bitcast(I32))
+        nc.sync.dma_start(scales_in[0:HEAD, N:].bitcast(I32), wd4_scales[0].bitcast(I32))
         nc.sync.dma_start(wd8_sb[:].bitcast(I32), wd8_words[0].rearrange("p n t -> p (n t)").bitcast(I32))
         nc.sync.dma_start(wd4_sb[:].bitcast(I32), wd4_words[0].bitcast(I32))
-        nc.sync.dma_start(res_sb[0][:], res_rows[:, :, 0:HALF])
+        deal_scales(scales_in, nc.sync)
+        for a0 in (0, 2):
+            nc.sync.dma_start(res_sb[0][:, a0 : a0 + 2], res_rows[:, a0 : a0 + 2, 0:HALF])
         nc.sync.dma_start(res_sb[1][:], res_rows[:, :, HALF:J])
 
         picked_flat = keep.tile([P, PACK * J], F32, name="picked", align_bytes=ALIGN)
         picked = picked_flat[:].rearrange("p (i j) -> p i j", i=PACK)
-        xg_bf = keep.tile([P, J, PACK], BF16, name="xg_bf", align_bytes=ALIGN)
+        xg_bf = keep.tile([P, J - CHUNK, PACK], BF16, name="xg_bf", align_bytes=ALIGN)
         xg_first = picked_flat[:, PACK * J - GROUP :].bitcast(BF16).rearrange("p (j i) -> p j i", i=PACK)
-        wg_bf = [
-            keep.tile([P, PACK, P, PACK], BF16, name=f"wg_bf{b}", align_bytes=ALIGN)
-            for b in range(2)
-        ]
+        wg_bf = [keep.tile([P, PACK, P, PACK], BF16, name=f"wg_bf{b}", align_bytes=ALIGN) for b in range(2)]
         wg_codes = [keep.tile([P, HALF], U32, name=f"wg_codes{b}", align_bytes=ALIGN) for b in range(2)]
         wg_sc = [keep.tile([P, HALF], U8, name=f"wg_sc{b}", align_bytes=ALIGN) for b in range(2)]
-        codes_early = keep.tile([P, EARLY], U32, name="codes_early", align_bytes=ALIGN)
-        codes_late = keep.tile([P, J - EARLY], U32, name="codes_late", tag="wg_in0", align_bytes=ALIGN)
+        codes_early = keep.tile([P, GROUP], U32, name="codes_early", align_bytes=ALIGN)
+        codes_late = keep.tile([P, J - GROUP], U32, name="codes_late", tag="wg_vector", align_bytes=ALIGN)
         xg_sc = keep.tile([P, J], U8, name="xg_sc", align_bytes=ALIGN)
-
-        def xg_codes(j0, n):
-            return (codes_early[:, j0 : j0 + n] if j0 < EARLY else codes_late[:, j0 - EARLY : j0 - EARLY + n]).bitcast(FP8X4)
-
-        def rounded(j0, n):
-            return xg_first[:, j0 : j0 + n] if j0 < CHUNK else xg_bf[:, j0 : j0 + n]
-
-        h_bf = [
-            keep.tile([P, 2, GROUP, PACK], BF16, name=f"h_bf{n}", tag=f"stage{n}", align_bytes=ALIGN)
-            for n in range(GROUPS)
-        ]
-        h_codes = [keep.tile([P, 2, GROUP], U32, name=f"h_codes{n}", align_bytes=ALIGN) for n in range(GROUPS - 1)]
-        h_sc = [keep.tile([P, 2, GROUP], U8, name=f"h_sc{n}", align_bytes=ALIGN) for n in range(GROUPS)]
-        zero_late = keep.tile([P, 1], F32, name="zero_late")
+        h_bf = [keep.tile([P, 2 * GROUP, PACK], BF16, name=f"h_bf{n}", align_bytes=ALIGN) for n in range(GROUPS)]
+        h_codes = [keep.tile([P, 2 * GROUP], U32, name=f"h_codes{n}", align_bytes=ALIGN) for n in range(GROUPS - 1)]
+        h_sc = [keep.tile([P, 2 * GROUP], U8, name=f"h_sc{n}", align_bytes=ALIGN) for n in range(GROUPS)]
         banks = [psum.tile([P, HALF], F32, name=f"bank{k}") for k in range(8)]
+        gate_banks = [bank[:] for bank in banks[:GATE_BANKS]]
 
-
-        rings = {
-            "gate": banks[:GATE_BANKS],
-        }
-
-        def take(name):
-            rings[name] = rings[name][1:] + rings[name][:1]
-            return rings[name][-1][:]
+        order = [(b, 2 * n + d) for n in range(GROUPS) for b in range(2) for d in range(2)]
+        order.insert(2, order.pop(order.index((0, 2))))
+        last = GROUPS - 1
+        quantised_at = [order.index((1, 2 * n + 1)) + 2 for n in range(last)]
 
         def gather(i, j0, n):
             nc.vector.tensor_tensor(
                 picked[:, i, j0 : j0 + n],
-                planes[i][:].indirect(offsets[:, j0 // 16 : (j0 + n) // 16]),
+                planes[i][:].indirect(offsets[:, j0 // HEAD : (j0 + n) // HEAD]),
                 wgt_sb[:, j0 : j0 + n],
                 MULT,
             )
+
+        def rounded(j0, n):
+            return xg_first[:, j0 : j0 + n] if j0 < CHUNK else xg_bf[:, j0 - CHUNK : j0 - CHUNK + n]
+
+        def xg_codes(j0, n):
+            codes = codes_early[:, j0 : j0 + n] if j0 < GROUP else codes_late[:, j0 - GROUP : j0 - GROUP + n]
+            return codes.bitcast(FP8X4)
 
         def round_x(j0, n, i0):
             if j0 < CHUNK < j0 + n:
@@ -190,24 +168,18 @@ def tile_list_silu_mix_res_kernel(
 
         def quant_x(j0, n):
             nc.vector.quantize_mx(
-                out=xg_codes(j0, n),
-                scales=xg_sc[:, j0 : j0 + n],
-                in_=rounded(j0, n).rearrange("p j i -> p (j i)"),
+                out=xg_codes(j0, n), scales=xg_sc[:, j0 : j0 + n], in_=rounded(j0, n).rearrange("p j i -> p (j i)")
             )
 
-        def round_wg(copy, b, m0, m1, t0=0, t1=PACK):
-            c0, c1 = HALF * b + PACK * m0, HALF * b + PACK * m1
-            rows = wg_in[0][:, :, c0:c1] if c1 <= edge else wg_in[1][:, :, c0 - edge : c1 - edge]
+        def round_wg(copy, b, m0, m1, rows):
             copy(
-                wg_bf[b][:, t0:t1, m0:m1, :].rearrange("p t m i -> p m i t"),
-                rows.rearrange("p i (m t) -> p m i t", t=PACK)[:, :, :, t0:t1],
+                wg_bf[b][:, :, m0:m1, :].rearrange("p t m i -> p m i t"),
+                rows.rearrange("p i (m t) -> p m i t", t=PACK),
             )
 
-        def quant_wg(b, t0=0, t1=PACK):
+        def quant_wg(b):
             nc.vector.quantize_mx(
-                out=wg_codes[b][:, P * t0 : P * t1].bitcast(FP8X4),
-                scales=wg_sc[b][:, P * t0 : P * t1],
-                in_=wg_bf[b][:, t0:t1].rearrange("p t m i -> p (t m i)"),
+                out=wg_codes[b][:].bitcast(FP8X4), scales=wg_sc[b][:], in_=wg_bf[b][:].rearrange("p t m i -> p (t m i)")
             )
 
         def first_stage(dst, codes, scales, j0, n):
@@ -221,141 +193,124 @@ def tile_list_silu_mix_res_kernel(
                 stop=True,
             )
 
-        def gate_pass(dst, b, t, j0, n):
-            cols = slice(P * t, P * (t + 1))
-            first_stage(dst, wg_codes[b][:, cols].bitcast(FP8X4), wg_sc[b][:, cols], j0, n)
+        def gate_sums(b, t0, results, j0, n):
+            gate_banks.append(gate_banks.pop(0))
+            bank = gate_banks[-1].rearrange("p (t j) -> p t j", t=results)
+            for e in range(results):
+                cols = slice(P * (t0 + e), P * (t0 + e + 1))
+                first_stage(bank[:, e, :], wg_codes[b][:, cols].bitcast(FP8X4), wg_sc[b][:, cols], j0, n)
+            return bank.rearrange("p t j -> p j t")
 
         gate_of, up_of = {}, {}
 
-        made = []
-
-        def silu(dst, bank):
-            if len(made) < HOLD:
-                nc.scalar.activation(dst, bank, SILU, bias=zero_late[:])
-            else:
-                nc.scalar.activation(dst, bank, SILU)
-            made.append(dst)
+        def gate_tag(b, c):
+            return f"gate{b}{c}"
 
         def gate_tile(b, c, shape):
-            tile = keep.tile(shape, F32, name=f"gate{b}{c}", align_bytes=ALIGN)
+            tile = keep.tile(shape, F32, name=gate_tag(b, c), align_bytes=ALIGN)
             return tile[:]
 
-        def gate_chunk(b, c):
-            bank = take("gate").rearrange("p (t j) -> p t j", t=PACK)
-            for t in range(PACK):
-                gate_pass(bank[:, t, :], b, t, CHUNK * c, CHUNK)
+        def gate_single(b, c):
+            sums = gate_sums(b, 0, PACK, CHUNK * c, CHUNK)
             gate = gate_tile(b, c, [P, CHUNK, PACK])
-            silu(gate, bank.rearrange("p t j -> p j t"))
+            if len(gate_of) < GATE_BANKS:
+                nc.scalar.activation(gate, sums, SILU, bias=first_bias[:])
+            else:
+                nc.scalar.activation(gate, sums, SILU)
             gate_of[b, c] = gate.rearrange("p j (u e) -> p j u e", u=2)
 
-        def gate_group(b, c):
-            gate = gate_tile(b, c, [P, 2, GROUP, 2])
+        def gate_pair(b, c, tiles):
+            width = GROUP // tiles
+            gates = [gate_tile(b, c + d, [P, 2, width, 2]) for d in range(tiles)]
             for u in range(2):
-                bank = take("gate").rearrange("p (e j) -> p e j", e=2)
-                for e in range(2):
-                    gate_pass(bank[:, e, :], b, 2 * u + e, CHUNK * c, GROUP)
-                silu(gate[:, u, :, :], bank.rearrange("p e j -> p j e"))
+                sums = gate_sums(b, 2 * u, 2, CHUNK * c, GROUP)
+                for d in range(tiles):
+                    nc.scalar.activation(gates[d][:, u], sums[:, width * d : width * (d + 1)], SILU)
             for d in range(2):
-                gate_of[b, c + d] = gate[:, :, CHUNK * d : CHUNK * (d + 1), :].rearrange("p u j e -> p j u e")
+                tile, j0 = divmod(CHUNK * d, width)
+                gate_of[b, c + d] = gates[tile][:, :, j0 : j0 + CHUNK, :].rearrange("p u j e -> p j u e")
 
-        def up(b, c, whole):
-            bank = whole.rearrange("p (t j) -> p t j", t=PACK)
+        def gate_for(m):
+            b, c = order[m]
+            if (b, c) in gate_of:
+                return
+            if m < SINGLES or m >= len(order) - 2:
+                gate_single(b, c)
+            else:
+                gate_pair(b, c, 2 if m + 1 in quantised_at else 1)
+
+        def up(b, c, bank):
+            sums = bank.rearrange("p (t j) -> p t j", t=PACK)
             for t in range(PACK):
                 c0 = HALF * b + P * t
                 first_stage(
-                    bank[:, t, :], wu_codes[:, 2 * c0 : 2 * (c0 + P)].bitcast(FP4X4), wu_sc[:, c0 : c0 + P], CHUNK * c, CHUNK
+                    sums[:, t, :], wu_codes[:, 2 * c0 : 2 * (c0 + P)].bitcast(FP4X4), wu_sc[:, c0 : c0 + P], CHUNK * c, CHUNK
                 )
-            up_of[b, c] = bank.rearrange("p (u e) j -> p j u e", u=2)
-
-        def place(n, b, j0):
-            return GROUP * b + j0
+            up_of[b, c] = sums.rearrange("p (u e) j -> p j u e", u=2)
 
         def product(b, c):
             n, d = divmod(c, 2)
+            c0 = GROUP * b + CHUNK * d
             nc.vector.tensor_tensor(
-                h_bf[n][:].rearrange("p b j t -> p (b j) t")[:, place(n, b, CHUNK * d) : place(n, b, CHUNK * d) + CHUNK, :].rearrange("p j (u e) -> p j u e", u=2),
-                up_of[b, c],
-                gate_of[b, c],
-                MULT,
-            )
-
-        def product_on_gpsimd(b, c):
-            n, d = divmod(c, 2)
-            up_sb = keep.tile([P, CHUNK, 2, 2], F32, name=f"up{b}{c}", align_bytes=ALIGN)
-            nc.scalar.copy(up_sb[:], up_of[b, c])
-            c0 = place(n, b, CHUNK * d)
-            nc.gpsimd.tensor_tensor(
-                h_bf[n][:].rearrange("p b j t -> p (b j) t")[:, c0 : c0 + CHUNK, :].rearrange("p j (u e) -> p j u e", u=2),
-                up_sb[:],
-                gate_of[b, c],
-                MULT,
+                h_bf[n][:, c0 : c0 + CHUNK, :].rearrange("p j (u e) -> p j u e", u=2), up_of[b, c], gate_of[b, c], MULT
             )
 
         def quant_h(n, c0, width):
             nc.vector.quantize_mx(
-                out=h_codes[n][:].rearrange("p b j -> p (b j)")[:, c0 : c0 + width].bitcast(FP8X4),
-                scales=h_sc[n][:].rearrange("p b j -> p (b j)")[:, c0 : c0 + width],
-                in_=h_bf[n][:].rearrange("p b j t -> p (b j t)")[:, PACK * c0 : PACK * (c0 + width)],
+                out=h_codes[n][:, c0 : c0 + width].bitcast(FP8X4),
+                scales=h_sc[n][:, c0 : c0 + width],
+                in_=h_bf[n][:, c0 : c0 + width, :].rearrange("p j t -> p (j t)"),
             )
 
-        def down_pass(dst, a, b, n, j0, width, start, stop):
+        def second_stage(dst, a, b, n):
+            width = CHUNK if b else GROUP
             if b == 0:
                 codes = wd8_sb[:, P * a : P * (a + 1)].bitcast(FP8X4)
             else:
                 codes = wd4_sb[:, 2 * P * a : 2 * P * (a + 1)].bitcast(FP4X4)
-            nc.tensor.matmul_mx(
-                out=dst,
-                lhsT=codes,
-                lhsT_scale=wd_sc[:, N * b + P * a : N * b + P * (a + 1)],
-                rhs=h_codes[n][:].rearrange("p b j -> p (b j)")[:, place(n, b, j0) : place(n, b, j0) + width].bitcast(FP8X4),
-                rhs_scale=h_sc[n][:].rearrange("p b j -> p (b j)")[:, place(n, b, j0) : place(n, b, j0) + width],
-                start=start,
-                stop=stop,
-            )
+            for j0 in range(0, GROUP, width):
+                cols = slice(GROUP * b + j0, GROUP * b + j0 + width)
+                nc.tensor.matmul_mx(
+                    out=dst[:, j0 : j0 + width],
+                    lhsT=codes,
+                    lhsT_scale=scales_in[:, N * b + P * a : N * b + P * (a + 1)],
+                    rhs=h_codes[n][:, cols].bitcast(FP8X4),
+                    rhs_scale=h_sc[n][:, cols],
+                    start=b == 0,
+                    stop=b == 1 and j0 + width == GROUP,
+                )
 
-        def operands(bank, a0, a1, j0, width):
-            s, c = divmod(j0, HALF)
-            y = bank.rearrange("p (a j) -> p a j", j=width)
-            return y, res_sb[s][:, a0:a1, c : c + width], out_rows[:, a0:a1, j0 : j0 + width]
+        def operands(bank, a0, a1, n):
+            s, c = divmod(GROUP * n, HALF)
+            y = bank.rearrange("p (a j) -> p a j", j=GROUP)
+            return y, res_sb[s][:, a0:a1, c : c + GROUP], out_rows[:, a0:a1, GROUP * n : GROUP * (n + 1)]
 
-        def down_group(n, u, bank):
+        def fill_y(n, u, bank):
             for e in range(2):
-                c0 = GROUP * e
-                down_pass(bank[:, c0 : c0 + GROUP], 2 * u + e, 0, n, 0, GROUP, True, False)
-                for d in range(2):
-                    dst = bank[:, c0 + CHUNK * d : c0 + CHUNK * (d + 1)]
-                    down_pass(dst, 2 * u + e, 1, n, CHUNK * d, CHUNK, False, d == 1)
-            return operands(bank, 2 * u, 2 * u + 2, GROUP * n, GROUP)
+                for b in range(2):
+                    second_stage(bank[:, GROUP * e : GROUP * (e + 1)], 2 * u + e, b, n)
+            return operands(bank, 2 * u, 2 * u + 2, n)
 
-        def down_half(bank, u, b, n):
-            width = CHUNK if b else GROUP
-            for e in range(2):
-                for j0 in range(0, GROUP, width):
-                    c0 = GROUP * e + j0
-                    down_pass(bank[:, c0 : c0 + width], 2 * u + e, b, n, j0, width, b == 0 and c0 == 0, c0 + width == HALF and b == 1)
-
-        def add_on_vector(y, res_part, out_part, held=False):
-            if held:
-                result = keep.tile(list(res_part.shape), F32, name="result_held", tag=f"stage{GROUPS - 1}", align_bytes=ALIGN)
-            else:
-                result = ring.tile(list(res_part.shape), F32, name="result")
+        def add_on_vector(y, res_part, out_part):
+            result = ring.tile(list(res_part.shape), F32, name="result")
             nc.vector.tensor_tensor(result[:], y, res_part, ADD)
             nc.sync.dma_start(out_part, result[:])
 
-        def leave_psum(y, res_part, out_part):
+        def leave_psum(y, res_part):
             y_sb = ring.tile(list(res_part.shape), F32, name="y_sb")
             nc.scalar.copy(y_sb[:], y)
-            return y_sb[:], res_part, out_part
+            return y_sb[:], res_part
 
-        sums = {}
-
-        def add_on_gpsimd(n, y, res_part, out_part):
-            if n not in sums:
-                sums[n] = [keep.tile([P, 2, 2, GROUP], F32, name=f"result{n}", tag="gate%d%d" % ORDER[QUANT_AT[n] - 1], align_bytes=ALIGN) if EARLY_RELEASE[n] else keep.tile([P, 2, 2, GROUP], F32, name=f"result{n}", tag=f"stage{n}", align_bytes=ALIGN), 0]
-            result = sums[n][0][:, sums[n][1]]
-            sums[n][1] = sums[n][1] + 1
-            nc.gpsimd.tensor_tensor(result, y, res_part, ADD)
-            nc.sync.dma_start(out_part, result)
+        def add_on_gpsimd(behind, n, copies):
+            result = keep.tile(
+                [P, len(copies), 2, GROUP], F32, name=f"sums{n}", tag=gate_tag(*order[quantised_at[behind] - 1]), align_bytes=ALIGN
+            )
+            for e, (u, y, res_part) in enumerate(copies):
+                nc.gpsimd.tensor_tensor(result[:, e], y, res_part, ADD)
+            a0 = 2 * copies[0][0]
+            nc.sync.dma_start(
+                out_rows[:, a0 : a0 + 2 * len(copies), GROUP * n : GROUP * (n + 1)], result[:].rearrange("p e a j -> p (e a) j")
+            )
 
         for i in range(2):
             for j0 in (0, HALF):
@@ -367,67 +322,64 @@ def tile_list_silu_mix_res_kernel(
         for n in LAST_PLANE_PIECES:
             gather(PACK - 1, j0, n)
             round_x(j0, n, 2)
-            if j0 < EARLY:
+            if j0 < GROUP:
                 quant_x(j0, n)
             j0 = j0 + n
-        round_wg(nc.vector.tensor_copy, 0, 0, P)
-        round_wg(nc.vector.tensor_copy, 1, 0, VSHARE)
+
+        round_wg(nc.vector.tensor_copy, 0, 0, P, wg_vector[:, :, 0:HALF])
+        round_wg(nc.vector.tensor_copy, 1, 0, VECTOR_SHARE, wg_vector[:, :, HALF:edge])
         quant_wg(0)
-        nc.scalar.activation(zero_late[:], wg_in[1][:, 0, 0:1], IDENTITY, bias=zero[:], scale=0.0)
-        round_wg(nc.scalar.copy, 1, VSHARE, P)
+        nc.scalar.activation(first_bias[:], wg_scalar[:, 0, 0:1], IDENTITY, bias=zero[:], scale=0.0)
+        round_wg(nc.scalar.copy, 1, VECTOR_SHARE, P, wg_scalar[:])
         quant_x(GROUP, GROUP)
         quant_x(HALF, HALF)
         quant_wg(1)
 
-        last = GROUPS - 1
-        waiting, to_add, tail_banks = [], [], []
         free = [(0, bank[:]) for bank in banks[GATE_BANKS:]]
-        bank_of, downs, ups = {}, [], 0
-        for k in range(len(ORDER) + 1):
-            for step, b, c, chunks in GATES:
-                if step == k:
-                    (gate_chunk if chunks == 1 else gate_group)(b, c)
+        shared = len(free)
+        up_banks, due, copied, to_add = [], [], [], []
+        for m in range(AHEAD):
+            gate_for(m)
+        for k in range(len(order) + 1):
+            if k + AHEAD < len(order):
+                gate_for(k + AHEAD)
             if k >= 1:
-                product(*ORDER[k - 1])
-                free.append((k, bank_of[k - 1]))
+                product(*order[k - 1])
+                free.append((k, up_banks[k - 1]))
             for n in range(last):
-                if k == QUANT_AT[n]:
+                if k == quantised_at[n]:
                     quant_h(n, 0, 2 * GROUP)
-                    for held in [w for w in waiting if w[0] == n]:
-                        add_on_gpsimd(*held)
-                downs.extend((n, u) for u in range(2) if k == QUANT_AT[n] + DOWN_LAG[u])
-            free.sort(key=lambda f: f[0])
-            while free and free[0][0] <= k and (downs or ups < min(len(ORDER), k + LEAD)):
+                    add_here = [c for c in copied if ON_GPSIMD[c[0], c[1]] == n]
+                    if add_here:
+                        add_on_gpsimd(n, add_here[0][0], [c[1:] for c in add_here])
+                due.extend((n, u) for u in range(2) if k == quantised_at[n] + u)
+            free.sort(key=lambda entry: entry[0])
+            while free and free[0][0] <= k and (due or len(up_banks) < min(len(order), k + shared)):
                 bank = free.pop(0)[1]
-                if downs and ups >= min(len(ORDER), k + LEAST):
-                    n, u = downs.pop(0)
-                    sums_in = down_group(n, u, bank)
-                    if (n, u) not in GB:
-                        to_add.append((k + ADD_LAG, sums_in, bank))
-                        continue
-                    if QUANT_AT[GB[n, u]] <= k:
-                        add_on_gpsimd(GB[n, u], *leave_psum(*sums_in))
+                if due and len(up_banks) >= min(len(order), k + AHEAD):
+                    n, u = due.pop(0)
+                    y, res_part, out_part = fill_y(n, u, bank)
+                    if (n, u) in ON_GPSIMD:
+                        copied.append((n, u, *leave_psum(y, res_part)))
+                        free.append((k + COPIED_AFTER, bank))
                     else:
-                        waiting.append((GB[n, u], *leave_psum(*sums_in)))
-                    free.append((k + RETURN, bank))
+                        to_add.append((k + ADDED_AFTER, bank, (y, res_part, out_part)))
                 else:
-                    up(*ORDER[ups], bank)
-                    bank_of[ups] = bank
-                    ups = ups + 1
-            while to_add and to_add[0][0] <= k and k <= QUANT_AT[last - 1]:
-                free.append((k + 1, to_add[0][2]))
-                add_on_vector(*to_add.pop(0)[1])
-        spare = [take("gate") for u in range(GATE_BANKS)] + [bank for step, bank in free]
-        ends = [spare[a // SHARE][:, GROUP * (a % SHARE) : GROUP * (a % SHARE + 1)] for a in range(N // P)]
-        h_codes.append(keep.tile([P, 2, GROUP], U32, name="h_codes_last", tag="gate%d%d" % ORDER[-2], align_bytes=ALIGN))
-        quant_h(last, 0, GROUP)
-        quant_h(last, GROUP, GROUP)
-        for a in range(N // P):
-            down_pass(ends[a], a, 0, last, 0, GROUP, a % SHARE == 0, False)
-        for a in range(N // P):
-            for d in range(2):
-                down_pass(ends[a][:, CHUNK * d : CHUNK * (d + 1)], a, 1, last, CHUNK * d, CHUNK, False, d == 1 and a % SHARE == SHARE - 1)
-        for step, sums_in, bank in to_add:
-            add_on_vector(*sums_in)
-        for a in range(N // P):
-            add_on_vector(*operands(ends[a], a, a + 1, J - GROUP, GROUP))
+                    up(*order[len(up_banks)], bank)
+                    up_banks.append(bank)
+            while to_add and to_add[0][0] <= k <= quantised_at[-1]:
+                step, bank, parts = to_add.pop(0)
+                add_on_vector(*parts)
+                free.append((k + 1, bank))
+
+        h_codes.append(keep.tile([P, 2 * GROUP], U32, name="h_codes_last", tag=gate_tag(*order[-2]), align_bytes=ALIGN))
+        ends = [bank[:, 0:GROUP] for bank in gate_banks + [free[0][1]]]
+        for b in range(2):
+            quant_h(last, GROUP * b, GROUP)
+        for b in range(2):
+            for a in range(BLOCKS):
+                second_stage(ends[a], a, b, last)
+        for step, bank, parts in to_add:
+            add_on_vector(*parts)
+        for a in range(BLOCKS):
+            add_on_vector(*operands(ends[a], a, a + 1, last))

@@ -28,8 +28,8 @@ ALIGN = 256
 QUAD = 32
 HEAD = 16
 BLOCKS = N // P
-LAST_PLANE_PIECES = (CHUNK, CHUNK, GROUP, GROUP, GROUP)
-VECTOR_SHARE = 48
+LAST_PLANE_PIECES = (CHUNK, CHUNK, GROUP, GROUP)
+VECTOR_SHARE = 32
 GATE_BANKS = 3
 AHEAD = 3
 SINGLES = 6
@@ -122,13 +122,14 @@ def tile_list_silu_mix_res_kernel(
 
         picked_flat = keep.tile([P, PACK * J], F32, name="picked", align_bytes=ALIGN)
         picked = picked_flat[:].rearrange("p (i j) -> p i j", i=PACK)
-        xg_bf = keep.tile([P, J - CHUNK, PACK], BF16, name="xg_bf", align_bytes=ALIGN)
-        xg_first = picked_flat[:, PACK * J - GROUP :].bitcast(BF16).rearrange("p (j i) -> p j i", i=PACK)
+        xg_bf = keep.tile([P, J, PACK], BF16, name="xg_bf", align_bytes=ALIGN)
+        xg_aside = picked_flat[:, PACK * J - GROUP :].bitcast(BF16).rearrange("p (j i) -> p j i", i=PACK)
         wg_bf = [keep.tile([P, PACK, P, PACK], BF16, name=f"wg_bf{b}", align_bytes=ALIGN) for b in range(2)]
         wg_codes = [keep.tile([P, HALF], U32, name=f"wg_codes{b}", align_bytes=ALIGN) for b in range(2)]
         wg_sc = [keep.tile([P, HALF], U8, name=f"wg_sc{b}", align_bytes=ALIGN) for b in range(2)]
         codes_early = keep.tile([P, GROUP], U32, name="codes_early", align_bytes=ALIGN)
-        codes_late = keep.tile([P, J - GROUP], U32, name="codes_late", tag="wg_vector", align_bytes=ALIGN)
+        codes_late = keep.tile([P, 2 * GROUP], U32, name="codes_late", tag="wg_vector", align_bytes=ALIGN)
+        codes_of = [codes_early[:], codes_late[:, 0:GROUP], codes_late[:, GROUP:]]
         xg_sc = keep.tile([P, J], U8, name="xg_sc", align_bytes=ALIGN)
         h_bf = [keep.tile([P, 2 * GROUP, PACK], BF16, name=f"h_bf{n}", align_bytes=ALIGN) for n in range(GROUPS)]
         h_codes = [keep.tile([P, 2 * GROUP], U32, name=f"h_codes{n}", align_bytes=ALIGN) for n in range(GROUPS - 1)]
@@ -150,17 +151,18 @@ def tile_list_silu_mix_res_kernel(
             )
 
         def rounded(j0, n):
-            return xg_first[:, j0 : j0 + n] if j0 < CHUNK else xg_bf[:, j0 - CHUNK : j0 - CHUNK + n]
+            return xg_aside[:, 0:n] if j0 == GROUP else xg_bf[:, j0 : j0 + n]
 
         def xg_codes(j0, n):
-            codes = codes_early[:, j0 : j0 + n] if j0 < GROUP else codes_late[:, j0 - GROUP : j0 - GROUP + n]
-            return codes.bitcast(FP8X4)
+            group, c0 = divmod(j0, GROUP)
+            return codes_of[group][:, c0 : c0 + n].bitcast(FP8X4)
 
         def round_x(j0, n, i0):
-            if j0 < CHUNK < j0 + n:
-                round_x(j0, CHUNK, i0)
-                round_x(CHUNK, n - CHUNK, i0)
-                return
+            for cut in (GROUP, GROUP + CHUNK):
+                if j0 < cut < j0 + n:
+                    round_x(j0, cut - j0, i0)
+                    round_x(cut, j0 + n - cut, i0)
+                    return
             nc.scalar.copy(
                 rounded(j0, n)[:, :, i0 : i0 + 2],
                 picked[:, i0 : i0 + 2, j0 : j0 + n].rearrange("p i j -> p j i"),
@@ -331,9 +333,16 @@ def tile_list_silu_mix_res_kernel(
         quant_wg(0)
         nc.scalar.activation(first_bias[:], wg_scalar[:, 0, 0:1], IDENTITY, bias=zero[:], scale=0.0)
         round_wg(nc.scalar.copy, 1, VECTOR_SHARE, P, wg_scalar[:])
-        quant_x(GROUP, GROUP)
-        quant_x(HALF, HALF)
+        for j0, n in ((GROUP, CHUNK), (GROUP + CHUNK, CHUNK), (HALF, GROUP)):
+            quant_x(j0, n)
+
+        gather(PACK - 1, J - GROUP, GROUP)
         quant_wg(1)
+        one = keep.tile([P, 1], F32, name="one", tag="wg_bf1", align_bytes=ALIGN)
+        nc.gpsimd.tensor_scalar(one[:], zero_in[:], 1.0, 1.0, MULT, ADD)
+        nc.gpsimd.tensor_scalar(
+            xg_bf[:, J - GROUP :, 2:PACK], picked[:, 2:PACK, J - GROUP :].rearrange("p i j -> p j i"), one[:], 0.0, MULT, ADD
+        )
 
         free = [(0, bank[:]) for bank in banks[GATE_BANKS:]]
         shared = len(free)
@@ -346,6 +355,10 @@ def tile_list_silu_mix_res_kernel(
             if k >= 1:
                 product(*order[k - 1])
                 free.append((k, up_banks[k - 1]))
+            if k == quantised_at[0]:
+                codes_last = keep.tile([P, GROUP], U32, name="codes_last", tag=gate_tag(1, 1), align_bytes=ALIGN)
+                codes_of.append(codes_last[:])
+                quant_x(J - GROUP, GROUP)
             for n in range(last):
                 if k == quantised_at[n]:
                     quant_h(n, 0, 2 * GROUP)

@@ -387,12 +387,10 @@ def tile_list_silu_mix_res_kernel(
 
         h_codes.append(keep.tile([P, 2 * GROUP], U32, name="h_codes_last", tag=gate_tag(*order[-2]), align_bytes=ALIGN))
         ends = [bank[:, 0:GROUP] for bank in gate_banks + [free[0][1]]]
-        for b in range(2):
+        for b, (step, bank, parts) in enumerate(to_add):
             quant_h(last, GROUP * b, GROUP)
-        for b in range(2):
             for a in range(BLOCKS):
                 second_stage(ends[a], a, b, last)
-        for step, bank, parts in to_add:
             add_on_vector(*parts)
         for a in range(BLOCKS):
             add_on_vector(*operands(ends[a], a, a + 1, last))

@@ -66,10 +66,11 @@ def tile_list_silu_mix_res_kernel(
         planes = [keep.tile([P, T], F32, name=f"plane{i}") for i in range(PACK)]
         edge = HALF + PACK * VECTOR_SHARE
         wg_vector = keep.tile([P, PACK, edge], F32, name="wg_vector", align_bytes=ALIGN)
-        wg_scalar = keep.tile([P, PACK, R - edge], F32, name="wg_scalar", align_bytes=ALIGN)
+        piece = (R - edge) // 2
+        wg_scalar = [keep.tile([P, PACK, piece], F32, name=f"wg_scalar{e}", align_bytes=ALIGN) for e in range(2)]
         wd8_sb = keep.tile([P, N], U32, name="wd8_sb", align_bytes=ALIGN)
         wd4_sb = keep.tile([P, 2 * N], U8, name="wd4_sb", align_bytes=ALIGN)
-        res_sb = [keep.tile([P, BLOCKS, HALF], F32, name=f"res{s}") for s in range(2)]
+        res_sb = keep.tile([P, BLOCKS, J], F32, name="res_sb")
         x_rows = xT.rearrange("(p i) t -> i p t", i=PACK)
         wg_rows = wg.rearrange("(p i) r -> p i r", i=PACK)
         res_rows = res.rearrange("(a p) j -> p a j", p=P)
@@ -110,15 +111,15 @@ def tile_list_silu_mix_res_kernel(
             if i == PACK - 2:
                 deal_scales(wu_sc, nc.scalar)
         nc.sync.dma_start(wg_vector[:], wg_rows[:, :, 0:edge])
-        nc.sync.dma_start(wg_scalar[:], wg_rows[:, :, edge:R])
+        for e in range(2):
+            nc.sync.dma_start(wg_scalar[e][:], wg_rows[:, :, edge + piece * e : edge + piece * (e + 1)])
         nc.sync.dma_start(scales_in[0:HEAD, 0:N].bitcast(I32), wd8_scales[0].bitcast(I32))
         nc.sync.dma_start(scales_in[0:HEAD, N:].bitcast(I32), wd4_scales[0].bitcast(I32))
         nc.sync.dma_start(wd8_sb[:].bitcast(I32), wd8_words[0].rearrange("p n t -> p (n t)").bitcast(I32))
         nc.sync.dma_start(wd4_sb[:].bitcast(I32), wd4_words[0].bitcast(I32))
         deal_scales(scales_in, nc.sync)
-        for a0 in (0, 2):
-            nc.sync.dma_start(res_sb[0][:, a0 : a0 + 2], res_rows[:, a0 : a0 + 2, 0:HALF])
-        nc.sync.dma_start(res_sb[1][:], res_rows[:, :, HALF:J])
+        for a0, a1 in ((0, 1), (1, BLOCKS)):
+            nc.sync.dma_start(res_sb[:, a0:a1], res_rows[:, a0:a1])
 
         picked_flat = keep.tile([P, PACK * J], F32, name="picked", align_bytes=ALIGN)
         picked = picked_flat[:].rearrange("p (i j) -> p i j", i=PACK)
@@ -265,7 +266,7 @@ def tile_list_silu_mix_res_kernel(
             )
 
         def second_stage(dst, a, b, n):
-            width = CHUNK if b else GROUP
+            width = GROUP
             if b == 0:
                 codes = wd8_sb[:, P * a : P * (a + 1)].bitcast(FP8X4)
             else:
@@ -283,9 +284,9 @@ def tile_list_silu_mix_res_kernel(
                 )
 
         def operands(bank, a0, a1, n):
-            s, c = divmod(GROUP * n, HALF)
             y = bank.rearrange("p (a j) -> p a j", j=GROUP)
-            return y, res_sb[s][:, a0:a1, c : c + GROUP], out_rows[:, a0:a1, GROUP * n : GROUP * (n + 1)]
+            cols = slice(GROUP * n, GROUP * (n + 1))
+            return y, res_sb[:, a0:a1, cols], out_rows[:, a0:a1, cols]
 
         def fill_y(n, u, bank):
             for e in range(2):
@@ -331,8 +332,10 @@ def tile_list_silu_mix_res_kernel(
         round_wg(nc.vector.tensor_copy, 0, 0, P, wg_vector[:, :, 0:HALF])
         round_wg(nc.vector.tensor_copy, 1, 0, VECTOR_SHARE, wg_vector[:, :, HALF:edge])
         quant_wg(0)
-        nc.scalar.activation(first_bias[:], wg_scalar[:, 0, 0:1], IDENTITY, bias=zero[:], scale=0.0)
-        round_wg(nc.scalar.copy, 1, VECTOR_SHARE, P, wg_scalar[:])
+        middle = (VECTOR_SHARE + P) // 2
+        round_wg(nc.scalar.copy, 1, VECTOR_SHARE, middle, wg_scalar[0][:])
+        nc.scalar.activation(first_bias[:], wg_scalar[1][:, 0, 0:1], IDENTITY, bias=zero[:], scale=0.0)
+        round_wg(nc.scalar.copy, 1, middle, P, wg_scalar[1][:])
         for j0, n in ((GROUP, CHUNK), (GROUP + CHUNK, CHUNK), (HALF, GROUP)):
             quant_x(j0, n)
 

@@ -202,7 +202,7 @@ def tile_list_silu_mix_res_kernel(
             for e in range(results):
                 cols = slice(P * (t0 + e), P * (t0 + e + 1))
                 first_stage(bank[:, e, :], wg_codes[b][:, cols].bitcast(FP8X4), wg_sc[b][:, cols], j0, n)
-            return bank.rearrange("p t j -> p j t")
+            return bank.rearrange("p t (k s) -> p k t s", s=2)
 
         gate_of, up_of = {}, {}
 
@@ -215,23 +215,23 @@ def tile_list_silu_mix_res_kernel(
 
         def gate_single(b, c):
             sums = gate_sums(b, 0, PACK, CHUNK * c, CHUNK)
-            gate = gate_tile(b, c, [P, CHUNK, PACK])
+            gate = gate_tile(b, c, [P, CHUNK // 2, PACK, 2])
             if len(gate_of) < GATE_BANKS:
                 nc.scalar.activation(gate, sums, SILU, bias=first_bias[:])
             else:
                 nc.scalar.activation(gate, sums, SILU)
-            gate_of[b, c] = gate.rearrange("p j (u e) -> p j u e", u=2)
+            gate_of[b, c] = gate
 
         def gate_pair(b, c, tiles):
-            width = GROUP // tiles
-            gates = [gate_tile(b, c + d, [P, 2, width, 2]) for d in range(tiles)]
+            width = CHUNK // tiles
+            gates = [gate_tile(b, c + d, [P, width, PACK, 2]) for d in range(tiles)]
             for u in range(2):
                 sums = gate_sums(b, 2 * u, 2, CHUNK * c, GROUP)
                 for d in range(tiles):
-                    nc.scalar.activation(gates[d][:, u], sums[:, width * d : width * (d + 1)], SILU)
+                    nc.scalar.activation(gates[d][:, :, 2 * u : 2 * u + 2], sums[:, width * d : width * (d + 1)], SILU)
             for d in range(2):
-                tile, j0 = divmod(CHUNK * d, width)
-                gate_of[b, c + d] = gates[tile][:, :, j0 : j0 + CHUNK, :].rearrange("p u j e -> p j u e")
+                tile, k0 = divmod(CHUNK // 2 * d, width)
+                gate_of[b, c + d] = gates[tile][:, k0 : k0 + CHUNK // 2]
 
         def gate_for(m):
             b, c = order[m]
@@ -249,13 +249,13 @@ def tile_list_silu_mix_res_kernel(
                 first_stage(
                     sums[:, t, :], wu_codes[:, 2 * c0 : 2 * (c0 + P)].bitcast(FP4X4), wu_sc[:, c0 : c0 + P], CHUNK * c, CHUNK
                 )
-            up_of[b, c] = sums.rearrange("p (u e) j -> p j u e", u=2)
+            up_of[b, c] = sums.rearrange("p t (k s) -> p k t s", s=2)
 
         def product(b, c):
             n, d = divmod(c, 2)
             c0 = GROUP * b + CHUNK * d
             nc.vector.tensor_tensor(
-                h_bf[n][:, c0 : c0 + CHUNK, :].rearrange("p j (u e) -> p j u e", u=2), up_of[b, c], gate_of[b, c], MULT
+                h_bf[n][:, c0 : c0 + CHUNK, :].rearrange("p (k s) t -> p k t s", s=2), up_of[b, c], gate_of[b, c], MULT
             )
 
         def quant_h(n, c0, width):

from contextlib import ExitStack

import concourse.mybir as mybir

K, R, N, T, J = 512, 1024, 512, 2048, 1024
FLOPS = 2 * K * R * J * 2 + 2 * R * N * J

F32 = mybir.dt.float32
BF16 = mybir.dt.bfloat16
I32 = mybir.dt.int32
U32 = mybir.dt.uint32
U16 = mybir.dt.uint16
U8 = mybir.dt.uint8
FP8X4 = mybir.dt.float8_e4m3fn_x4
FP4X4 = mybir.dt.float4_e2m1fn_x4
MULT = mybir.AluOpType.mult
ADD = mybir.AluOpType.add
SILU = mybir.ActivationFunctionType.Silu
IDENTITY = mybir.ActivationFunctionType.Identity

P = 128
PACK = 4
HALF = 512
CHUNK = 128
GROUP = 2 * CHUNK
GROUPS = J // GROUP
ALIGN = 256
QUAD = 32
HEAD = 16
BLOCKS = N // P
LAST_PLANE_PIECES = (CHUNK, CHUNK, GROUP, GROUP)
VECTOR_SHARE = 32
GATE_BANKS = 3
AHEAD = 3
SINGLES = 6
COPIED_AFTER = 3
ADDED_AFTER = 2
RESULT_TILES = 6
ON_GPSIMD = {(0, 0): 1, (0, 1): 1, (1, 1): 2}


def tile_list_silu_mix_res_kernel(
    tc, xT, wgt, wg, wu_words, wu_scales, wd8_words, wd8_scales, wd4_words, wd4_scales, res, offs, out
):
    nc = tc.nc
    with ExitStack() as ctx:
        keep = ctx.enter_context(tc.tile_pool(name="keep", bufs=1))
        ring = ctx.enter_context(tc.tile_pool(name="ring", bufs=RESULT_TILES))
        psum = ctx.enter_context(tc.psum_pool(name="psum", bufs=1))

        scales_in = keep.tile([P, R], U8, name="scales_in", align_bytes=ALIGN)
        nc.vector.memset(scales_in[:].bitcast(I32), 0)
        zero_in = keep.tile([P, 1], F32, name="zero_in")
        nc.vector.memset(zero_in[:], 0.0)
        zero = keep.tile([P, 1], F32, name="zero")
        first_bias = keep.tile([P, 1], F32, name="first_bias")

        offsets = keep.tile([P, J // HEAD], U16, name="offsets")
        wu_in = keep.tile([P, 2 * R], U8, name="wu_in", align_bytes=ALIGN)
        wu_codes = keep.tile([P, 2 * R], U8, name="wu_codes", align_bytes=ALIGN)
        wu_sc = keep.tile([P, R], U8, name="wu_sc", align_bytes=ALIGN)
        wgt_in = keep.tile([P, 2 * QUAD], F32, name="wgt_in", align_bytes=ALIGN)
        wgt_turned = keep.tile([P, 2, 2, HEAD], F32, name="wgt_turned", align_bytes=ALIGN)
        wgt_wide = keep.tile([P, HEAD, 2, 2, HEAD], F32, name="wgt_wide", align_bytes=ALIGN)
        wgt_sb = keep.tile([P, J], F32, name="wgt_sb", align_bytes=ALIGN)
        planes = [keep.tile([P, T], F32, name=f"plane{i}") for i in range(PACK)]
        edge = HALF + PACK * VECTOR_SHARE
        wg_vector = keep.tile([P, PACK, edge], F32, name="wg_vector", align_bytes=ALIGN)
        piece = (R - edge) // 2
        wg_scalar = [keep.tile([P, PACK, piece], F32, name=f"wg_scalar{e}", align_bytes=ALIGN) for e in range(2)]
        wd8_sb = keep.tile([P, N], U32, name="wd8_sb", align_bytes=ALIGN)
        wd4_sb = keep.tile([P, 2 * N], U8, name="wd4_sb", align_bytes=ALIGN)
        res_sb = keep.tile([P, BLOCKS, J], F32, name="res_sb")
        x_rows = xT.rearrange("(p i) t -> i p t", i=PACK)
        wg_rows = wg.rearrange("(p i) r -> p i r", i=PACK)
        res_rows = res.rearrange("(a p) j -> p a j", p=P)
        out_rows = out.rearrange("(a p) j -> p a j", p=P)

        def deal_scales(plane, queue):
            for q in range(1, P // QUAD):
                queue.dma_start(plane[QUAD * q : QUAD * q + 4, :].bitcast(I32), plane[4 * q : 4 * q + 4, :].bitcast(I32))

        nc.sync.dma_start(wgt_in[:], wgt.rearrange("(g c) (a s) -> c g a s", c=HEAD, a=HEAD)[0])
        nc.sync.dma_start(wu_in[:].bitcast(I32), wu_words[0].bitcast(I32))
        nc.sync.dma_start(scales_in[0:HEAD, :].bitcast(I32), wu_scales[0].bitcast(I32))
        nc.scalar.activation(zero[:], zero_in[:], SILU)
        for u in range(2):
            nc.vector.transpose(wgt_turned[:, u].rearrange("p h a -> p (h a)"), wgt_in[:, QUAD * u : QUAD * (u + 1)])
        nc.vector.tensor_copy(
            wu_sc[:].rearrange("p (b t m) -> p b t m", b=2, t=PACK),
            scales_in[:].rearrange("p (b m t) -> p b t m", b=2, t=PACK),
        )
        nc.vector.tensor_copy(
            wu_codes[:].bitcast(U16).rearrange("p (b t m) -> p b t m", b=2, t=PACK),
            wu_in[:].bitcast(U16).rearrange("p (b m t) -> p b t m", b=2, t=PACK),
        )
        for s in range(2):
            part = slice(HEAD // 2 * s, HEAD // 2 * (s + 1))
            nc.scalar.copy(
                wgt_wide[:, part].rearrange("p a u h c -> p a (u h) c"),
                wgt_turned[:, :, :, part].rearrange("p u h a -> p a (u h)").unsqueeze(3).to_broadcast([P, HEAD // 2, 4, HEAD]),
            )
            nc.vector.transpose(
                wgt_sb[:, HALF * s : HALF * (s + 1)], wgt_wide[:, part].rearrange("p a u h c -> p (a u h c)")
            )

        for i in range(PACK):
            nc.sync.dma_start(planes[i][:], x_rows[i])
            if i == 0:
                nc.sync.dma_start(offsets[:], offs)
            if i == PACK - 2:
                deal_scales(wu_sc, nc.scalar)
        nc.sync.dma_start(wg_vector[:], wg_rows[:, :, 0:edge])
        for e in range(2):
            nc.sync.dma_start(wg_scalar[e][:], wg_rows[:, :, edge + piece * e : edge + piece * (e + 1)])
        nc.sync.dma_start(scales_in[0:HEAD, 0:N].bitcast(I32), wd8_scales[0].bitcast(I32))
        nc.sync.dma_start(scales_in[0:HEAD, N:].bitcast(I32), wd4_scales[0].bitcast(I32))
        nc.sync.dma_start(wd8_sb[:].bitcast(I32), wd8_words[0].rearrange("p n t -> p (n t)").bitcast(I32))
        nc.sync.dma_start(wd4_sb[:].bitcast(I32), wd4_words[0].bitcast(I32))
        deal_scales(scales_in, nc.sync)
        for a0, a1 in ((0, 1), (1, BLOCKS)):
            nc.sync.dma_start(res_sb[:, a0:a1], res_rows[:, a0:a1])

        picked_flat = keep.tile([P, PACK * J], F32, name="picked", align_bytes=ALIGN)
        picked = picked_flat[:].rearrange("p (i j) -> p i j", i=PACK)
        xg_bf = keep.tile([P, J, PACK], BF16, name="xg_bf", align_bytes=ALIGN)
        xg_aside = picked_flat[:, PACK * J - GROUP :].bitcast(BF16).rearrange("p (j i) -> p j i", i=PACK)
        wg_bf = [keep.tile([P, PACK, P, PACK], BF16, name=f"wg_bf{b}", align_bytes=ALIGN) for b in range(2)]
        wg_codes = [keep.tile([P, HALF], U32, name=f"wg_codes{b}", align_bytes=ALIGN) for b in range(2)]
        wg_sc = [keep.tile([P, HALF], U8, name=f"wg_sc{b}", align_bytes=ALIGN) for b in range(2)]
        codes_early = keep.tile([P, GROUP], U32, name="codes_early", align_bytes=ALIGN)
        codes_late = keep.tile([P, 2 * GROUP], U32, name="codes_late", tag="wg_vector", align_bytes=ALIGN)
        codes_of = [codes_early[:], codes_late[:, 0:GROUP], codes_late[:, GROUP:]]
        xg_sc = keep.tile([P, J], U8, name="xg_sc", align_bytes=ALIGN)
        h_bf = [keep.tile([P, 2 * GROUP, PACK], BF16, name=f"h_bf{n}", align_bytes=ALIGN) for n in range(GROUPS)]
        h_codes = [keep.tile([P, 2 * GROUP], U32, name=f"h_codes{n}", align_bytes=ALIGN) for n in range(GROUPS - 1)]
        h_sc = [keep.tile([P, 2 * GROUP], U8, name=f"h_sc{n}", align_bytes=ALIGN) for n in range(GROUPS)]
        banks = [psum.tile([P, HALF], F32, name=f"bank{k}") for k in range(8)]
        gate_banks = [bank[:] for bank in banks[:GATE_BANKS]]

        order = [(b, 2 * n + d) for n in range(GROUPS) for b in range(2) for d in range(2)]
        order.insert(2, order.pop(order.index((0, 2))))
        last = GROUPS - 1
        quantised_at = [order.index((1, 2 * n + 1)) + 2 for n in range(last)]

        def gather(i, j0, n):
            nc.vector.tensor_tensor(
                picked[:, i, j0 : j0 + n],
                planes[i][:].indirect(offsets[:, j0 // HEAD : (j0 + n) // HEAD]),
                wgt_sb[:, j0 : j0 + n],
                MULT,
            )

        def rounded(j0, n):
            return xg_aside[:, 0:n] if j0 == GROUP else xg_bf[:, j0 : j0 + n]

        def xg_codes(j0, n):
            group, c0 = divmod(j0, GROUP)
            return codes_of[group][:, c0 : c0 + n].bitcast(FP8X4)

        def round_x(j0, n, i0):
            for cut in (GROUP, GROUP + CHUNK):
                if j0 < cut < j0 + n:
                    round_x(j0, cut - j0, i0)
                    round_x(cut, j0 + n - cut, i0)
                    return
            nc.scalar.copy(
                rounded(j0, n)[:, :, i0 : i0 + 2],
                picked[:, i0 : i0 + 2, j0 : j0 + n].rearrange("p i j -> p j i"),
            )

        def quant_x(j0, n):
            nc.vector.quantize_mx(
                out=xg_codes(j0, n), scales=xg_sc[:, j0 : j0 + n], in_=rounded(j0, n).rearrange("p j i -> p (j i)")
            )

        def round_wg(copy, b, m0, m1, rows):
            copy(
                wg_bf[b][:, :, m0:m1, :].rearrange("p t m i -> p m i t"),
                rows.rearrange("p i (m t) -> p m i t", t=PACK),
            )

        def quant_wg(b):
            nc.vector.quantize_mx(
                out=wg_codes[b][:].bitcast(FP8X4), scales=wg_sc[b][:], in_=wg_bf[b][:].rearrange("p t m i -> p (t m i)")
            )

        def first_stage(dst, codes, scales, j0, n):
            nc.tensor.matmul_mx(
                out=dst,
                lhsT=codes,
                lhsT_scale=scales,
                rhs=xg_codes(j0, n),
                rhs_scale=xg_sc[:, j0 : j0 + n],
                start=True,
                stop=True,
            )

        def gate_sums(b, t0, results, j0, n):
            gate_banks.append(gate_banks.pop(0))
            bank = gate_banks[-1].rearrange("p (t j) -> p t j", t=results)
            for e in range(results):
                cols = slice(P * (t0 + e), P * (t0 + e + 1))
                first_stage(bank[:, e, :], wg_codes[b][:, cols].bitcast(FP8X4), wg_sc[b][:, cols], j0, n)
            return bank.rearrange("p t (k s) -> p k t s", s=2)

        gate_of, up_of = {}, {}

        def gate_tag(b, c):
            return f"gate{b}{c}"

        def gate_tile(b, c, shape):
            tile = keep.tile(shape, F32, name=gate_tag(b, c), align_bytes=ALIGN)
            return tile[:]

        def gate_single(b, c):
            sums = gate_sums(b, 0, PACK, CHUNK * c, CHUNK)
            gate = gate_tile(b, c, [P, CHUNK // 2, PACK, 2])
            if len(gate_of) < GATE_BANKS:
                nc.scalar.activation(gate, sums, SILU, bias=first_bias[:])
            else:
                nc.scalar.activation(gate, sums, SILU)
            gate_of[b, c] = gate

        def gate_pair(b, c, tiles):
            width = CHUNK // tiles
            gates = [gate_tile(b, c + d, [P, width, PACK, 2]) for d in range(tiles)]
            for u in range(2):
                sums = gate_sums(b, 2 * u, 2, CHUNK * c, GROUP)
                for d in range(tiles):
                    nc.scalar.activation(gates[d][:, :, 2 * u : 2 * u + 2], sums[:, width * d : width * (d + 1)], SILU)
            for d in range(2):
                tile, k0 = divmod(CHUNK // 2 * d, width)
                gate_of[b, c + d] = gates[tile][:, k0 : k0 + CHUNK // 2]

        def gate_for(m):
            b, c = order[m]
            if (b, c) in gate_of:
                return
            if m < SINGLES or m >= len(order) - 2:
                gate_single(b, c)
            else:
                gate_pair(b, c, 2 if m + 1 in quantised_at else 1)

        def up(b, c, bank):
            sums = bank.rearrange("p (t j) -> p t j", t=PACK)
            for t in range(PACK):
                c0 = HALF * b + P * t
                first_stage(
                    sums[:, t, :], wu_codes[:, 2 * c0 : 2 * (c0 + P)].bitcast(FP4X4), wu_sc[:, c0 : c0 + P], CHUNK * c, CHUNK
                )
            up_of[b, c] = sums.rearrange("p t (k s) -> p k t s", s=2)

        def product(b, c):
            n, d = divmod(c, 2)
            c0 = GROUP * b + CHUNK * d
            nc.vector.tensor_tensor(
                h_bf[n][:, c0 : c0 + CHUNK, :].rearrange("p (k s) t -> p k t s", s=2), up_of[b, c], gate_of[b, c], MULT
            )

        def quant_h(n, c0, width):
            nc.vector.quantize_mx(
                out=h_codes[n][:, c0 : c0 + width].bitcast(FP8X4),
                scales=h_sc[n][:, c0 : c0 + width],
                in_=h_bf[n][:, c0 : c0 + width, :].rearrange("p j t -> p (j t)"),
            )

        def second_stage(dst, a, b, n):
            width = GROUP
            if b == 0:
                codes = wd8_sb[:, P * a : P * (a + 1)].bitcast(FP8X4)
            else:
                codes = wd4_sb[:, 2 * P * a : 2 * P * (a + 1)].bitcast(FP4X4)
            for j0 in range(0, GROUP, width):
                cols = slice(GROUP * b + j0, GROUP * b + j0 + width)
                nc.tensor.matmul_mx(
                    out=dst[:, j0 : j0 + width],
                    lhsT=codes,
                    lhsT_scale=scales_in[:, N * b + P * a : N * b + P * (a + 1)],
                    rhs=h_codes[n][:, cols].bitcast(FP8X4),
                    rhs_scale=h_sc[n][:, cols],
                    start=b == 0,
                    stop=b == 1 and j0 + width == GROUP,
                )

        def operands(bank, a0, a1, n):
            y = bank.rearrange("p (a j) -> p a j", j=GROUP)
            cols = slice(GROUP * n, GROUP * (n + 1))
            return y, res_sb[:, a0:a1, cols], out_rows[:, a0:a1, cols]

        def fill_y(n, u, bank):
            for e in range(2):
                for b in range(2):
                    second_stage(bank[:, GROUP * e : GROUP * (e + 1)], 2 * u + e, b, n)
            return operands(bank, 2 * u, 2 * u + 2, n)

        def add_on_vector(y, res_part, out_part):
            result = ring.tile(list(res_part.shape), F32, name="result")
            nc.vector.tensor_tensor(result[:], y, res_part, ADD)
            nc.sync.dma_start(out_part, result[:])

        def leave_psum(y, res_part):
            y_sb = ring.tile(list(res_part.shape), F32, name="y_sb")
            nc.scalar.copy(y_sb[:], y)
            return y_sb[:], res_part

        def add_on_gpsimd(behind, n, copies):
            result = keep.tile(
                [P, len(copies), 2, GROUP], F32, name=f"sums{n}", tag=gate_tag(*order[quantised_at[behind] - 1]), align_bytes=ALIGN
            )
            for e, (u, y, res_part) in enumerate(copies):
                nc.gpsimd.tensor_tensor(result[:, e], y, res_part, ADD)
            a0 = 2 * copies[0][0]
            nc.sync.dma_start(
                out_rows[:, a0 : a0 + 2 * len(copies), GROUP * n : GROUP * (n + 1)], result[:].rearrange("p e a j -> p (e a) j")
            )

        for i in range(2):
            for j0 in (0, HALF):
                gather(i, j0, HALF)
                if i == 1:
                    round_x(j0, HALF, 0)
        gather(2, 0, J)
        j0 = 0
        for n in LAST_PLANE_PIECES:
            gather(PACK - 1, j0, n)
            round_x(j0, n, 2)
            if j0 < GROUP:
                quant_x(j0, n)
            j0 = j0 + n

        round_wg(nc.vector.tensor_copy, 0, 0, P, wg_vector[:, :, 0:HALF])
        round_wg(nc.vector.tensor_copy, 1, 0, VECTOR_SHARE, wg_vector[:, :, HALF:edge])
        quant_wg(0)
        middle = (VECTOR_SHARE + P) // 2
        round_wg(nc.scalar.copy, 1, VECTOR_SHARE, middle, wg_scalar[0][:])
        nc.scalar.activation(first_bias[:], wg_scalar[1][:, 0, 0:1], IDENTITY, bias=zero[:], scale=0.0)
        round_wg(nc.scalar.copy, 1, middle, P, wg_scalar[1][:])
        for j0, n in ((GROUP, CHUNK), (GROUP + CHUNK, CHUNK), (HALF, GROUP)):
            quant_x(j0, n)

        gather(PACK - 1, J - GROUP, GROUP)
        quant_wg(1)
        one = keep.tile([P, 1], F32, name="one", tag="wg_bf1", align_bytes=ALIGN)
        nc.gpsimd.tensor_scalar(one[:], zero_in[:], 1.0, 1.0, MULT, ADD)
        nc.gpsimd.tensor_scalar(
            xg_bf[:, J - GROUP :, 2:PACK], picked[:, 2:PACK, J - GROUP :].rearrange("p i j -> p j i"), one[:], 0.0, MULT, ADD
        )

        free = [(0, bank[:]) for bank in banks[GATE_BANKS:]]
        shared = len(free)
        up_banks, due, copied, to_add = [], [], [], []
        for m in range(AHEAD):
            gate_for(m)
        for k in range(len(order) + 1):
            if k + AHEAD < len(order):
                gate_for(k + AHEAD)
            if k >= 1:
                product(*order[k - 1])
                free.append((k, up_banks[k - 1]))
            if k == quantised_at[0]:
                codes_last = keep.tile([P, GROUP], U32, name="codes_last", tag=gate_tag(1, 1), align_bytes=ALIGN)
                codes_of.append(codes_last[:])
                quant_x(J - GROUP, GROUP)
            for n in range(last):
                if k == quantised_at[n]:
                    quant_h(n, 0, 2 * GROUP)
                    add_here = [c for c in copied if ON_GPSIMD[c[0], c[1]] == n]
                    if add_here:
                        add_on_gpsimd(n, add_here[0][0], [c[1:] for c in add_here])
                due.extend((n, u) for u in range(2) if k == quantised_at[n] + u)
            free.sort(key=lambda entry: entry[0])
            while free and free[0][0] <= k and (due or len(up_banks) < min(len(order), k + shared)):
                bank = free.pop(0)[1]
                if due and len(up_banks) >= min(len(order), k + AHEAD):
                    n, u = due.pop(0)
                    y, res_part, out_part = fill_y(n, u, bank)
                    if (n, u) in ON_GPSIMD:
                        copied.append((n, u, *leave_psum(y, res_part)))
                        free.append((k + COPIED_AFTER, bank))
                    else:
                        to_add.append((k + ADDED_AFTER, bank, (y, res_part, out_part)))
                else:
                    up(*order[len(up_banks)], bank)
                    up_banks.append(bank)
            while to_add and to_add[0][0] <= k <= quantised_at[-1]:
                step, bank, parts = to_add.pop(0)
                add_on_vector(*parts)
                free.append((k + 1, bank))

        h_codes.append(keep.tile([P, 2 * GROUP], U32, name="h_codes_last", tag=gate_tag(*order[-2]), align_bytes=ALIGN))
        ends = [bank[:, 0:GROUP] for bank in gate_banks + [free[0][1]]]
        for b, (step, bank, parts) in enumerate(to_add):
            quant_h(last, GROUP * b, GROUP)
            for a in range(BLOCKS):
                second_stage(ends[a], a, b, last)
            add_on_vector(*parts)
        for a in range(BLOCKS):
            add_on_vector(*operands(ends[a], a, a + 1, last))
